import numpy as np
import ml_dtypes


def mxq(x, axis, fmt="e4m3"):
    dtype, down = {"e4m3": (ml_dtypes.float8_e4m3fn, 7), "e5m2": (ml_dtypes.float8_e5m2, 14)}[fmt]
    v = np.moveaxis(np.asarray(x, np.float32).astype(ml_dtypes.bfloat16).astype(np.float64), axis, -1)
    blocks = v.reshape(v.shape[:-1] + (-1, 32))
    amax = np.abs(blocks).max(-1, keepdims=True)
    byte = np.maximum(np.where(amax > 0, np.frexp(amax)[1] - 1 + 127, 0) - down, 1)
    scale = np.exp2(byte - 127.0)
    codes = (blocks / scale).astype(np.float32).astype(dtype).astype(np.float64)
    return np.moveaxis((codes * scale).reshape(v.shape), -1, axis)


WIDE = False


def mx_kscale(k):
    if not WIDE:
        return np.ones(k)
    levels = np.array([10, -10, 5, -5, 0])
    if k % 512:
        return np.exp2(np.random.permutation(np.resize(levels, k // 32))).repeat(32)
    a = np.empty((k // 512, 16))
    for p in range(k // 512):
        a[p, :8] = np.random.permutation(np.resize(levels, 8))
        for g in range(8):
            far = levels[np.abs(levels - a[p, g]) >= 10]
            a[p, g + 8] = far[np.random.randint(len(far))]
    return np.exp2(a.ravel()).repeat(32)


BF16 = ml_dtypes.bfloat16


def bf(x):
    return np.asarray(x, np.float32).astype(BF16)


def f64(x):
    return np.asarray(x).astype(np.float64)


E2M1 = np.array([0.0, 0.5, 1.0, 1.5, 2.0, 3.0, 4.0, 6.0, -0.0, -0.5, -1.0, -1.5, -2.0, -3.0, -4.0, -6.0])


def pack_weight(w, fmt):
    k, n = w.shape
    w = f64(bf(w)).reshape(k // 32, 32, n)
    amax = np.abs(w).max(1)
    if fmt == "e4m3":
        byte = np.frexp(amax)[1] - 1 + 127 - 7
    else:
        mant, ex = np.frexp(amax / 6.0)
        byte = np.where(mant > 0.5, ex, ex - 1) + 127
    byte = np.clip(np.where(amax > 0, byte, 1), 1, 254)
    scaled = (w * np.exp2(127.0 - byte)[:, None, :]).reshape(k, n).astype(np.float32)
    by_word = np.ascontiguousarray(scaled.reshape(k // 512, 128, 4, n).transpose(0, 1, 3, 2))
    if fmt == "e4m3":
        words = by_word.astype(ml_dtypes.float8_e4m3fn).view(np.uint8)
    else:
        c = by_word.astype(ml_dtypes.float4_e2m1fn).view(np.uint8) & 0xF
        words = c[..., 0::2] | (c[..., 1::2] << 4)
    return np.ascontiguousarray(words), np.ascontiguousarray(byte.astype(np.uint8).reshape(k // 512, 16, n))


def unpack_weight(words, scales, fmt):
    g, p, n, _ = words.shape
    if fmt == "e4m3":
        vals = np.ascontiguousarray(words).view(ml_dtypes.float8_e4m3fn).astype(np.float64)
    else:
        nib = np.empty((g, p, n, 4), np.uint8)
        nib[..., 0::2] = words & 0xF
        nib[..., 1::2] = words >> 4
        vals = E2M1[nib]
    vals = vals * np.repeat(np.exp2(scales.astype(np.float64) - 127.0), 8, axis=1)[..., None]
    return vals.transpose(0, 1, 3, 2).reshape(g * 512, n)
def pack4(w):
    words, scales = pack_weight(w, "e2m1")
    return words.reshape(words.shape[0], 128, -1), scales


def unpack4(words, scales):
    return unpack_weight(words.reshape(words.shape[0], 128, -1, 2), scales, "e2m1")


F, D, M, P, R = 1024, 1536, 1024, 2048, 512


def draw0():
    s, t, u = mx_kscale(D), mx_kscale(M), mx_kscale(F)
    sigma = bf(np.random.uniform(0.4, 1.6, M))
    lam = bf(np.random.uniform(0.2, 1.0, F))
    meas = bf(np.random.standard_normal((F, D)) * s * u[:, None])
    us = bf(np.random.standard_normal((D, M)) / np.sqrt(D) * f64(sigma) / s[:, None] * t)
    vt_words, vt_scales = pack4(np.random.standard_normal((M, P)) / np.sqrt(M) / t[:, None])
    basis = bf(np.random.standard_normal((R, F)) / np.sqrt(F) / u)
    return {"meas": meas, "us": us, "sigma": sigma, "lam": lam,
            "vt_words": vt_words, "vt_scales": vt_scales, "basis": basis}


def core(meas, us, sigma, lam, vt_words, vt_scales, basis):
    c = mxq(f64(meas), 1, "e4m3") @ mxq(f64(us), 0, "e4m3")
    h = c / (f64(sigma)[None, :] ** 2 + f64(lam)[:, None])
    image = mxq(h, 1, "e4m3") @ unpack4(vt_words, vt_scales)
    comps = mxq(f64(basis), 1, "e4m3") @ mxq(h, 0, "e4m3")
    return image, comps


def e4m3fn_bytes(y):
    return np.clip(np.asarray(y, np.float64), -448.0, 448.0).astype(np.float32).astype(ml_dtypes.float8_e4m3fn).view(np.uint8)


def e4m3fn_values(b):
    return np.asarray(b, np.uint8).view(ml_dtypes.float8_e4m3fn).astype(np.float64)


def setup_inputs():
    d = draw0()
    x0 = np.asarray(d['basis']).astype(np.float64)
    s = (np.max(np.abs(x0), axis=(0,), keepdims=True) / 448.0).astype(np.float32)
    out = {}
    for k, v in d.items():
        if k == 'basis':
            out['basis_bytes'] = e4m3fn_bytes(x0 / s.astype(np.float64))
            out['basis_scale'] = s
        else:
            out[k] = v
    return out


def reference(meas, us, sigma, lam, vt_words, vt_scales, basis_bytes, basis_scale):
    return core(meas, us, sigma, lam, vt_words, vt_scales, e4m3fn_values(basis_bytes) * basis_scale.astype(np.float64))

@@ -1,0 +1,384 @@
+from contextlib import ExitStack
+
+import concourse.mybir as mybir
+from concourse.masks import make_identity
+
+F, D, M, P, R = 1024, 1536, 1024, 2048, 512
+FLOPS = 2 * (F * D * M + F * M * P + R * F * M)
+
+F32 = mybir.dt.float32
+BF16 = mybir.dt.bfloat16
+U32 = mybir.dt.uint32
+U8 = mybir.dt.uint8
+I32 = mybir.dt.int32
+E4M3 = mybir.dt.float8_e4m3fn
+FP8X4 = mybir.dt.float8_e4m3fn_x4
+FP4X4 = mybir.dt.float4_e2m1fn_x4
+ACT = mybir.ActivationFunctionType
+MULT = mybir.AluOpType.mult
+SUB = mybir.AluOpType.subtract
+
+PD = D // 512
+PM = M // 512
+PF = F // 512
+AB, TP = 5, 3
+
+
+def tile_spectral_tikhonov_imaging_s8_kernel(
+    tc, meas, us, sigma, lam, vt_words, vt_scales, basis_bytes, basis_scale, image, comps
+):
+    nc = tc.nc
+    with ExitStack() as ctx:
+        keep = ctx.enter_context(tc.tile_pool(name="keep", bufs=1))
+        work = ctx.enter_context(tc.tile_pool(name="work", bufs=2))
+        stage = ctx.enter_context(tc.tile_pool(name="stage", bufs=6))
+        psum = ctx.enter_context(tc.psum_pool(name="psum", bufs=1))
+
+        ctx.enter_context(tc.manual_schedule())
+
+        lam_raw = keep.tile([128, F], BF16, name="lam_raw")
+        nc.vector.memset(lam_raw[0:64, :], 0.0)
+        d_rhs = keep.tile([128, F], BF16, name="d_rhs")
+        nc.gpsimd.memset(d_rhs[:], 1.0)
+        d_cols = keep.tile([128, PM * 4, 128], BF16, name="d_cols")
+        nc.vector.memset(d_cols[:], 0.0)
+        nc.vector.memset(d_cols[:, :, 0:33:32], 1.0)
+        warm = keep.tile([128, 1], F32, name="warm")
+        nc.vector.memset(warm[:], 1.0)
+        nc.scalar.activation(out=warm[:], in_=warm[:], func=ACT.Abs_reciprocal_sqrt)
+        ident = keep.tile([128, 128], F32, name="ident")
+        make_identity(nc, ident[:])
+        ident_b = keep.tile([128, 128], BF16, name="ident_b")
+        make_identity(nc, ident_b[:])
+        vs = keep.tile([128, PM, P], U8, name="vs", align_bytes=64)
+        nc.gpsimd.memset(vs[:].bitcast(I32), 0)
+
+        sig = keep.tile([128, PM * 4], BF16, name="sig")
+        nc.sync.dma_start(out=sig[:].rearrange("q (j t) -> q j t", j=PM), in_=sigma.rearrange("(j q t) -> q j t", j=PM, q=128))
+        nc.sync.dma_start(out=lam_raw[0:64:32, :], in_=lam.partition_broadcast(2))
+        nc.sync.dma_start(out=lam_raw[64:66, :], in_=lam.partition_broadcast(2))
+
+        raw_meas = []
+        for pr in range(4):
+            raw_meas.append(keep.tile([128, 2, D], BF16, name="raw_meas%d" % pr))
+        meas_v = meas.rearrange("(g p t) d -> g p t d", g=2, p=128)
+        us_v = us.rearrange("(g p k) m -> g p k m", p=128, k=4)
+        raw_us = {}
+
+        def load_meas(pr):
+            nc.sync.dma_start(out=raw_meas[pr][:], in_=meas_v[pr // 2, :, 2 * (pr % 2) : 2 * (pr % 2) + 2, :])
+
+        load_meas(0)
+        for j in range(PM):
+            if j == 1:
+                load_meas(1)
+            for g in range(PD):
+                t = stage.tile([128, 4, 512], BF16, name="raw_us", tag="stage", bufs=6)
+                nc.sync.dma_start(out=t[:], in_=us_v[g, :, :, 512 * j : 512 * j + 512])
+                raw_us[j, g] = t
+        for q in range(4):
+            nc.sync.dma_start(
+                out=vs[32 * q : 32 * q + 4, :, :].bitcast(I32),
+                in_=vt_scales[:, 4 * q : 4 * q + 4, :].rearrange("g r n -> r g n").bitcast(I32),
+            )
+        vt = keep.tile([128, PM, 2 * P], U8, name="vt", align_bytes=64)
+        nc.sync.dma_start(out=vt[:], in_=vt_words.rearrange("g p n -> p g n"))
+        for pr in range(2, 4):
+            load_meas(pr)
+        b_raw = keep.tile([128, 4, F], U8, name="b_raw")
+        nc.sync.dma_start(out=b_raw[:], in_=basis_bytes.rearrange("(r p) f -> p r f", p=128))
+        b_scale = keep.tile([128, F], F32, name="b_scale")
+        nc.sync.dma_start(out=b_scale[:], in_=basis_scale.rearrange("o k -> (o k)").partition_broadcast(128))
+
+        s2 = keep.tile([128, PM * 4], F32, name="s2")
+        nc.vector.tensor_tensor(out=s2[:], in0=sig[:], in1=sig[:], op=MULT)
+        by_chunk = "k (g p t) -> k g t p"
+        lam_v = lam_raw[:].rearrange(by_chunk, g=2, t=4)
+        d_rhs_v = d_rhs[:].rearrange("k (g t p) -> k g t p", g=2, t=4)
+        nc.vector.tensor_tensor(out=d_rhs_v[0:64], in0=lam_v[0:64], in1=lam_v[0:64], op=MULT)
+        nc.gpsimd.tensor_copy(out=d_rhs_v[64:66], in_=lam_v[64:66])
+        lam_sq = keep.tile([128, F], F32, name="lam_sq")
+        nc.scalar.activation(
+            out=lam_sq[:].rearrange("k (g t p) -> k g t p", g=2, t=4)[0:64], in_=lam_v[0:64], func=ACT.Square
+        )
+        nc.vector.tensor_scalar(out=d_cols[:, :, 64], in0=s2[:], scalar1=2.0, scalar2=None, op0=MULT)
+        s4 = keep.tile([128, PM * 4], F32, name="s4")
+        nc.vector.tensor_tensor(out=s4[:], in0=s2[:], in1=s2[:], op=MULT)
+        nc.vector.scalar_tensor_tensor(out=d_cols[:, :, 65], in0=s2[:], scalar=2.0, in1=d_cols[:, :, 64], op0=MULT, op1=SUB)
+        nc.vector.tensor_copy(out=d_cols[:, :, 96], in_=s4[:])
+        rest = keep.tile([128, PM * 4], F32, name="rest")
+        nc.vector.tensor_tensor(out=rest[:], in0=s4[:], in1=d_cols[:, :, 96], op=SUB)
+        nc.vector.tensor_copy(out=d_cols[:, :, 97], in_=rest[:])
+        nc.vector.tensor_tensor(out=d_cols[:, :, 98], in0=rest[:], in1=d_cols[:, :, 97], op=SUB)
+        nc.vector.tensor_tensor(out=d_rhs[32:64, :], in0=lam_sq[32:64, :], in1=d_rhs[32:64, :], op=SUB)
+        d_lhs = keep.tile([128, PM * 4, 128], BF16, name="d_lhs")
+
+        def square_lhs():
+            d_turn = psum.tile([128, PM * 4, 128], BF16, name="d_turn", tag="acc", bufs=AB)
+            for i in range(PM * 4):
+                nc.tensor.transpose(d_turn[:, i, :], d_cols[:, i, :], ident_b[:])
+            nc.vector.tensor_copy(out=d_lhs[:], in_=d_turn[:])
+
+        copy_on = {"S": nc.scalar.copy, "V": nc.vector.tensor_copy}
+        r2, tiles = {}, {}
+
+        def weights(c, j):
+            bank = psum.tile([128, 4, 128], F32, name="wb", tag="tp", bufs=TP)
+            for t in range(4):
+                nc.tensor.matmul(
+                    out=bank[:, t, :],
+                    lhsT=d_lhs[:, 4 * j + t, :],
+                    rhs=d_rhs[:, 128 * c : 128 * c + 128],
+                    start=True,
+                    stop=True,
+                )
+            r2[c, j] = work.tile([128, 128, 4], F32, name="r2", bufs=16)
+            nc.scalar.activation(out=r2[c, j][:], in_=bank[:].rearrange("q t f -> q f t"), func=ACT.Abs_reciprocal_sqrt)
+
+        def turn_meas(pr, g, eng):
+            if g == 0:
+                tiles["mc", pr] = keep.tile([128, PD, 256], U32, name="mc%d" % pr, align_bytes=64)
+                tiles["ms", pr] = keep.tile([128, PD, 256], U8, name="ms%d" % pr, align_bytes=64)
+            words = raw_meas[pr][:].bitcast(F32)
+            tp = psum.tile([128, 2, 2, 128], F32, name="tp", tag="tp", bufs=TP)
+            for c in range(2):
+                for u in range(2):
+                    nc.tensor.transpose(tp[:, c, u, :], words[:, c, 256 * g + u : 256 * g + 256 : 2], ident[:])
+            grouped = work.tile([128, 1024], BF16, name="mg", align_bytes=64, bufs=4)
+            tiles["mg", pr, g] = grouped
+            dst = grouped[:].bitcast(F32).rearrange("p (c r u) -> p c r u", c=2, u=2)
+            copy_on[eng](out=dst, in_=tp[:].rearrange("p c u r -> p c r u"))
+
+        def quantize_meas(pr, g):
+            nc.vector.quantize_mx(
+                out=tiles["mc", pr][:, g, :].bitcast(FP8X4), scales=tiles["ms", pr][:, g, :], in_=tiles["mg", pr, g][:]
+            )
+
+        uc = keep.tile([128, PD, M], U32, name="uc", align_bytes=64)
+        usc = keep.tile([128, PD, M], U8, name="usc", align_bytes=64)
+
+        def group_us(j, g, eng):
+            grouped = work.tile([128, 4, 128, 4], BF16, name="ug", align_bytes=64, bufs=3)
+            tiles["ug", j, g] = grouped
+            copy_on[eng](out=grouped[:], in_=raw_us[j, g][:].rearrange("p k (q t) -> p t q k", t=4))
+
+        def quantize_us(j, g):
+            nc.vector.quantize_mx(
+                out=uc[:, g, 512 * j : 512 * j + 512].bitcast(FP8X4),
+                scales=usc[:, g, 512 * j : 512 * j + 512],
+                in_=tiles["ug", j, g][:].rearrange("p t q k -> p (t q k)"),
+            )
+
+        hb, hc, hs = {}, {}, {}
+
+        def project(c, j):
+            bank = psum.tile([128, 4, 128], F32, name="cb", tag="acc", bufs=AB)
+            pr, half = c // 2, c % 2
+            mc, ms = tiles["mc", pr], tiles["ms", pr]
+            for t in range(4):
+                col = 512 * j + 128 * t
+                for g in range(PD):
+                    nc.tensor.matmul_mx(
+                        out=bank[:, t, :],
+                        lhsT=uc[:, g, col : col + 128].bitcast(FP8X4),
+                        lhsT_scale=usc[:, g, col : col + 128],
+                        rhs=mc[:, g, 128 * half : 128 * half + 128].bitcast(FP8X4),
+                        rhs_scale=ms[:, g, 128 * half : 128 * half + 128],
+                        start=(g == 0),
+                        stop=(g == PD - 1),
+                    )
+            tiles["cb", c, j] = bank
+
+        def weigh(c, j):
+            if j == 0:
+                hb[c] = work.tile([128, PM, 128, 4], BF16, name="hb", align_bytes=64, bufs=6)
+            bank = tiles["cb", c, j]
+            nc.vector.tensor_tensor(out=hb[c][:, j], in0=bank[:].rearrange("q t f -> q f t"), in1=r2[c, j][:], op=MULT)
+
+        def quantize_chunk(c):
+            hc[c] = work.tile([128, PM, 128], U32, name="hc", align_bytes=64, bufs=3)
+            hs[c] = work.tile([128, PM, 128], U8, name="hs", align_bytes=64, bufs=3)
+            nc.vector.quantize_mx(
+                out=hc[c][:].rearrange("q j f -> q (j f)").bitcast(FP8X4),
+                scales=hs[c][:].rearrange("q j f -> q (j f)"),
+                in_=hb[c][:].rearrange("q j f t -> q (j f t)"),
+            )
+
+        image_v = image.rearrange("(g p t) n -> g t p n", g=2, p=128)
+
+        def image_part(c, n, eng):
+            if n % 2 == 0:
+                tiles["ob"] = stage.tile([128, 1024], F32, name="ob", tag="stage", bufs=6)
+            ob = tiles["ob"]
+            bank = psum.tile([128, 512], F32, name="ib", tag="acc", bufs=AB)
+            for j in range(PM):
+                nc.tensor.matmul_mx(
+                    out=bank[:],
+                    lhsT=hc[c][:, j, :].bitcast(FP8X4),
+                    lhsT_scale=hs[c][:, j, :],
+                    rhs=vt[:, j, 1024 * n : 1024 * n + 1024].bitcast(FP4X4),
+                    rhs_scale=vs[:, j, 512 * n : 512 * n + 512],
+                    start=(j == 0),
+                    stop=(j == PM - 1),
+                )
+            copy_on[eng](out=ob[:, 512 * (n % 2) : 512 * (n % 2) + 512], in_=bank[:])
+            if n % 2 == 1:
+                two = slice(512 * n - 512, 512 * n + 512)
+                nc.sync.dma_start(out=image_v[c // 4, c % 4, :, two], in_=ob[:])
+
+        bc = keep.tile([128, PF, R], U32, name="bc", align_bytes=64)
+        bsc = keep.tile([128, PF, R], U8, name="bsc", align_bytes=64)
+
+        def widen_basis(r):
+            tiles["bw", r] = keep.tile([128, F], BF16, name="bw%d" % r)
+            nc.vector.tensor_tensor(out=tiles["bw", r][:], in0=b_raw[:, r, :].bitcast(E4M3), in1=b_scale[:], op=MULT)
+
+        def turn_basis(g, h, eng):
+            if h == 0:
+                tiles["bg", g] = work.tile([128, 2, 1024], BF16, name="bg", align_bytes=64)
+            tp = psum.tile([128, 2, 2, 128], F32, name="tp", tag="tp", bufs=TP)
+            for r in range(2):
+                words = tiles["bw", 2 * h + r][:].bitcast(F32)
+                for u in range(2):
+                    nc.tensor.transpose(tp[:, r, u, :], words[:, 256 * g + u : 256 * g + 256 : 2], ident[:])
+            dst = tiles["bg", g][:, h].bitcast(F32).rearrange("p (r n u) -> p r n u", r=2, u=2)
+            copy_on[eng](out=dst, in_=tp[:].rearrange("p r u n -> p r n u"))
+
+        def quantize_basis(g):
+            nc.vector.quantize_mx(
+                out=bc[:, g, :].bitcast(FP8X4), scales=bsc[:, g, :], in_=tiles["bg", g][:].rearrange("p h n -> p (h n)")
+            )
+
+        ac, asc = {}, {}
+
+        def turn_group(g, j, u, eng):
+            if u == 0:
+                if j == 0:
+                    ac[g] = keep.tile([128, PM, 512], U32, name="ac%d" % g, align_bytes=64)
+                    asc[g] = keep.tile([128, PM, 512], U8, name="asc%d" % g, align_bytes=64)
+                tiles["ha"] = work.tile([128, 2, 256, 4], BF16, name="ha", align_bytes=64)
+            tp = psum.tile([128, 4, 128], F32, name="tp", tag="tp", bufs=TP)
+            for t in range(4):
+                words = hb[4 * g + t][:, j].rearrange("q f t -> q (f t)").bitcast(F32)
+                nc.tensor.transpose(tp[:, t, :], words[:, u:256:2], ident[:])
+            copy_on[eng](out=tiles["ha"][:, u], in_=tp[:].bitcast(BF16).rearrange("p t n -> p n t"))
+            tiles["ha", g, j] = tiles["ha"]
+
+        def quantize_group(g, j):
+            nc.vector.quantize_mx(
+                out=ac[g][:, j, :].bitcast(FP8X4), scales=asc[g][:, j, :], in_=tiles["ha", g, j][:].rearrange("p u n t -> p (u n t)")
+            )
+
+        def comps_part(r, j, eng):
+            if j == 0:
+                tiles["co"] = stage.tile([128, M], F32, name="co", tag="stage", bufs=6)
+            co = tiles["co"]
+            bank = psum.tile([128, 512], F32, name="ib", tag="acc", bufs=AB)
+            for g in range(PF):
+                nc.tensor.matmul_mx(
+                    out=bank[:],
+                    lhsT=bc[:, g, 128 * r : 128 * r + 128].bitcast(FP8X4),
+                    lhsT_scale=bsc[:, g, 128 * r : 128 * r + 128],
+                    rhs=ac[g][:, j, :].bitcast(FP8X4),
+                    rhs_scale=asc[g][:, j, :],
+                    start=(g == 0),
+                    stop=(g == PF - 1),
+                )
+            cols = slice(512 * j, 512 * j + 512)
+            copy_on[eng](
+                out=co[:, cols].rearrange("p (q u e) -> p q u e", u=2, e=2), in_=bank[:].rearrange("p (u q e) -> p q u e", u=2, e=2)
+            )
+            nc.sync.dma_start(out=comps[128 * r : 128 * r + 128, cols], in_=co[:, cols])
+
+        square_lhs()
+        for g in range(PD):
+            turn_meas(0, g, "S")
+        group_us(0, 0, "V")
+        group_us(0, 1, "S")
+        quantize_meas(0, 0)
+        quantize_us(0, 0)
+        quantize_meas(0, 1)
+        quantize_meas(0, 2)
+        group_us(0, 2, "V")
+        weights(0, 0)
+        quantize_us(0, 1)
+        quantize_us(0, 2)
+        for g in range(PD):
+            turn_meas(1, g, "S")
+        project(0, 0)
+        project(1, 0)
+        group_us(1, 0, "V")
+        group_us(1, 1, "S")
+        quantize_us(1, 0)
+        for g in range(PD):
+            quantize_meas(1, g)
+        weights(1, 0)
+        weights(0, 1)
+        project(2, 0)
+        project(3, 0)
+        group_us(1, 2, "V")
+        quantize_us(1, 1)
+        weigh(0, 0)
+        quantize_us(1, 2)
+        weights(1, 1)
+        project(0, 1)
+        weights(2, 0)
+        weigh(1, 0)
+        weigh(0, 1)
+        project(1, 1)
+        quantize_chunk(0)
+        weigh(2, 0)
+        weights(2, 1)
+        weigh(1, 1)
+        weights(3, 0)
+        side = [(("T", 2),), (("T", 3),), (("A", 0),), (), (("B", 0),), (("B", 1),), (("A", 1),), ()]
+        for c in range(8):
+            nxt = c + 2
+            if c == 4:
+                weights(c + 3, 0)
+            if 4 <= nxt < 8:
+                project(nxt, 0)
+            image_part(c, 0, "V")
+            if 4 <= nxt < 8:
+                weigh(nxt, 0)
+            if nxt == 3:
+                weigh(3, 0)
+            if c < 7:
+                quantize_chunk(c + 1)
+            image_part(c, 1, "S")
+            if nxt < 8:
+                project(nxt, 1)
+            if c < 5:
+                weights(c + 3, 1)
+            for kind, i in side[c]:
+                if kind == "T":
+                    for g in range(PD):
+                        turn_meas(i, g, "S")
+                if kind == "A":
+                    for j in range(PM):
+                        turn_group(i, j, 0, "V")
+                        turn_group(i, j, 1, "S")
+                if kind == "B":
+                    turn_basis(i, 0, "S")
+                    turn_basis(i, 1, "S")
+            if nxt < 8:
+                weigh(nxt, 1)
+            image_part(c, 2, "S")
+            if c < 3:
+                weights(c + 4, 0)
+            image_part(c, 3, "V" if c > 5 else "S")
+            for kind, i in side[c]:
+                if kind == "T":
+                    for g in range(PD):
+                        quantize_meas(i, g)
+                if kind == "A":
+                    for j in range(PM):
+                        quantize_group(i, j)
+                if kind == "B":
+                    quantize_basis(i)
+            if c == 3:
+                for r in range(4):
+                    widen_basis(r)
+        for r in range(4):
+            for j in range(PM):
+                comps_part(r, j, "VS"[j])

@@ -21,7 +21,8 @@ SUB = mybir.AluOpType.subtract
 PD = D // 512
 PM = M // 512
 PF = F // 512
-AB, TP = 5, 3
+UNITS = 4
+BANKS = 8
 
 
 def tile_spectral_tikhonov_imaging_s8_kernel(
@@ -31,354 +32,400 @@ def tile_spectral_tikhonov_imaging_s8_kernel(
     with ExitStack() as ctx:
         keep = ctx.enter_context(tc.tile_pool(name="keep", bufs=1))
         work = ctx.enter_context(tc.tile_pool(name="work", bufs=2))
-        stage = ctx.enter_context(tc.tile_pool(name="stage", bufs=6))
+        stage = ctx.enter_context(tc.tile_pool(name="stage", bufs=8))
         psum = ctx.enter_context(tc.psum_pool(name="psum", bufs=1))
 
         ctx.enter_context(tc.manual_schedule())
 
-        lam_raw = keep.tile([128, F], BF16, name="lam_raw")
-        nc.vector.memset(lam_raw[0:64, :], 0.0)
-        d_rhs = keep.tile([128, F], BF16, name="d_rhs")
-        nc.gpsimd.memset(d_rhs[:], 1.0)
-        d_cols = keep.tile([128, PM * 4, 128], BF16, name="d_cols")
-        nc.vector.memset(d_cols[:], 0.0)
-        nc.vector.memset(d_cols[:, :, 0:33:32], 1.0)
-        warm = keep.tile([128, 1], F32, name="warm")
-        nc.vector.memset(warm[:], 1.0)
-        nc.scalar.activation(out=warm[:], in_=warm[:], func=ACT.Abs_reciprocal_sqrt)
+        taken = []
+
+        def next_bank(shape, name):
+            taken.append(name)
+            return psum.tile(shape, F32, name=name, tag="bank%d" % (len(taken) % BANKS), bufs=1)
+
+        factors = keep.tile([128, 2, 8, 128], BF16, name="factors")
+        nc.vector.memset(factors[:], 0.0)
+        vs = keep.tile([128, PM, P], U8, name="vs", align_bytes=64)
+        nc.vector.memset(vs[:].bitcast(I32), 0)
         ident = keep.tile([128, 128], F32, name="ident")
         make_identity(nc, ident[:])
         ident_b = keep.tile([128, 128], BF16, name="ident_b")
-        make_identity(nc, ident_b[:])
-        vs = keep.tile([128, PM, P], U8, name="vs", align_bytes=64)
-        nc.gpsimd.memset(vs[:].bitcast(I32), 0)
+        nc.vector.tensor_copy(out=ident_b[:], in_=ident[:])
 
-        sig = keep.tile([128, PM * 4], BF16, name="sig")
-        nc.sync.dma_start(out=sig[:].rearrange("q (j t) -> q j t", j=PM), in_=sigma.rearrange("(j q t) -> q j t", j=PM, q=128))
-        nc.sync.dma_start(out=lam_raw[0:64:32, :], in_=lam.partition_broadcast(2))
-        nc.sync.dma_start(out=lam_raw[64:66, :], in_=lam.partition_broadcast(2))
-
-        raw_meas = []
-        for pr in range(4):
-            raw_meas.append(keep.tile([128, 2, D], BF16, name="raw_meas%d" % pr))
-        meas_v = meas.rearrange("(g p t) d -> g p t d", g=2, p=128)
+        raw_meas, raw_us = {}, {}
+        meas_v = meas.rearrange("(g p t) d -> g p t d", g=PF, p=128)
         us_v = us.rearrange("(g p k) m -> g p k m", p=128, k=4)
-        raw_us = {}
 
-        def load_meas(pr):
-            nc.sync.dma_start(out=raw_meas[pr][:], in_=meas_v[pr // 2, :, 2 * (pr % 2) : 2 * (pr % 2) + 2, :])
+        def load_meas(un):
+            raw_meas[un] = keep.tile([128, 2, D], BF16, name="raw_meas%d" % un)
+            nc.sync.dma_start(out=raw_meas[un][:], in_=meas_v[un // 2, :, 2 * (un % 2) : 2 * (un % 2) + 2, :])
 
+        def load_us(j, g):
+            raw_us[j, g] = stage.tile([128, 4, 512], BF16, name="raw_us", tag="stage", bufs=8)
+            nc.sync.dma_start(out=raw_us[j, g][:], in_=us_v[g, :, :, 512 * j : 512 * j + 512])
+
+        roots = keep.tile([128, 2, 16], BF16, name="roots")
+        for i, vec in enumerate((lam, sigma)):
+            nc.scalar.dma_start(out=roots[:, i, 0:8].rearrange("q (g t) -> q g t", t=4), in_=vec.rearrange("(g q t) -> q g t", q=128, t=4))
+        nc.scalar.activation(out=factors[:, 1, :, 0:2], in_=factors[:, 1, :, 8:10], func=ACT.Abs_reciprocal_sqrt, bias=1.0)
+        nc.scalar.activation(out=factors[:, 0, :, 4:8], in_=factors[:, 0, :, 8:12], func=ACT.Abs_reciprocal_sqrt, bias=1.0)
+        load_us(0, 0)
         load_meas(0)
-        for j in range(PM):
-            if j == 1:
-                load_meas(1)
-            for g in range(PD):
-                t = stage.tile([128, 4, 512], BF16, name="raw_us", tag="stage", bufs=6)
-                nc.sync.dma_start(out=t[:], in_=us_v[g, :, :, 512 * j : 512 * j + 512])
-                raw_us[j, g] = t
+        load_us(0, 1)
+        load_us(0, 2)
+        load_meas(1)
+        load_us(1, 0)
+        load_us(1, 1)
+        load_meas(2)
+        load_us(1, 2)
         for q in range(4):
-            nc.sync.dma_start(
+            nc.gpsimd.dma_start(
                 out=vs[32 * q : 32 * q + 4, :, :].bitcast(I32),
                 in_=vt_scales[:, 4 * q : 4 * q + 4, :].rearrange("g r n -> r g n").bitcast(I32),
             )
         vt = keep.tile([128, PM, 2 * P], U8, name="vt", align_bytes=64)
         nc.sync.dma_start(out=vt[:], in_=vt_words.rearrange("g p n -> p g n"))
-        for pr in range(2, 4):
-            load_meas(pr)
+        load_meas(3)
         b_raw = keep.tile([128, 4, F], U8, name="b_raw")
         nc.sync.dma_start(out=b_raw[:], in_=basis_bytes.rearrange("(r p) f -> p r f", p=128))
-        b_scale = keep.tile([128, F], F32, name="b_scale")
-        nc.sync.dma_start(out=b_scale[:], in_=basis_scale.rearrange("o k -> (o k)").partition_broadcast(128))
+        b_scale = keep.tile([128, PF, 4], F32, name="b_scale")
+        nc.sync.dma_start(out=b_scale[:], in_=basis_scale.rearrange("o (g p t) -> p (o g) t", p=128, t=4))
 
-        s2 = keep.tile([128, PM * 4], F32, name="s2")
-        nc.vector.tensor_tensor(out=s2[:], in0=sig[:], in1=sig[:], op=MULT)
-        by_chunk = "k (g p t) -> k g t p"
-        lam_v = lam_raw[:].rearrange(by_chunk, g=2, t=4)
-        d_rhs_v = d_rhs[:].rearrange("k (g t p) -> k g t p", g=2, t=4)
-        nc.vector.tensor_tensor(out=d_rhs_v[0:64], in0=lam_v[0:64], in1=lam_v[0:64], op=MULT)
-        nc.gpsimd.tensor_copy(out=d_rhs_v[64:66], in_=lam_v[64:66])
-        lam_sq = keep.tile([128, F], F32, name="lam_sq")
-        nc.scalar.activation(
-            out=lam_sq[:].rearrange("k (g t p) -> k g t p", g=2, t=4)[0:64], in_=lam_v[0:64], func=ACT.Square
-        )
-        nc.vector.tensor_scalar(out=d_cols[:, :, 64], in0=s2[:], scalar1=2.0, scalar2=None, op0=MULT)
+        squares = keep.tile([128, 2, 8], F32, name="squares")
+        nc.vector.tensor_tensor(out=squares[:], in0=roots[:, :, 0:8], in1=roots[:, :, 0:8], op=MULT)
+        nc.vector.tensor_copy(out=factors[:, 0, :, 2:4], in_=roots[:, 0, 0:8].unsqueeze(2).to_broadcast([128, 8, 2]))
+        nc.vector.tensor_copy(out=factors[:, 0, :, 0], in_=squares[:, 0, :])
         s4 = keep.tile([128, PM * 4], F32, name="s4")
-        nc.vector.tensor_tensor(out=s4[:], in0=s2[:], in1=s2[:], op=MULT)
-        nc.vector.scalar_tensor_tensor(out=d_cols[:, :, 65], in0=s2[:], scalar=2.0, in1=d_cols[:, :, 64], op0=MULT, op1=SUB)
-        nc.vector.tensor_copy(out=d_cols[:, :, 96], in_=s4[:])
+        nc.vector.tensor_tensor(out=s4[:], in0=squares[:, 1, :], in1=squares[:, 1, :], op=MULT)
+        nc.vector.tensor_scalar(out=factors[:, 1, :, 2], in0=squares[:, 1, :], scalar1=2.0, scalar2=None, op0=MULT)
+        nc.vector.tensor_tensor(out=factors[:, 0, :, 1], in0=squares[:, 0, :], in1=factors[:, 0, :, 0], op=SUB)
+        nc.vector.tensor_copy(out=factors[:, 1, :, 4], in_=s4[:])
+        nc.vector.scalar_tensor_tensor(
+            out=factors[:, 1, :, 3], in0=squares[:, 1, :], scalar=2.0, in1=factors[:, 1, :, 2], op0=MULT, op1=SUB
+        )
         rest = keep.tile([128, PM * 4], F32, name="rest")
-        nc.vector.tensor_tensor(out=rest[:], in0=s4[:], in1=d_cols[:, :, 96], op=SUB)
-        nc.vector.tensor_copy(out=d_cols[:, :, 97], in_=rest[:])
-        nc.vector.tensor_tensor(out=d_cols[:, :, 98], in0=rest[:], in1=d_cols[:, :, 97], op=SUB)
-        nc.vector.tensor_tensor(out=d_rhs[32:64, :], in0=lam_sq[32:64, :], in1=d_rhs[32:64, :], op=SUB)
-        d_lhs = keep.tile([128, PM * 4, 128], BF16, name="d_lhs")
+        nc.vector.tensor_tensor(out=rest[:], in0=s4[:], in1=factors[:, 1, :, 4], op=SUB)
+        nc.vector.tensor_copy(out=factors[:, 1, :, 5], in_=rest[:])
+        nc.vector.tensor_tensor(out=factors[:, 1, :, 6], in0=rest[:], in1=factors[:, 1, :, 5], op=SUB)
+        rows = keep.tile([128, 2, 8, 128], BF16, name="rows")
 
-        def square_lhs():
-            d_turn = psum.tile([128, PM * 4, 128], BF16, name="d_turn", tag="acc", bufs=AB)
-            for i in range(PM * 4):
-                nc.tensor.transpose(d_turn[:, i, :], d_cols[:, i, :], ident_b[:])
-            nc.vector.tensor_copy(out=d_lhs[:], in_=d_turn[:])
+        def turn_factors(i, eng):
+            taken.append("ft")
+            bank = psum.tile([128, 8, 128], BF16, name="ft", tag="bank%d" % (len(taken) % BANKS), bufs=1)
+            for c in range(8):
+                nc.tensor.transpose(bank[:, c, :], factors[:, i, c, :], ident_b[:])
+            copy_on[eng](out=rows[:, i], in_=bank[:])
 
         copy_on = {"S": nc.scalar.copy, "V": nc.vector.tensor_copy}
-        r2, tiles = {}, {}
+        tiles = {}
 
-        def weights(c, j):
-            bank = psum.tile([128, 4, 128], F32, name="wb", tag="tp", bufs=TP)
-            for t in range(4):
+        def weights(un, j, th):
+            bank = next_bank([128, 2, 2, 128], "wb")
+            for i in range(2):
                 nc.tensor.matmul(
-                    out=bank[:, t, :],
-                    lhsT=d_lhs[:, 4 * j + t, :],
-                    rhs=d_rhs[:, 128 * c : 128 * c + 128],
+                    out=bank[:, i].rearrange("q e r -> q (e r)"),
+                    lhsT=rows[:, 1, 4 * j + 2 * th + i, :],
+                    rhs=rows[:, 0, 2 * un : 2 * un + 2, :].rearrange("k e r -> k (e r)"),
                     start=True,
                     stop=True,
                 )
-            r2[c, j] = work.tile([128, 128, 4], F32, name="r2", bufs=16)
-            nc.scalar.activation(out=r2[c, j][:], in_=bank[:].rearrange("q t f -> q f t"), func=ACT.Abs_reciprocal_sqrt)
+            tiles["rw", un, j, th] = work.tile([128, 2, 128, 2], F32, name="rw", bufs=8)
+            nc.scalar.activation(
+                out=tiles["rw", un, j, th][:], in_=bank[:].rearrange("q i e r -> q i r e"), func=ACT.Abs_reciprocal_sqrt
+            )
 
-        def turn_meas(pr, g, eng):
+        def turn_meas(un, g, eng):
             if g == 0:
-                tiles["mc", pr] = keep.tile([128, PD, 256], U32, name="mc%d" % pr, align_bytes=64)
-                tiles["ms", pr] = keep.tile([128, PD, 256], U8, name="ms%d" % pr, align_bytes=64)
-            words = raw_meas[pr][:].bitcast(F32)
-            tp = psum.tile([128, 2, 2, 128], F32, name="tp", tag="tp", bufs=TP)
-            for c in range(2):
-                for u in range(2):
-                    nc.tensor.transpose(tp[:, c, u, :], words[:, c, 256 * g + u : 256 * g + 256 : 2], ident[:])
+                tiles["mc", un] = keep.tile([128, PD, 256], U32, name="mc%d" % un, align_bytes=64)
+                tiles["ms", un] = keep.tile([128, PD, 256], U8, name="ms%d" % un, align_bytes=64)
+            words = raw_meas[un][:].bitcast(F32)
+            bank = next_bank([128, 2, 2, 128], "mt")
+            for e in range(2):
+                for w in range(2):
+                    nc.tensor.transpose(bank[:, e, w, :], words[:, e, 256 * g + w : 256 * g + 256 : 2], ident[:])
             grouped = work.tile([128, 1024], BF16, name="mg", align_bytes=64, bufs=4)
-            tiles["mg", pr, g] = grouped
-            dst = grouped[:].bitcast(F32).rearrange("p (c r u) -> p c r u", c=2, u=2)
-            copy_on[eng](out=dst, in_=tp[:].rearrange("p c u r -> p c r u"))
+            tiles["mg", un, g] = grouped
+            dst = grouped[:].bitcast(F32).rearrange("p (r e w) -> p r e w", e=2, w=2)
+            copy_on[eng](out=dst, in_=bank[:].rearrange("p e w r -> p r e w"))
 
-        def quantize_meas(pr, g):
+        def quantize_meas(un, g):
             nc.vector.quantize_mx(
-                out=tiles["mc", pr][:, g, :].bitcast(FP8X4), scales=tiles["ms", pr][:, g, :], in_=tiles["mg", pr, g][:]
+                out=tiles["mc", un][:, g, :].bitcast(FP8X4), scales=tiles["ms", un][:, g, :], in_=tiles["mg", un, g][:]
             )
 
         uc = keep.tile([128, PD, M], U32, name="uc", align_bytes=64)
         usc = keep.tile([128, PD, M], U8, name="usc", align_bytes=64)
 
-        def group_us(j, g, eng):
-            grouped = work.tile([128, 4, 128, 4], BF16, name="ug", align_bytes=64, bufs=3)
-            tiles["ug", j, g] = grouped
-            copy_on[eng](out=grouped[:], in_=raw_us[j, g][:].rearrange("p k (q t) -> p t q k", t=4))
+        def group_us(j, g, eng, lo, hi):
+            if lo == 0:
+                tiles["ug", j, g] = work.tile([128, 2048], BF16, name="ug", align_bytes=64, bufs=3)
+            dst = tiles["ug", j, g][:].rearrange("p (t a b k) -> p a t b k", t=4, b=2, k=4)
+            src = raw_us[j, g][:].rearrange("p k (a b t) -> p a t b k", b=2, t=4)
+            copy_on[eng](out=dst[:, lo:hi], in_=src[:, lo:hi])
 
         def quantize_us(j, g):
             nc.vector.quantize_mx(
                 out=uc[:, g, 512 * j : 512 * j + 512].bitcast(FP8X4),
                 scales=usc[:, g, 512 * j : 512 * j + 512],
-                in_=tiles["ug", j, g][:].rearrange("p t q k -> p (t q k)"),
+                in_=tiles["ug", j, g][:],
             )
 
-        hb, hc, hs = {}, {}, {}
-
-        def project(c, j):
-            bank = psum.tile([128, 4, 128], F32, name="cb", tag="acc", bufs=AB)
-            pr, half = c // 2, c % 2
-            mc, ms = tiles["mc", pr], tiles["ms", pr]
-            for t in range(4):
-                col = 512 * j + 128 * t
+        def project(un, j, th):
+            bank = next_bank([128, 2, 256], "cb")
+            for i in range(2):
+                col = 512 * j + 128 * (2 * th + i)
                 for g in range(PD):
                     nc.tensor.matmul_mx(
-                        out=bank[:, t, :],
+                        out=bank[:, i, :],
                         lhsT=uc[:, g, col : col + 128].bitcast(FP8X4),
                         lhsT_scale=usc[:, g, col : col + 128],
-                        rhs=mc[:, g, 128 * half : 128 * half + 128].bitcast(FP8X4),
-                        rhs_scale=ms[:, g, 128 * half : 128 * half + 128],
+                        rhs=tiles["mc", un][:, g, :].bitcast(FP8X4),
+                        rhs_scale=tiles["ms", un][:, g, :],
                         start=(g == 0),
                         stop=(g == PD - 1),
                     )
-            tiles["cb", c, j] = bank
+            tiles["cb", un, j, th] = bank
 
-        def weigh(c, j):
+        def weigh(un, j, th):
+            if (j, th) == (0, 0):
+                tiles["hn", un] = keep.tile([128, PM * 4, 256], BF16, name="hn%d" % un)
+            places = slice(4 * j + 2 * th, 4 * j + 2 * th + 2)
+            weight = tiles["rw", un, j, th][:].rearrange("q i r e -> q i (r e)")
+            nc.vector.tensor_tensor(out=tiles["hn", un][:, places, :], in0=tiles["cb", un, j, th][:], in1=weight, op=MULT)
+
+        def group_h(un, j, eng):
+            tiles["ha", un, j] = work.tile([128, 1024], BF16, name="ha", align_bytes=64, bufs=4)
+            dst = tiles["ha", un, j][:].rearrange("q (e a b t) -> q a e b t", e=2, b=4, t=4)
+            src = tiles["hn", un][:, 4 * j : 4 * j + 4, :].rearrange("q t (a b e) -> q a e b t", b=4, e=2)
+            copy_on[eng](out=dst, in_=src)
+
+        def quantize_h(un, j):
             if j == 0:
-                hb[c] = work.tile([128, PM, 128, 4], BF16, name="hb", align_bytes=64, bufs=6)
-            bank = tiles["cb", c, j]
-            nc.vector.tensor_tensor(out=hb[c][:, j], in0=bank[:].rearrange("q t f -> q f t"), in1=r2[c, j][:], op=MULT)
-
-        def quantize_chunk(c):
-            hc[c] = work.tile([128, PM, 128], U32, name="hc", align_bytes=64, bufs=3)
-            hs[c] = work.tile([128, PM, 128], U8, name="hs", align_bytes=64, bufs=3)
+                tiles["hc", un] = keep.tile([128, PM, 256], U32, name="hc%d" % un, align_bytes=64)
+                tiles["hs", un] = keep.tile([128, PM, 256], U8, name="hs%d" % un, align_bytes=64)
             nc.vector.quantize_mx(
-                out=hc[c][:].rearrange("q j f -> q (j f)").bitcast(FP8X4),
-                scales=hs[c][:].rearrange("q j f -> q (j f)"),
-                in_=hb[c][:].rearrange("q j f t -> q (j f t)"),
+                out=tiles["hc", un][:, j, :].bitcast(FP8X4), scales=tiles["hs", un][:, j, :], in_=tiles["ha", un, j][:]
             )
 
-        image_v = image.rearrange("(g p t) n -> g t p n", g=2, p=128)
+        image_v = image.rearrange("(g p t) n -> g t p n", g=PF, p=128)
 
-        def image_part(c, n, eng):
+        def image_part(un, e, n, eng):
             if n % 2 == 0:
-                tiles["ob"] = stage.tile([128, 1024], F32, name="ob", tag="stage", bufs=6)
+                tiles["ob"] = stage.tile([128, 1024], F32, name="ob", tag="stage", bufs=8)
             ob = tiles["ob"]
-            bank = psum.tile([128, 512], F32, name="ib", tag="acc", bufs=AB)
+            bank = next_bank([128, 512], "ib")
+            cols = slice(128 * e, 128 * e + 128)
             for j in range(PM):
                 nc.tensor.matmul_mx(
                     out=bank[:],
-                    lhsT=hc[c][:, j, :].bitcast(FP8X4),
-                    lhsT_scale=hs[c][:, j, :],
+                    lhsT=tiles["hc", un][:, j, cols].bitcast(FP8X4),
+                    lhsT_scale=tiles["hs", un][:, j, cols],
                     rhs=vt[:, j, 1024 * n : 1024 * n + 1024].bitcast(FP4X4),
                     rhs_scale=vs[:, j, 512 * n : 512 * n + 512],
                     start=(j == 0),
                     stop=(j == PM - 1),
                 )
             copy_on[eng](out=ob[:, 512 * (n % 2) : 512 * (n % 2) + 512], in_=bank[:])
-            if n % 2 == 1:
-                two = slice(512 * n - 512, 512 * n + 512)
-                nc.sync.dma_start(out=image_v[c // 4, c % 4, :, two], in_=ob[:])
+            rows_out = image_v[un // 2, 2 * (un % 2) + e]
+            if (un, e) == (UNITS - 1, 1) and n >= 2:
+                nc.sync.dma_start(out=rows_out[:, 512 * n : 512 * n + 512], in_=ob[:, 512 * (n % 2) : 512 * (n % 2) + 512])
+            elif n % 2 == 1:
+                nc.sync.dma_start(out=rows_out[:, 512 * n - 512 : 512 * n + 512], in_=ob[:])
 
         bc = keep.tile([128, PF, R], U32, name="bc", align_bytes=64)
         bsc = keep.tile([128, PF, R], U8, name="bsc", align_bytes=64)
 
-        def widen_basis(r):
+        def widen_basis(r, eng):
             tiles["bw", r] = keep.tile([128, F], BF16, name="bw%d" % r)
-            nc.vector.tensor_tensor(out=tiles["bw", r][:], in0=b_raw[:, r, :].bitcast(E4M3), in1=b_scale[:], op=MULT)
+            copy_on[eng](out=tiles["bw", r][:], in_=b_raw[:, r, :].bitcast(E4M3))
 
-        def turn_basis(g, h, eng):
+        def turn_basis(g, h):
             if h == 0:
-                tiles["bg", g] = work.tile([128, 2, 1024], BF16, name="bg", align_bytes=64)
-            tp = psum.tile([128, 2, 2, 128], F32, name="tp", tag="tp", bufs=TP)
+                tiles["bg", g] = work.tile([128, 2048], BF16, name="bg", align_bytes=64)
+            bank = next_bank([128, 2, 2, 128], "bt")
             for r in range(2):
                 words = tiles["bw", 2 * h + r][:].bitcast(F32)
-                for u in range(2):
-                    nc.tensor.transpose(tp[:, r, u, :], words[:, 256 * g + u : 256 * g + 256 : 2], ident[:])
-            dst = tiles["bg", g][:, h].bitcast(F32).rearrange("p (r n u) -> p r n u", r=2, u=2)
-            copy_on[eng](out=dst, in_=tp[:].rearrange("p r u n -> p r n u"))
+                for w in range(2):
+                    nc.tensor.transpose(bank[:, w, r, :], words[:, 256 * g + w : 256 * g + 256 : 2], ident[:])
+            src = bank[:].rearrange("p w r n -> p w (r n)").bitcast(BF16).rearrange("p w (c e) -> p c w e", e=2)
+            dst = tiles["bg", g][:, 1024 * h : 1024 * h + 1024].rearrange("p (c w e) -> p c w e", w=2, e=2)
+            scale = b_scale[:, g, :].rearrange("p (w e) -> p w e", e=2).unsqueeze(1).to_broadcast([128, 256, 2, 2])
+            nc.vector.tensor_tensor(out=dst, in0=src, in1=scale, op=MULT)
 
         def quantize_basis(g):
-            nc.vector.quantize_mx(
-                out=bc[:, g, :].bitcast(FP8X4), scales=bsc[:, g, :], in_=tiles["bg", g][:].rearrange("p h n -> p (h n)")
-            )
+            nc.vector.quantize_mx(out=bc[:, g, :].bitcast(FP8X4), scales=bsc[:, g, :], in_=tiles["bg", g][:])
 
-        ac, asc = {}, {}
+        ac = keep.tile([128, PF, M], U32, name="ac", align_bytes=64)
+        asc = keep.tile([128, PF, M], U8, name="asc", align_bytes=64)
 
-        def turn_group(g, j, u, eng):
-            if u == 0:
-                if j == 0:
-                    ac[g] = keep.tile([128, PM, 512], U32, name="ac%d" % g, align_bytes=64)
-                    asc[g] = keep.tile([128, PM, 512], U8, name="asc%d" % g, align_bytes=64)
-                tiles["ha"] = work.tile([128, 2, 256, 4], BF16, name="ha", align_bytes=64)
-            tp = psum.tile([128, 4, 128], F32, name="tp", tag="tp", bufs=TP)
-            for t in range(4):
-                words = hb[4 * g + t][:, j].rearrange("q f t -> q (f t)").bitcast(F32)
-                nc.tensor.transpose(tp[:, t, :], words[:, u:256:2], ident[:])
-            copy_on[eng](out=tiles["ha"][:, u], in_=tp[:].bitcast(BF16).rearrange("p t n -> p n t"))
-            tiles["ha", g, j] = tiles["ha"]
+        def turn_h(g, j, th, eng):
+            if th == 0:
+                tiles["hb", g, j] = work.tile([128, 2048], BF16, name="hb", align_bytes=64, bufs=4)
+            bank = next_bank([128, 2, 2, 128], "ht")
+            for u in range(2):
+                words = tiles["hn", 2 * g + u][:].bitcast(F32)
+                for i in range(2):
+                    nc.tensor.transpose(bank[:, u, i, :], words[:, 4 * j + 2 * th + i, :], ident[:])
+            dst = tiles["hb", g, j][:, 1024 * th : 1024 * th + 1024].bitcast(F32).rearrange("p (c u) -> p c u", u=2)
+            copy_on[eng](out=dst, in_=bank[:].rearrange("p u i q -> p (i q) u"))
 
-        def quantize_group(g, j):
-            nc.vector.quantize_mx(
-                out=ac[g][:, j, :].bitcast(FP8X4), scales=asc[g][:, j, :], in_=tiles["ha", g, j][:].rearrange("p u n t -> p (u n t)")
-            )
+        def quantize_hb(g, j):
+            cols = slice(512 * j, 512 * j + 512)
+            nc.vector.quantize_mx(out=ac[:, g, cols].bitcast(FP8X4), scales=asc[:, g, cols], in_=tiles["hb", g, j][:])
 
         def comps_part(r, j, eng):
             if j == 0:
-                tiles["co"] = stage.tile([128, M], F32, name="co", tag="stage", bufs=6)
+                tiles["co"] = stage.tile([128, M], F32, name="co", tag="stage", bufs=8)
             co = tiles["co"]
-            bank = psum.tile([128, 512], F32, name="ib", tag="acc", bufs=AB)
+            bank = next_bank([128, 512], "kb")
+            cols = slice(512 * j, 512 * j + 512)
             for g in range(PF):
                 nc.tensor.matmul_mx(
                     out=bank[:],
                     lhsT=bc[:, g, 128 * r : 128 * r + 128].bitcast(FP8X4),
                     lhsT_scale=bsc[:, g, 128 * r : 128 * r + 128],
-                    rhs=ac[g][:, j, :].bitcast(FP8X4),
-                    rhs_scale=asc[g][:, j, :],
+                    rhs=ac[:, g, cols].bitcast(FP8X4),
+                    rhs_scale=asc[:, g, cols],
                     start=(g == 0),
                     stop=(g == PF - 1),
                 )
-            cols = slice(512 * j, 512 * j + 512)
-            copy_on[eng](
-                out=co[:, cols].rearrange("p (q u e) -> p q u e", u=2, e=2), in_=bank[:].rearrange("p (u q e) -> p q u e", u=2, e=2)
-            )
-            nc.sync.dma_start(out=comps[128 * r : 128 * r + 128, cols], in_=co[:, cols])
+            copy_on[eng](out=co[:, cols].rearrange("p (q t) -> p q t", t=4), in_=bank[:].rearrange("p (t q) -> p q t", t=4))
+            if j == PM - 1:
+                nc.sync.dma_start(out=comps[128 * r : 128 * r + 128, :], in_=co[:])
 
-        square_lhs()
-        for g in range(PD):
-            turn_meas(0, g, "S")
-        group_us(0, 0, "V")
-        group_us(0, 1, "S")
-        quantize_meas(0, 0)
+        def both(step, un, j):
+            for th in range(2):
+                step(un, j, th)
+
+        def image_banks(un, e, first, engs):
+            for i, eng in enumerate(engs):
+                image_part(un, e, first + i, eng)
+
+        def prepare_us(j, g, split):
+            group_us(j, g, "V", 0, split)
+            if split < 64:
+                group_us(j, g, "S", split, 64)
+
+        def turn_unit(un):
+            for g in range(PD):
+                turn_meas(un, g, "S")
+
+        def quantize_unit(un):
+            for g in range(PD):
+                quantize_meas(un, g)
+
+        prepare_us(0, 0, 64)
+        turn_factors(0, "S")
+        turn_factors(1, "S")
+        turn_unit(0)
         quantize_us(0, 0)
+        prepare_us(0, 1, 64)
+        quantize_meas(0, 0)
+        quantize_us(0, 1)
+        prepare_us(0, 2, 40)
+        both(weights, 0, 0)
         quantize_meas(0, 1)
         quantize_meas(0, 2)
-        group_us(0, 2, "V")
-        weights(0, 0)
-        quantize_us(0, 1)
         quantize_us(0, 2)
-        for g in range(PD):
-            turn_meas(1, g, "S")
-        project(0, 0)
-        project(1, 0)
-        group_us(1, 0, "V")
-        group_us(1, 1, "S")
+        both(weights, 1, 0)
+        turn_meas(1, 0, "S")
+        turn_meas(1, 1, "S")
+        weights(0, 1, 0)
+        turn_meas(1, 2, "S")
+        weights(0, 1, 1)
+        both(project, 0, 0)
+        prepare_us(1, 0, 64)
+        quantize_meas(1, 0)
         quantize_us(1, 0)
-        for g in range(PD):
-            quantize_meas(1, g)
-        weights(1, 0)
-        weights(0, 1)
-        project(2, 0)
-        project(3, 0)
-        group_us(1, 2, "V")
+        quantize_meas(1, 1)
+        quantize_meas(1, 2)
+        prepare_us(1, 1, 32)
+        both(weigh, 0, 0)
+        both(project, 1, 0)
         quantize_us(1, 1)
-        weigh(0, 0)
+        prepare_us(1, 2, 32)
+        turn_meas(2, 0, "S")
+        turn_meas(2, 1, "S")
+        weights(1, 1, 0)
+        turn_meas(2, 2, "S")
+        weights(1, 1, 1)
+        weigh(1, 0, 0)
         quantize_us(1, 2)
-        weights(1, 1)
-        project(0, 1)
-        weights(2, 0)
-        weigh(1, 0)
-        weigh(0, 1)
-        project(1, 1)
-        quantize_chunk(0)
-        weigh(2, 0)
-        weights(2, 1)
-        weigh(1, 1)
-        weights(3, 0)
-        side = [(("T", 2),), (("T", 3),), (("A", 0),), (), (("B", 0),), (("B", 1),), (("A", 1),), ()]
-        for c in range(8):
-            nxt = c + 2
-            if c == 4:
-                weights(c + 3, 0)
-            if 4 <= nxt < 8:
-                project(nxt, 0)
-            image_part(c, 0, "V")
-            if 4 <= nxt < 8:
-                weigh(nxt, 0)
-            if nxt == 3:
-                weigh(3, 0)
-            if c < 7:
-                quantize_chunk(c + 1)
-            image_part(c, 1, "S")
-            if nxt < 8:
-                project(nxt, 1)
-            if c < 5:
-                weights(c + 3, 1)
-            for kind, i in side[c]:
-                if kind == "T":
-                    for g in range(PD):
-                        turn_meas(i, g, "S")
-                if kind == "A":
-                    for j in range(PM):
-                        turn_group(i, j, 0, "V")
-                        turn_group(i, j, 1, "S")
-                if kind == "B":
-                    turn_basis(i, 0, "S")
-                    turn_basis(i, 1, "S")
-            if nxt < 8:
-                weigh(nxt, 1)
-            image_part(c, 2, "S")
-            if c < 3:
-                weights(c + 4, 0)
-            image_part(c, 3, "V" if c > 5 else "S")
-            for kind, i in side[c]:
-                if kind == "T":
-                    for g in range(PD):
-                        quantize_meas(i, g)
-                if kind == "A":
-                    for j in range(PM):
-                        quantize_group(i, j)
-                if kind == "B":
-                    quantize_basis(i)
-            if c == 3:
-                for r in range(4):
-                    widen_basis(r)
+        weigh(1, 0, 1)
+        both(project, 0, 1)
+        group_h(0, 0, "V")
+        both(weigh, 0, 1)
+        both(project, 1, 1)
+        quantize_h(0, 0)
+        group_h(0, 1, "V")
+        group_h(1, 0, "S")
+        quantize_meas(2, 0)
+        quantize_h(0, 1)
+        quantize_meas(2, 1)
+        quantize_meas(2, 2)
+        both(weights, 2, 0)
+        both(weigh, 1, 1)
+        image_banks(0, 0, 0, "SSSS")
+        both(project, 2, 0)
+        quantize_h(1, 0)
+        group_h(1, 1, "V")
+        weigh(2, 0, 0)
+        quantize_h(1, 1)
+        weigh(2, 0, 1)
+        image_banks(0, 1, 0, "VS")
+        turn_meas(3, 0, "S")
+        turn_meas(3, 1, "S")
+        weights(2, 1, 0)
+        turn_meas(3, 2, "S")
+        weights(2, 1, 1)
+        for r in range(4):
+            widen_basis(r, "V")
+        image_banks(0, 1, 2, "VV")
+        both(project, 2, 1)
+        quantize_unit(3)
+        for th in range(2):
+            turn_h(0, 0, th, "S")
+        both(weigh, 2, 1)
+        image_banks(1, 0, 0, "SS")
+        group_h(2, 0, "V")
+        both(weights, 3, 0)
+        group_h(2, 1, "V")
+        quantize_h(2, 0)
+        image_banks(1, 0, 2, "SS")
+        quantize_h(2, 1)
+        both(project, 3, 0)
+        for h in range(2):
+            turn_basis(0, h)
+        image_banks(1, 1, 0, "SS")
+        both(weights, 3, 1)
+        both(weigh, 3, 0)
+        image_banks(1, 1, 2, "SS")
+        both(project, 3, 1)
+        group_h(3, 0, "V")
+        for th in range(2):
+            turn_h(0, 1, th, "S")
+        both(weigh, 3, 1)
+        image_banks(2, 0, 0, "SS")
+        for h in range(2):
+            turn_basis(1, h)
+        image_banks(2, 0, 2, "SS")
+        for th in range(2):
+            turn_h(1, 0, th, "S")
+        group_h(3, 1, "V")
+        quantize_h(3, 0)
+        quantize_basis(0)
+        quantize_h(3, 1)
+        image_banks(2, 1, 0, "SS")
+        for th in range(2):
+            turn_h(1, 1, th, "S")
+        quantize_basis(1)
+        quantize_hb(0, 0)
+        quantize_hb(0, 1)
+        image_banks(2, 1, 2, "SS")
+        quantize_hb(1, 0)
+        quantize_hb(1, 1)
+        image_banks(3, 0, 0, "SVSV")
         for r in range(4):
             for j in range(PM):
-                comps_part(r, j, "VS"[j])
+                comps_part(r, j, "SV"[j])
+        image_banks(3, 1, 0, "SVSV")

@@ -32,16 +32,18 @@ def tile_spectral_tikhonov_imaging_s8_kernel(
     with ExitStack() as ctx:
         keep = ctx.enter_context(tc.tile_pool(name="keep", bufs=1))
         work = ctx.enter_context(tc.tile_pool(name="work", bufs=2))
-        stage = ctx.enter_context(tc.tile_pool(name="stage", bufs=8))
+        stage = ctx.enter_context(tc.tile_pool(name="stage", bufs=7))
         psum = ctx.enter_context(tc.psum_pool(name="psum", bufs=1))
 
         ctx.enter_context(tc.manual_schedule())
 
         taken = []
 
-        def next_bank(shape, name):
-            taken.append(name)
-            return psum.tile(shape, F32, name=name, tag="bank%d" % (len(taken) % BANKS), bufs=1)
+        def next_bank(shape, name, dtype=F32, bank=None):
+            if bank is None:
+                taken.append(name)
+                bank = len(taken) % (6 if len(taken) < 18 else BANKS)
+            return psum.tile(shape, dtype, name=name, tag="bank%d" % bank, bufs=1)
 
         factors = keep.tile([128, 2, 8, 128], BF16, name="factors")
         nc.vector.memset(factors[:], 0.0)
@@ -57,11 +59,11 @@ def tile_spectral_tikhonov_imaging_s8_kernel(
         us_v = us.rearrange("(g p k) m -> g p k m", p=128, k=4)
 
         def load_meas(un):
-            raw_meas[un] = keep.tile([128, 2, D], BF16, name="raw_meas%d" % un)
+            raw_meas[un] = work.tile([128, 2, D], BF16, name="raw_meas", tag="raw_meas", bufs=4)
             nc.sync.dma_start(out=raw_meas[un][:], in_=meas_v[un // 2, :, 2 * (un % 2) : 2 * (un % 2) + 2, :])
 
         def load_us(j, g):
-            raw_us[j, g] = stage.tile([128, 4, 512], BF16, name="raw_us", tag="stage", bufs=8)
+            raw_us[j, g] = stage.tile([128, 4, 512], BF16, name="raw_us", tag="stage", bufs=7)
             nc.sync.dma_start(out=raw_us[j, g][:], in_=us_v[g, :, :, 512 * j : 512 * j + 512])
 
         roots = keep.tile([128, 2, 16], BF16, name="roots")
@@ -79,7 +81,7 @@ def tile_spectral_tikhonov_imaging_s8_kernel(
         load_meas(2)
         load_us(1, 2)
         for q in range(4):
-            nc.gpsimd.dma_start(
+            nc.sync.dma_start(
                 out=vs[32 * q : 32 * q + 4, :, :].bitcast(I32),
                 in_=vt_scales[:, 4 * q : 4 * q + 4, :].rearrange("g r n -> r g n").bitcast(I32),
             )
@@ -88,8 +90,8 @@ def tile_spectral_tikhonov_imaging_s8_kernel(
         load_meas(3)
         b_raw = keep.tile([128, 4, F], U8, name="b_raw")
         nc.sync.dma_start(out=b_raw[:], in_=basis_bytes.rearrange("(r p) f -> p r f", p=128))
-        b_scale = keep.tile([128, PF, 4], F32, name="b_scale")
-        nc.sync.dma_start(out=b_scale[:], in_=basis_scale.rearrange("o (g p t) -> p (o g) t", p=128, t=4))
+        b_scale = keep.tile([128, F], F32, name="b_scale")
+        nc.sync.dma_start(out=b_scale[:], in_=basis_scale.rearrange("o k -> (o k)").partition_broadcast(128))
 
         squares = keep.tile([128, 2, 8], F32, name="squares")
         nc.vector.tensor_tensor(out=squares[:], in0=roots[:, :, 0:8], in1=roots[:, :, 0:8], op=MULT)
@@ -110,17 +112,16 @@ def tile_spectral_tikhonov_imaging_s8_kernel(
         rows = keep.tile([128, 2, 8, 128], BF16, name="rows")
 
         def turn_factors(i, eng):
-            taken.append("ft")
-            bank = psum.tile([128, 8, 128], BF16, name="ft", tag="bank%d" % (len(taken) % BANKS), bufs=1)
+            bank = next_bank([128, 8, 128], "ft", BF16)
             for c in range(8):
-                nc.tensor.transpose(bank[:, c, :], factors[:, i, c, :], ident_b[:])
+                nc.tensor.matmul(out=bank[:, c, :], lhsT=factors[:, i, c, :], rhs=ident_b[:], start=True, stop=True)
             copy_on[eng](out=rows[:, i], in_=bank[:])
 
         copy_on = {"S": nc.scalar.copy, "V": nc.vector.tensor_copy}
         tiles = {}
 
         def weights(un, j, th):
-            bank = next_bank([128, 2, 2, 128], "wb")
+            bank = next_bank([128, 2, 2, 128], "wb", bank=6 + th)
             for i in range(2):
                 nc.tensor.matmul(
                     out=bank[:, i].rearrange("q e r -> q (e r)"),
@@ -134,6 +135,39 @@ def tile_spectral_tikhonov_imaging_s8_kernel(
                 out=tiles["rw", un, j, th][:], in_=bank[:].rearrange("q i e r -> q i r e"), func=ACT.Abs_reciprocal_sqrt
             )
 
+        lam_wide = keep.tile([128, 2, 128, 2], F32, name="lam_wide")
+
+        def spread_lam(eng):
+            bank = next_bank([128, 2, 2, 128], "lb")
+            for t in range(4):
+                column = roots[:, 0, 4 + t : 5 + t].to_broadcast([128, 128])
+                nc.tensor.matmul(out=bank[:, t // 2, t % 2, :], lhsT=column, rhs=ident_b[:], start=True, stop=True)
+            copy_on[eng](out=lam_wide[:], in_=bank[:].rearrange("q u e r -> q u r e"))
+
+        def roots_of(un, j, th):
+            tiles["rt", un, j, th] = work.tile([128, 2, 128, 2], F32, name="rt", bufs=3)
+            for i in range(2):
+                place = 4 * j + 2 * th + i
+                nc.scalar.activation(
+                    out=tiles["rt", un, j, th][:, i],
+                    in_=lam_wide[:, un % 2],
+                    func=ACT.Abs_reciprocal_sqrt,
+                    bias=squares[:, 1, place : place + 1],
+                )
+
+        def square_of(un, j, th, eng):
+            tiles["rw", un, j, th] = work.tile([128, 2, 128, 2], F32, name="rw", bufs=8)
+            root = tiles["rt", un, j, th]
+            if eng == "S":
+                nc.scalar.activation(out=tiles["rw", un, j, th][:], in_=root[:], func=ACT.Square)
+            else:
+                nc.vector.tensor_tensor(out=tiles["rw", un, j, th][:], in0=root[:], in1=root[:], op=MULT)
+
+        def split_meas(un, eng):
+            tiles["split", un] = work.tile([128, 2, 2, D // 4], F32, name="split", tag="raw_meas", bufs=4)
+            src = raw_meas[un][:].bitcast(F32).rearrange("r e (c w) -> r e w c", w=2)
+            copy_on[eng](out=tiles["split", un][:], in_=src)
+
         def turn_meas(un, g, eng):
             if g == 0:
                 tiles["mc", un] = keep.tile([128, PD, 256], U32, name="mc%d" % un, align_bytes=64)
@@ -142,7 +176,11 @@ def tile_spectral_tikhonov_imaging_s8_kernel(
             bank = next_bank([128, 2, 2, 128], "mt")
             for e in range(2):
                 for w in range(2):
-                    nc.tensor.transpose(bank[:, e, w, :], words[:, e, 256 * g + w : 256 * g + 256 : 2], ident[:])
+                    if ("split", un) in tiles:
+                        src = tiles["split", un][:, e, w, 128 * g : 128 * g + 128]
+                    else:
+                        src = words[:, e, 256 * g + w : 256 * g + 256 : 2]
+                    nc.tensor.transpose(bank[:, e, w, :], src, ident[:])
             grouped = work.tile([128, 1024], BF16, name="mg", align_bytes=64, bufs=4)
             tiles["mg", un, g] = grouped
             dst = grouped[:].bitcast(F32).rearrange("p (r e w) -> p r e w", e=2, w=2)
@@ -211,7 +249,7 @@ def tile_spectral_tikhonov_imaging_s8_kernel(
 
         def image_part(un, e, n, eng):
             if n % 2 == 0:
-                tiles["ob"] = stage.tile([128, 1024], F32, name="ob", tag="stage", bufs=8)
+                tiles["ob"] = stage.tile([128, 1024], F32, name="ob", tag="stage", bufs=7)
             ob = tiles["ob"]
             bank = next_bank([128, 512], "ib")
             cols = slice(128 * e, 128 * e + 128)
@@ -235,22 +273,23 @@ def tile_spectral_tikhonov_imaging_s8_kernel(
         bc = keep.tile([128, PF, R], U32, name="bc", align_bytes=64)
         bsc = keep.tile([128, PF, R], U8, name="bsc", align_bytes=64)
 
-        def widen_basis(r, eng):
-            tiles["bw", r] = keep.tile([128, F], BF16, name="bw%d" % r)
-            copy_on[eng](out=tiles["bw", r][:], in_=b_raw[:, r, :].bitcast(E4M3))
+        def widen_basis(r):
+            tiles["bw", r] = work.tile([128, F], BF16, name="bw")
+            nc.vector.tensor_tensor(out=tiles["bw", r][:], in0=b_raw[:, r, :].bitcast(E4M3), in1=b_scale[:], op=MULT)
 
-        def turn_basis(g, h):
+        def split_basis(r, eng):
+            tiles["bs", r] = keep.tile([128, 2, F // 4], F32, name="bs%d" % r)
+            copy_on[eng](out=tiles["bs", r][:], in_=tiles["bw", r][:].bitcast(F32).rearrange("n (c w) -> n w c", w=2))
+
+        def turn_basis(g, h, eng):
             if h == 0:
                 tiles["bg", g] = work.tile([128, 2048], BF16, name="bg", align_bytes=64)
             bank = next_bank([128, 2, 2, 128], "bt")
             for r in range(2):
-                words = tiles["bw", 2 * h + r][:].bitcast(F32)
                 for w in range(2):
-                    nc.tensor.transpose(bank[:, w, r, :], words[:, 256 * g + w : 256 * g + 256 : 2], ident[:])
-            src = bank[:].rearrange("p w r n -> p w (r n)").bitcast(BF16).rearrange("p w (c e) -> p c w e", e=2)
-            dst = tiles["bg", g][:, 1024 * h : 1024 * h + 1024].rearrange("p (c w e) -> p c w e", w=2, e=2)
-            scale = b_scale[:, g, :].rearrange("p (w e) -> p w e", e=2).unsqueeze(1).to_broadcast([128, 256, 2, 2])
-            nc.vector.tensor_tensor(out=dst, in0=src, in1=scale, op=MULT)
+                    nc.tensor.transpose(bank[:, w, r, :], tiles["bs", 2 * h + r][:, w, 128 * g : 128 * g + 128], ident[:])
+            dst = tiles["bg", g][:, 1024 * h : 1024 * h + 1024].bitcast(F32).rearrange("p (c w) -> p c w", w=2)
+            copy_on[eng](out=dst, in_=bank[:].rearrange("p w r n -> p (r n) w"))
 
         def quantize_basis(g):
             nc.vector.quantize_mx(out=bc[:, g, :].bitcast(FP8X4), scales=bsc[:, g, :], in_=tiles["bg", g][:])
@@ -260,7 +299,7 @@ def tile_spectral_tikhonov_imaging_s8_kernel(
 
         def turn_h(g, j, th, eng):
             if th == 0:
-                tiles["hb", g, j] = work.tile([128, 2048], BF16, name="hb", align_bytes=64, bufs=4)
+                tiles["hb", g, j] = work.tile([128, 2048], BF16, name="hb", align_bytes=64, bufs=3)
             bank = next_bank([128, 2, 2, 128], "ht")
             for u in range(2):
                 words = tiles["hn", 2 * g + u][:].bitcast(F32)
@@ -275,7 +314,7 @@ def tile_spectral_tikhonov_imaging_s8_kernel(
 
         def comps_part(r, j, eng):
             if j == 0:
-                tiles["co"] = stage.tile([128, M], F32, name="co", tag="stage", bufs=8)
+                tiles["co"] = stage.tile([128, M], F32, name="co", tag="stage", bufs=7)
             co = tiles["co"]
             bank = next_bank([128, 512], "kb")
             cols = slice(512 * j, 512 * j + 512)
@@ -314,6 +353,12 @@ def tile_spectral_tikhonov_imaging_s8_kernel(
             for g in range(PD):
                 quantize_meas(un, g)
 
+        def slow_weights(un, j, engs):
+            for th in range(2):
+                roots_of(un, j, th)
+            for th in range(2):
+                square_of(un, j, th, engs[th])
+
         prepare_us(0, 0, 64)
         turn_factors(0, "S")
         turn_factors(1, "S")
@@ -322,17 +367,19 @@ def tile_spectral_tikhonov_imaging_s8_kernel(
         prepare_us(0, 1, 64)
         quantize_meas(0, 0)
         quantize_us(0, 1)
-        prepare_us(0, 2, 40)
+        prepare_us(0, 2, 64)
         both(weights, 0, 0)
         quantize_meas(0, 1)
         quantize_meas(0, 2)
         quantize_us(0, 2)
         both(weights, 1, 0)
-        turn_meas(1, 0, "S")
-        turn_meas(1, 1, "S")
         weights(0, 1, 0)
-        turn_meas(1, 2, "S")
+        turn_meas(1, 0, "S")
         weights(0, 1, 1)
+        turn_meas(1, 1, "S")
+        weights(1, 1, 0)
+        turn_meas(1, 2, "S")
+        weights(1, 1, 1)
         both(project, 0, 0)
         prepare_us(1, 0, 64)
         quantize_meas(1, 0)
@@ -340,91 +387,90 @@ def tile_spectral_tikhonov_imaging_s8_kernel(
         quantize_meas(1, 1)
         quantize_meas(1, 2)
         prepare_us(1, 1, 32)
-        both(weigh, 0, 0)
-        both(project, 1, 0)
+        weigh(0, 0, 0)
+        project(1, 0, 0)
         quantize_us(1, 1)
         prepare_us(1, 2, 32)
         turn_meas(2, 0, "S")
         turn_meas(2, 1, "S")
-        weights(1, 1, 0)
-        turn_meas(2, 2, "S")
-        weights(1, 1, 1)
-        weigh(1, 0, 0)
+        weigh(0, 0, 1)
+        project(1, 0, 1)
         quantize_us(1, 2)
-        weigh(1, 0, 1)
+        turn_meas(2, 2, "S")
+        both(weigh, 1, 0)
         both(project, 0, 1)
-        group_h(0, 0, "V")
-        both(weigh, 0, 1)
+        group_h(0, 0, "S")
+        quantize_meas(2, 0)
+        weigh(0, 1, 0)
+        quantize_meas(2, 1)
+        weigh(0, 1, 1)
         both(project, 1, 1)
+        spread_lam("S")
         quantize_h(0, 0)
         group_h(0, 1, "V")
         group_h(1, 0, "S")
-        quantize_meas(2, 0)
-        quantize_h(0, 1)
-        quantize_meas(2, 1)
         quantize_meas(2, 2)
-        both(weights, 2, 0)
+        quantize_h(0, 1)
         both(weigh, 1, 1)
-        image_banks(0, 0, 0, "SSSS")
+        slow_weights(2, 0, "SS")
         both(project, 2, 0)
         quantize_h(1, 0)
         group_h(1, 1, "V")
-        weigh(2, 0, 0)
+        image_banks(0, 0, 0, "VVSS")
         quantize_h(1, 1)
-        weigh(2, 0, 1)
-        image_banks(0, 1, 0, "VS")
-        turn_meas(3, 0, "S")
-        turn_meas(3, 1, "S")
-        weights(2, 1, 0)
-        turn_meas(3, 2, "S")
-        weights(2, 1, 1)
-        for r in range(4):
-            widen_basis(r, "V")
-        image_banks(0, 1, 2, "VV")
+        both(weigh, 2, 0)
+        split_meas(3, "V")
+        slow_weights(2, 1, "SS")
         both(project, 2, 1)
-        quantize_unit(3)
-        for th in range(2):
-            turn_h(0, 0, th, "S")
-        both(weigh, 2, 1)
-        image_banks(1, 0, 0, "SS")
+        image_banks(0, 1, 0, "VS")
+        turn_unit(3)
         group_h(2, 0, "V")
-        both(weights, 3, 0)
-        group_h(2, 1, "V")
+        both(weigh, 2, 1)
+        image_banks(0, 1, 2, "SS")
+        quantize_unit(3)
         quantize_h(2, 0)
-        image_banks(1, 0, 2, "SS")
+        group_h(2, 1, "V")
+        image_banks(1, 0, 0, "SV")
+        slow_weights(3, 0, "SS")
         quantize_h(2, 1)
+        widen_basis(0)
+        image_banks(1, 0, 2, "SV")
         both(project, 3, 0)
-        for h in range(2):
-            turn_basis(0, h)
-        image_banks(1, 1, 0, "SS")
-        both(weights, 3, 1)
+        widen_basis(1)
+        split_basis(0, "S")
         both(weigh, 3, 0)
-        image_banks(1, 1, 2, "SS")
+        slow_weights(3, 1, "SS")
+        for j in range(PM):
+            for th in range(2):
+                turn_h(0, j, th, "VS"[th])
         both(project, 3, 1)
-        group_h(3, 0, "V")
-        for th in range(2):
-            turn_h(0, 1, th, "S")
+        split_basis(1, "S")
+        widen_basis(2)
         both(weigh, 3, 1)
-        image_banks(2, 0, 0, "SS")
-        for h in range(2):
-            turn_basis(1, h)
-        image_banks(2, 0, 2, "SS")
-        for th in range(2):
-            turn_h(1, 0, th, "S")
+        image_banks(1, 1, 0, "SSSS")
+        widen_basis(3)
+        split_basis(2, "V")
+        group_h(3, 0, "V")
+        split_basis(3, "V")
         group_h(3, 1, "V")
+        image_banks(2, 0, 0, "SSSS")
         quantize_h(3, 0)
-        quantize_basis(0)
         quantize_h(3, 1)
-        image_banks(2, 1, 0, "SS")
-        for th in range(2):
-            turn_h(1, 1, th, "S")
-        quantize_basis(1)
         quantize_hb(0, 0)
         quantize_hb(0, 1)
+        for j in range(PM):
+            for th in range(2):
+                turn_h(1, j, th, "SV"[th])
+        image_banks(2, 1, 0, "SV")
+        for g in range(PF):
+            for h in range(2):
+                turn_basis(g, h, "SV"[h])
         image_banks(2, 1, 2, "SS")
         quantize_hb(1, 0)
         quantize_hb(1, 1)
-        image_banks(3, 0, 0, "SVSV")
+        quantize_basis(0)
+        quantize_basis(1)
+        image_banks(3, 0, 0, "SSSV")
         for r in range(4):
             for j in range(PM):
                 comps_part(r, j, "SV"[j])

@@ -37,13 +37,16 @@ def tile_spectral_tikhonov_imaging_s8_kernel(
 
         ctx.enter_context(tc.manual_schedule())
 
-        taken = []
+        free_banks = list(range(BANKS - 2))
+        held = {}
 
-        def next_bank(shape, name, dtype=F32, bank=None):
-            if bank is None:
-                taken.append(name)
-                bank = len(taken) % (6 if len(taken) < 18 else BANKS)
-            return psum.tile(shape, dtype, name=name, tag="bank%d" % bank, bufs=1)
+        def take_bank(shape, name, dtype=F32):
+            held[name] = free_banks[0]
+            free_banks.remove(held[name])
+            return psum.tile(shape, dtype, name="bank", tag="bank%d" % held[name], bufs=1)
+
+        def give_bank(name):
+            free_banks.append(held[name])
 
         factors = keep.tile([128, 2, 8, 128], BF16, name="factors")
         nc.vector.memset(factors[:], 0.0)
@@ -112,16 +115,17 @@ def tile_spectral_tikhonov_imaging_s8_kernel(
         rows = keep.tile([128, 2, 8, 128], BF16, name="rows")
 
         def turn_factors(i, eng):
-            bank = next_bank([128, 8, 128], "ft", BF16)
+            bank = take_bank([128, 8, 128], "ft", BF16)
             for c in range(8):
                 nc.tensor.matmul(out=bank[:, c, :], lhsT=factors[:, i, c, :], rhs=ident_b[:], start=True, stop=True)
             copy_on[eng](out=rows[:, i], in_=bank[:])
+            give_bank("ft")
 
         copy_on = {"S": nc.scalar.copy, "V": nc.vector.tensor_copy}
         tiles = {}
 
         def weights(un, j, th):
-            bank = next_bank([128, 2, 2, 128], "wb", bank=6 + th)
+            bank = psum.tile([128, 2, 2, 128], F32, name="bank", tag="bank%d" % (BANKS - 2 + th), bufs=1)
             for i in range(2):
                 nc.tensor.matmul(
                     out=bank[:, i].rearrange("q e r -> q (e r)"),
@@ -138,11 +142,12 @@ def tile_spectral_tikhonov_imaging_s8_kernel(
         lam_wide = keep.tile([128, 2, 128, 2], F32, name="lam_wide")
 
         def spread_lam(eng):
-            bank = next_bank([128, 2, 2, 128], "lb")
+            bank = take_bank([128, 2, 2, 128], "lb")
             for t in range(4):
                 column = roots[:, 0, 4 + t : 5 + t].to_broadcast([128, 128])
                 nc.tensor.matmul(out=bank[:, t // 2, t % 2, :], lhsT=column, rhs=ident_b[:], start=True, stop=True)
             copy_on[eng](out=lam_wide[:], in_=bank[:].rearrange("q u e r -> q u r e"))
+            give_bank("lb")
 
         def roots_of(un, j, th):
             tiles["rt", un, j, th] = work.tile([128, 2, 128, 2], F32, name="rt", bufs=3)
@@ -173,7 +178,7 @@ def tile_spectral_tikhonov_imaging_s8_kernel(
                 tiles["mc", un] = keep.tile([128, PD, 256], U32, name="mc%d" % un, align_bytes=64)
                 tiles["ms", un] = keep.tile([128, PD, 256], U8, name="ms%d" % un, align_bytes=64)
             words = raw_meas[un][:].bitcast(F32)
-            bank = next_bank([128, 2, 2, 128], "mt")
+            bank = take_bank([128, 2, 2, 128], "mt")
             for e in range(2):
                 for w in range(2):
                     if ("split", un) in tiles:
@@ -181,10 +186,11 @@ def tile_spectral_tikhonov_imaging_s8_kernel(
                     else:
                         src = words[:, e, 256 * g + w : 256 * g + 256 : 2]
                     nc.tensor.transpose(bank[:, e, w, :], src, ident[:])
-            grouped = work.tile([128, 1024], BF16, name="mg", align_bytes=64, bufs=4)
+            grouped = work.tile([128, 1024], BF16, name="mg", align_bytes=64, bufs=3)
             tiles["mg", un, g] = grouped
             dst = grouped[:].bitcast(F32).rearrange("p (r e w) -> p r e w", e=2, w=2)
             copy_on[eng](out=dst, in_=bank[:].rearrange("p e w r -> p r e w"))
+            give_bank("mt")
 
         def quantize_meas(un, g):
             nc.vector.quantize_mx(
@@ -209,7 +215,7 @@ def tile_spectral_tikhonov_imaging_s8_kernel(
             )
 
         def project(un, j, th):
-            bank = next_bank([128, 2, 256], "cb")
+            bank = take_bank([128, 2, 256], ("cb", un, j, th))
             for i in range(2):
                 col = 512 * j + 128 * (2 * th + i)
                 for g in range(PD):
@@ -230,6 +236,7 @@ def tile_spectral_tikhonov_imaging_s8_kernel(
             places = slice(4 * j + 2 * th, 4 * j + 2 * th + 2)
             weight = tiles["rw", un, j, th][:].rearrange("q i r e -> q i (r e)")
             nc.vector.tensor_tensor(out=tiles["hn", un][:, places, :], in0=tiles["cb", un, j, th][:], in1=weight, op=MULT)
+            give_bank(("cb", un, j, th))
 
         def group_h(un, j, eng):
             tiles["ha", un, j] = work.tile([128, 1024], BF16, name="ha", align_bytes=64, bufs=4)
@@ -251,7 +258,7 @@ def tile_spectral_tikhonov_imaging_s8_kernel(
             if n % 2 == 0:
                 tiles["ob"] = stage.tile([128, 1024], F32, name="ob", tag="stage", bufs=7)
             ob = tiles["ob"]
-            bank = next_bank([128, 512], "ib")
+            bank = take_bank([128, 512], "ib")
             cols = slice(128 * e, 128 * e + 128)
             for j in range(PM):
                 nc.tensor.matmul_mx(
@@ -264,10 +271,9 @@ def tile_spectral_tikhonov_imaging_s8_kernel(
                     stop=(j == PM - 1),
                 )
             copy_on[eng](out=ob[:, 512 * (n % 2) : 512 * (n % 2) + 512], in_=bank[:])
+            give_bank("ib")
             rows_out = image_v[un // 2, 2 * (un % 2) + e]
-            if (un, e) == (UNITS - 1, 1) and n >= 2:
-                nc.sync.dma_start(out=rows_out[:, 512 * n : 512 * n + 512], in_=ob[:, 512 * (n % 2) : 512 * (n % 2) + 512])
-            elif n % 2 == 1:
+            if n % 2 == 1:
                 nc.sync.dma_start(out=rows_out[:, 512 * n - 512 : 512 * n + 512], in_=ob[:])
 
         bc = keep.tile([128, PF, R], U32, name="bc", align_bytes=64)
@@ -284,12 +290,13 @@ def tile_spectral_tikhonov_imaging_s8_kernel(
         def turn_basis(g, h, eng):
             if h == 0:
                 tiles["bg", g] = work.tile([128, 2048], BF16, name="bg", align_bytes=64)
-            bank = next_bank([128, 2, 2, 128], "bt")
+            bank = take_bank([128, 2, 2, 128], "bt")
             for r in range(2):
                 for w in range(2):
                     nc.tensor.transpose(bank[:, w, r, :], tiles["bs", 2 * h + r][:, w, 128 * g : 128 * g + 128], ident[:])
             dst = tiles["bg", g][:, 1024 * h : 1024 * h + 1024].bitcast(F32).rearrange("p (c w) -> p c w", w=2)
             copy_on[eng](out=dst, in_=bank[:].rearrange("p w r n -> p (r n) w"))
+            give_bank("bt")
 
         def quantize_basis(g):
             nc.vector.quantize_mx(out=bc[:, g, :].bitcast(FP8X4), scales=bsc[:, g, :], in_=tiles["bg", g][:])
@@ -299,14 +306,15 @@ def tile_spectral_tikhonov_imaging_s8_kernel(
 
         def turn_h(g, j, th, eng):
             if th == 0:
-                tiles["hb", g, j] = work.tile([128, 2048], BF16, name="hb", align_bytes=64, bufs=3)
-            bank = next_bank([128, 2, 2, 128], "ht")
+                tiles["hb", g, j] = work.tile([128, 2048], BF16, name="hb", align_bytes=64, bufs=4)
+            bank = take_bank([128, 2, 2, 128], "ht")
             for u in range(2):
                 words = tiles["hn", 2 * g + u][:].bitcast(F32)
                 for i in range(2):
                     nc.tensor.transpose(bank[:, u, i, :], words[:, 4 * j + 2 * th + i, :], ident[:])
             dst = tiles["hb", g, j][:, 1024 * th : 1024 * th + 1024].bitcast(F32).rearrange("p (c u) -> p c u", u=2)
             copy_on[eng](out=dst, in_=bank[:].rearrange("p u i q -> p (i q) u"))
+            give_bank("ht")
 
         def quantize_hb(g, j):
             cols = slice(512 * j, 512 * j + 512)
@@ -316,7 +324,7 @@ def tile_spectral_tikhonov_imaging_s8_kernel(
             if j == 0:
                 tiles["co"] = stage.tile([128, M], F32, name="co", tag="stage", bufs=7)
             co = tiles["co"]
-            bank = next_bank([128, 512], "kb")
+            bank = take_bank([128, 512], "kb")
             cols = slice(512 * j, 512 * j + 512)
             for g in range(PF):
                 nc.tensor.matmul_mx(
@@ -329,7 +337,10 @@ def tile_spectral_tikhonov_imaging_s8_kernel(
                     stop=(g == PF - 1),
                 )
             copy_on[eng](out=co[:, cols].rearrange("p (q t) -> p q t", t=4), in_=bank[:].rearrange("p (t q) -> p q t", t=4))
-            if j == PM - 1:
+            give_bank("kb")
+            if r == 3:
+                nc.sync.dma_start(out=comps[128 * r : 128 * r + 128, cols], in_=co[:, cols])
+            elif j == PM - 1:
                 nc.sync.dma_start(out=comps[128 * r : 128 * r + 128, :], in_=co[:])
 
         def both(step, un, j):
@@ -380,6 +391,7 @@ def tile_spectral_tikhonov_imaging_s8_kernel(
         weights(1, 1, 0)
         turn_meas(1, 2, "S")
         weights(1, 1, 1)
+        free_banks.extend([BANKS - 2, BANKS - 1])
         both(project, 0, 0)
         prepare_us(1, 0, 64)
         quantize_meas(1, 0)
@@ -426,52 +438,51 @@ def tile_spectral_tikhonov_imaging_s8_kernel(
         turn_unit(3)
         group_h(2, 0, "V")
         both(weigh, 2, 1)
-        image_banks(0, 1, 2, "SS")
+        image_banks(0, 1, 2, "VS")
         quantize_unit(3)
+        slow_weights(3, 0, "SS")
+        image_banks(1, 0, 0, "VVSS")
+        both(project, 3, 0)
+        slow_weights(3, 1, "SS")
         quantize_h(2, 0)
         group_h(2, 1, "V")
-        image_banks(1, 0, 0, "SV")
-        slow_weights(3, 0, "SS")
-        quantize_h(2, 1)
-        widen_basis(0)
-        image_banks(1, 0, 2, "SV")
-        both(project, 3, 0)
-        widen_basis(1)
-        split_basis(0, "S")
         both(weigh, 3, 0)
-        slow_weights(3, 1, "SS")
+        quantize_h(2, 1)
+        image_banks(1, 1, 0, "VV")
+        both(project, 3, 1)
+        image_banks(1, 1, 2, "SS")
+        both(weigh, 3, 1)
         for j in range(PM):
             for th in range(2):
-                turn_h(0, j, th, "VS"[th])
-        both(project, 3, 1)
-        split_basis(1, "S")
-        widen_basis(2)
-        both(weigh, 3, 1)
-        image_banks(1, 1, 0, "SSSS")
-        widen_basis(3)
-        split_basis(2, "V")
+                turn_h(0, j, th, "S")
         group_h(3, 0, "V")
-        split_basis(3, "V")
         group_h(3, 1, "V")
         image_banks(2, 0, 0, "SSSS")
         quantize_h(3, 0)
         quantize_h(3, 1)
-        quantize_hb(0, 0)
-        quantize_hb(0, 1)
+        widen_basis(0)
+        widen_basis(1)
+        split_basis(0, "V")
+        widen_basis(2)
+        split_basis(1, "V")
+        widen_basis(3)
+        image_banks(2, 1, 0, "SSSS")
         for j in range(PM):
             for th in range(2):
-                turn_h(1, j, th, "SV"[th])
-        image_banks(2, 1, 0, "SV")
+                turn_h(1, j, th, "S")
+        split_basis(2, "V")
+        quantize_hb(0, 0)
+        split_basis(3, "V")
+        quantize_hb(0, 1)
+        image_banks(3, 0, 0, "SVSV")
         for g in range(PF):
             for h in range(2):
                 turn_basis(g, h, "SV"[h])
-        image_banks(2, 1, 2, "SS")
         quantize_hb(1, 0)
-        quantize_hb(1, 1)
         quantize_basis(0)
         quantize_basis(1)
-        image_banks(3, 0, 0, "SSSV")
+        quantize_hb(1, 1)
+        image_banks(3, 1, 0, "SSSS")
         for r in range(4):
             for j in range(PM):
                 comps_part(r, j, "SV"[j])
-        image_banks(3, 1, 0, "SVSV")

@@ -124,8 +124,13 @@ def tile_spectral_tikhonov_imaging_s8_kernel(
         copy_on = {"S": nc.scalar.copy, "V": nc.vector.tensor_copy}
         tiles = {}
 
-        def weights(un, j, th):
-            bank = psum.tile([128, 2, 2, 128], F32, name="bank", tag="bank%d" % (BANKS - 2 + th), bufs=1)
+        def square_sum(un, j, th, bank_no=None):
+            if bank_no is None:
+                bank = take_bank([128, 2, 2, 128], ("wb", un, j, th))
+            else:
+                held["wb", un, j, th] = bank_no
+                bank = psum.tile([128, 2, 2, 128], F32, name="bank", tag="bank%d" % bank_no, bufs=1)
+            tiles["wb", un, j, th] = bank
             for i in range(2):
                 nc.tensor.matmul(
                     out=bank[:, i].rearrange("q e r -> q (e r)"),
@@ -134,10 +139,24 @@ def tile_spectral_tikhonov_imaging_s8_kernel(
                     start=True,
                     stop=True,
                 )
+
+        def invert(un, j, th, give=True):
             tiles["rw", un, j, th] = work.tile([128, 2, 128, 2], F32, name="rw", bufs=8)
             nc.scalar.activation(
-                out=tiles["rw", un, j, th][:], in_=bank[:].rearrange("q i e r -> q i r e"), func=ACT.Abs_reciprocal_sqrt
+                out=tiles["rw", un, j, th][:],
+                in_=tiles["wb", un, j, th][:].rearrange("q i e r -> q i r e"),
+                func=ACT.Abs_reciprocal_sqrt,
             )
+            if give:
+                give_bank(("wb", un, j, th))
+
+        def weights(un, j, th):
+            square_sum(un, j, th)
+            invert(un, j, th)
+
+        def paced_weights(un, j, th):
+            square_sum(un, j, th, BANKS - 2 + th)
+            invert(un, j, th, False)
 
         lam_wide = keep.tile([128, 2, 128, 2], F32, name="lam_wide")
 
@@ -177,6 +196,7 @@ def tile_spectral_tikhonov_imaging_s8_kernel(
             if g == 0:
                 tiles["mc", un] = keep.tile([128, PD, 256], U32, name="mc%d" % un, align_bytes=64)
                 tiles["ms", un] = keep.tile([128, PD, 256], U8, name="ms%d" % un, align_bytes=64)
+                tiles["mg", un] = work.tile([128, PD * 1024], BF16, name="mg", align_bytes=64)
             words = raw_meas[un][:].bitcast(F32)
             bank = take_bank([128, 2, 2, 128], "mt")
             for e in range(2):
@@ -186,15 +206,15 @@ def tile_spectral_tikhonov_imaging_s8_kernel(
                     else:
                         src = words[:, e, 256 * g + w : 256 * g + 256 : 2]
                     nc.tensor.transpose(bank[:, e, w, :], src, ident[:])
-            grouped = work.tile([128, 1024], BF16, name="mg", align_bytes=64, bufs=3)
-            tiles["mg", un, g] = grouped
-            dst = grouped[:].bitcast(F32).rearrange("p (r e w) -> p r e w", e=2, w=2)
+            dst = tiles["mg", un][:, 1024 * g : 1024 * g + 1024].bitcast(F32).rearrange("p (r e w) -> p r e w", e=2, w=2)
             copy_on[eng](out=dst, in_=bank[:].rearrange("p e w r -> p r e w"))
             give_bank("mt")
 
-        def quantize_meas(un, g):
+        def quantize_meas(un, lo, hi):
             nc.vector.quantize_mx(
-                out=tiles["mc", un][:, g, :].bitcast(FP8X4), scales=tiles["ms", un][:, g, :], in_=tiles["mg", un, g][:]
+                out=tiles["mc", un][:, lo:hi, :].rearrange("p g c -> p (g c)").bitcast(FP8X4),
+                scales=tiles["ms", un][:, lo:hi, :].rearrange("p g c -> p (g c)"),
+                in_=tiles["mg", un][:, 1024 * lo : 1024 * hi],
             )
 
         uc = keep.tile([128, PD, M], U32, name="uc", align_bytes=64)
@@ -239,17 +259,20 @@ def tile_spectral_tikhonov_imaging_s8_kernel(
             give_bank(("cb", un, j, th))
 
         def group_h(un, j, eng):
-            tiles["ha", un, j] = work.tile([128, 1024], BF16, name="ha", align_bytes=64, bufs=4)
-            dst = tiles["ha", un, j][:].rearrange("q (e a b t) -> q a e b t", e=2, b=4, t=4)
+            if j == 0:
+                tiles["ha", un] = work.tile([128, PM * 1024], BF16, name="ha", align_bytes=64)
+            dst = tiles["ha", un][:, 1024 * j : 1024 * j + 1024].rearrange("q (e a b t) -> q a e b t", e=2, b=4, t=4)
             src = tiles["hn", un][:, 4 * j : 4 * j + 4, :].rearrange("q t (a b e) -> q a e b t", b=4, e=2)
             copy_on[eng](out=dst, in_=src)
 
-        def quantize_h(un, j):
-            if j == 0:
-                tiles["hc", un] = keep.tile([128, PM, 256], U32, name="hc%d" % un, align_bytes=64)
-                tiles["hs", un] = keep.tile([128, PM, 256], U8, name="hs%d" % un, align_bytes=64)
+        def quantize_h(un, lo, hi):
+            if lo == 0:
+                tiles["hc", un] = keep.tile([128, PM * 256], U32, name="hc%d" % un, align_bytes=64)
+                tiles["hs", un] = keep.tile([128, PM * 256], U8, name="hs%d" % un, align_bytes=64)
             nc.vector.quantize_mx(
-                out=tiles["hc", un][:, j, :].bitcast(FP8X4), scales=tiles["hs", un][:, j, :], in_=tiles["ha", un, j][:]
+                out=tiles["hc", un][:, 256 * lo : 256 * hi].bitcast(FP8X4),
+                scales=tiles["hs", un][:, 256 * lo : 256 * hi],
+                in_=tiles["ha", un][:, 1024 * lo : 1024 * hi],
             )
 
         image_v = image.rearrange("(g p t) n -> g t p n", g=PF, p=128)
@@ -259,12 +282,12 @@ def tile_spectral_tikhonov_imaging_s8_kernel(
                 tiles["ob"] = stage.tile([128, 1024], F32, name="ob", tag="stage", bufs=7)
             ob = tiles["ob"]
             bank = take_bank([128, 512], "ib")
-            cols = slice(128 * e, 128 * e + 128)
             for j in range(PM):
+                cols = slice(256 * j + 128 * e, 256 * j + 128 * e + 128)
                 nc.tensor.matmul_mx(
                     out=bank[:],
-                    lhsT=tiles["hc", un][:, j, cols].bitcast(FP8X4),
-                    lhsT_scale=tiles["hs", un][:, j, cols],
+                    lhsT=tiles["hc", un][:, cols].bitcast(FP8X4),
+                    lhsT_scale=tiles["hs", un][:, cols],
                     rhs=vt[:, j, 1024 * n : 1024 * n + 1024].bitcast(FP4X4),
                     rhs_scale=vs[:, j, 512 * n : 512 * n + 512],
                     start=(j == 0),
@@ -279,6 +302,8 @@ def tile_spectral_tikhonov_imaging_s8_kernel(
         bc = keep.tile([128, PF, R], U32, name="bc", align_bytes=64)
         bsc = keep.tile([128, PF, R], U8, name="bsc", align_bytes=64)
 
+        bg = keep.tile([128, PF * 2048], BF16, name="bg", align_bytes=64)
+
         def widen_basis(r):
             tiles["bw", r] = work.tile([128, F], BF16, name="bw")
             nc.vector.tensor_tensor(out=tiles["bw", r][:], in0=b_raw[:, r, :].bitcast(E4M3), in1=b_scale[:], op=MULT)
@@ -288,37 +313,39 @@ def tile_spectral_tikhonov_imaging_s8_kernel(
             copy_on[eng](out=tiles["bs", r][:], in_=tiles["bw", r][:].bitcast(F32).rearrange("n (c w) -> n w c", w=2))
 
         def turn_basis(g, h, eng):
-            if h == 0:
-                tiles["bg", g] = work.tile([128, 2048], BF16, name="bg", align_bytes=64)
             bank = take_bank([128, 2, 2, 128], "bt")
             for r in range(2):
                 for w in range(2):
                     nc.tensor.transpose(bank[:, w, r, :], tiles["bs", 2 * h + r][:, w, 128 * g : 128 * g + 128], ident[:])
-            dst = tiles["bg", g][:, 1024 * h : 1024 * h + 1024].bitcast(F32).rearrange("p (c w) -> p c w", w=2)
+            dst = bg[:, 2048 * g + 1024 * h : 2048 * g + 1024 * h + 1024].bitcast(F32).rearrange("p (c w) -> p c w", w=2)
             copy_on[eng](out=dst, in_=bank[:].rearrange("p w r n -> p (r n) w"))
             give_bank("bt")
 
-        def quantize_basis(g):
-            nc.vector.quantize_mx(out=bc[:, g, :].bitcast(FP8X4), scales=bsc[:, g, :], in_=tiles["bg", g][:])
+        def quantize_basis():
+            nc.vector.quantize_mx(
+                out=bc[:].rearrange("p g r -> p (g r)").bitcast(FP8X4), scales=bsc[:].rearrange("p g r -> p (g r)"), in_=bg[:]
+            )
 
         ac = keep.tile([128, PF, M], U32, name="ac", align_bytes=64)
         asc = keep.tile([128, PF, M], U8, name="asc", align_bytes=64)
 
         def turn_h(g, j, th, eng):
-            if th == 0:
-                tiles["hb", g, j] = work.tile([128, 2048], BF16, name="hb", align_bytes=64, bufs=4)
+            if (j, th) == (0, 0):
+                tiles["hb", g] = work.tile([128, PM * 2048], BF16, name="hb", align_bytes=64)
             bank = take_bank([128, 2, 2, 128], "ht")
             for u in range(2):
                 words = tiles["hn", 2 * g + u][:].bitcast(F32)
                 for i in range(2):
                     nc.tensor.transpose(bank[:, u, i, :], words[:, 4 * j + 2 * th + i, :], ident[:])
-            dst = tiles["hb", g, j][:, 1024 * th : 1024 * th + 1024].bitcast(F32).rearrange("p (c u) -> p c u", u=2)
+            dst = tiles["hb", g][:, 2048 * j + 1024 * th : 2048 * j + 1024 * th + 1024].bitcast(F32).rearrange("p (c u) -> p c u", u=2)
             copy_on[eng](out=dst, in_=bank[:].rearrange("p u i q -> p (i q) u"))
             give_bank("ht")
 
-        def quantize_hb(g, j):
-            cols = slice(512 * j, 512 * j + 512)
-            nc.vector.quantize_mx(out=ac[:, g, cols].bitcast(FP8X4), scales=asc[:, g, cols], in_=tiles["hb", g, j][:])
+        def quantize_hb(g, lo, hi):
+            cols = slice(512 * lo, 512 * hi)
+            nc.vector.quantize_mx(
+                out=ac[:, g, cols].bitcast(FP8X4), scales=asc[:, g, cols], in_=tiles["hb", g][:, 2048 * lo : 2048 * hi]
+            )
 
         def comps_part(r, j, eng):
             if j == 0:
@@ -361,8 +388,8 @@ def tile_spectral_tikhonov_imaging_s8_kernel(
                 turn_meas(un, g, "S")
 
         def quantize_unit(un):
-            for g in range(PD):
-                quantize_meas(un, g)
+            quantize_meas(un, 0, 2)
+            quantize_meas(un, 2, 3)
 
         def slow_weights(un, j, engs):
             for th in range(2):
@@ -376,80 +403,81 @@ def tile_spectral_tikhonov_imaging_s8_kernel(
         turn_unit(0)
         quantize_us(0, 0)
         prepare_us(0, 1, 64)
-        quantize_meas(0, 0)
+        quantize_meas(0, 0, 2)
         quantize_us(0, 1)
         prepare_us(0, 2, 64)
-        both(weights, 0, 0)
-        quantize_meas(0, 1)
-        quantize_meas(0, 2)
+        both(paced_weights, 0, 0)
+        quantize_meas(0, 2, 3)
         quantize_us(0, 2)
-        both(weights, 1, 0)
-        weights(0, 1, 0)
+        both(paced_weights, 1, 0)
         turn_meas(1, 0, "S")
-        weights(0, 1, 1)
+        square_sum(0, 1, 0, BANKS - 2)
         turn_meas(1, 1, "S")
-        weights(1, 1, 0)
+        square_sum(0, 1, 1, BANKS - 1)
         turn_meas(1, 2, "S")
-        weights(1, 1, 1)
-        free_banks.extend([BANKS - 2, BANKS - 1])
+        both(invert, 0, 1)
         both(project, 0, 0)
         prepare_us(1, 0, 64)
-        quantize_meas(1, 0)
+        quantize_unit(1)
         quantize_us(1, 0)
-        quantize_meas(1, 1)
-        quantize_meas(1, 2)
         prepare_us(1, 1, 32)
-        weigh(0, 0, 0)
         project(1, 0, 0)
         quantize_us(1, 1)
         prepare_us(1, 2, 32)
         turn_meas(2, 0, "S")
         turn_meas(2, 1, "S")
-        weigh(0, 0, 1)
         project(1, 0, 1)
-        quantize_us(1, 2)
         turn_meas(2, 2, "S")
-        both(weigh, 1, 0)
+        weigh(0, 0, 0)
+        square_sum(1, 1, 0)
+        quantize_us(1, 2)
+        weigh(0, 0, 1)
+        square_sum(1, 1, 1)
         both(project, 0, 1)
         group_h(0, 0, "S")
-        quantize_meas(2, 0)
+        both(invert, 1, 1)
+        quantize_meas(2, 0, 2)
         weigh(0, 1, 0)
-        quantize_meas(2, 1)
+        weigh(1, 0, 0)
         weigh(0, 1, 1)
         both(project, 1, 1)
-        spread_lam("S")
-        quantize_h(0, 0)
-        group_h(0, 1, "V")
+        both(weights, 2, 0)
+        weigh(1, 0, 1)
         group_h(1, 0, "S")
-        quantize_meas(2, 2)
-        quantize_h(0, 1)
-        both(weigh, 1, 1)
-        slow_weights(2, 0, "SS")
+        quantize_meas(2, 2, 3)
+        group_h(0, 1, "V")
+        weigh(1, 1, 0)
+        quantize_h(0, 0, 2)
+        weigh(1, 1, 1)
         both(project, 2, 0)
-        quantize_h(1, 0)
         group_h(1, 1, "V")
-        image_banks(0, 0, 0, "VVSS")
-        quantize_h(1, 1)
-        both(weigh, 2, 0)
+        image_banks(0, 0, 0, "SSSS")
+        weigh(2, 0, 0)
+        quantize_h(1, 0, 2)
+        weigh(2, 0, 1)
         split_meas(3, "V")
-        slow_weights(2, 1, "SS")
+        both(weights, 2, 1)
         both(project, 2, 1)
-        image_banks(0, 1, 0, "VS")
-        turn_unit(3)
+        image_banks(0, 1, 0, "SS")
         group_h(2, 0, "V")
+        turn_unit(3)
         both(weigh, 2, 1)
         image_banks(0, 1, 2, "VS")
         quantize_unit(3)
-        slow_weights(3, 0, "SS")
-        image_banks(1, 0, 0, "VVSS")
-        both(project, 3, 0)
-        slow_weights(3, 1, "SS")
-        quantize_h(2, 0)
+        both(weights, 3, 0)
         group_h(2, 1, "V")
+        image_banks(1, 0, 0, "SSSS")
+        widen_basis(0)
+        quantize_h(2, 0, 2)
+        both(project, 3, 0)
+        both(weights, 3, 1)
+        widen_basis(1)
+        split_basis(0, "V")
         both(weigh, 3, 0)
-        quantize_h(2, 1)
-        image_banks(1, 1, 0, "VV")
+        image_banks(1, 1, 0, "SS")
+        split_basis(1, "V")
         both(project, 3, 1)
+        widen_basis(2)
         image_banks(1, 1, 2, "SS")
         both(weigh, 3, 1)
         for j in range(PM):
@@ -457,32 +485,26 @@ def tile_spectral_tikhonov_imaging_s8_kernel(
                 turn_h(0, j, th, "S")
         group_h(3, 0, "V")
         group_h(3, 1, "V")
-        image_banks(2, 0, 0, "SSSS")
-        quantize_h(3, 0)
-        quantize_h(3, 1)
-        widen_basis(0)
-        widen_basis(1)
-        split_basis(0, "V")
-        widen_basis(2)
-        split_basis(1, "V")
         widen_basis(3)
-        image_banks(2, 1, 0, "SSSS")
-        for j in range(PM):
-            for th in range(2):
-                turn_h(1, j, th, "S")
+        image_banks(2, 0, 0, "SSSS")
         split_basis(2, "V")
-        quantize_hb(0, 0)
+        quantize_h(3, 0, 2)
         split_basis(3, "V")
-        quantize_hb(0, 1)
-        image_banks(3, 0, 0, "SVSV")
+        quantize_hb(0, 0, 2)
+        image_banks(2, 1, 0, "SVSV")
         for g in range(PF):
             for h in range(2):
                 turn_basis(g, h, "SV"[h])
-        quantize_hb(1, 0)
-        quantize_basis(0)
-        quantize_basis(1)
-        quantize_hb(1, 1)
-        image_banks(3, 1, 0, "SSSS")
+        image_banks(3, 0, 0, "SS")
+        quantize_basis()
+        image_banks(3, 0, 2, "SV")
+        for j in range(PM):
+            for th in range(2):
+                turn_h(1, j, th, "SV"[th])
+        quantize_hb(1, 0, 1)
+        image_banks(3, 1, 0, "SS")
+        quantize_hb(1, 1, 2)
+        image_banks(3, 1, 2, "SS")
         for r in range(4):
             for j in range(PM):
                 comps_part(r, j, "SV"[j])

@@ -75,8 +75,8 @@ def tile_spectral_tikhonov_imaging_s8_kernel(
         nc.scalar.activation(out=factors[:, 1, :, 0:2], in_=factors[:, 1, :, 8:10], func=ACT.Abs_reciprocal_sqrt, bias=1.0)
         nc.scalar.activation(out=factors[:, 0, :, 4:8], in_=factors[:, 0, :, 8:12], func=ACT.Abs_reciprocal_sqrt, bias=1.0)
         load_us(0, 0)
-        load_meas(0)
         load_us(0, 1)
+        load_meas(0)
         load_us(0, 2)
         load_meas(1)
         load_us(1, 0)
@@ -99,18 +99,18 @@ def tile_spectral_tikhonov_imaging_s8_kernel(
         squares = keep.tile([128, 2, 8], F32, name="squares")
         nc.vector.tensor_tensor(out=squares[:], in0=roots[:, :, 0:8], in1=roots[:, :, 0:8], op=MULT)
         nc.vector.tensor_copy(out=factors[:, 0, :, 2:4], in_=roots[:, 0, 0:8].unsqueeze(2).to_broadcast([128, 8, 2]))
-        nc.vector.tensor_copy(out=factors[:, 0, :, 0], in_=squares[:, 0, :])
         s4 = keep.tile([128, PM * 4], F32, name="s4")
         nc.vector.tensor_tensor(out=s4[:], in0=squares[:, 1, :], in1=squares[:, 1, :], op=MULT)
+        nc.vector.tensor_copy(out=factors[:, 0, :, 0], in_=squares[:, 0, :])
         nc.vector.tensor_scalar(out=factors[:, 1, :, 2], in0=squares[:, 1, :], scalar1=2.0, scalar2=None, op0=MULT)
-        nc.vector.tensor_tensor(out=factors[:, 0, :, 1], in0=squares[:, 0, :], in1=factors[:, 0, :, 0], op=SUB)
         nc.vector.tensor_copy(out=factors[:, 1, :, 4], in_=s4[:])
+        nc.vector.tensor_tensor(out=factors[:, 0, :, 1], in0=squares[:, 0, :], in1=factors[:, 0, :, 0], op=SUB)
         nc.vector.scalar_tensor_tensor(
             out=factors[:, 1, :, 3], in0=squares[:, 1, :], scalar=2.0, in1=factors[:, 1, :, 2], op0=MULT, op1=SUB
         )
         rest = keep.tile([128, PM * 4], F32, name="rest")
         nc.vector.tensor_tensor(out=rest[:], in0=s4[:], in1=factors[:, 1, :, 4], op=SUB)
-        nc.vector.tensor_copy(out=factors[:, 1, :, 5], in_=rest[:])
+        nc.vector.tensor_tensor(out=factors[:, 1, :, 5], in0=s4[:], in1=factors[:, 1, :, 4], op=SUB)
         nc.vector.tensor_tensor(out=factors[:, 1, :, 6], in0=rest[:], in1=factors[:, 1, :, 5], op=SUB)
         rows = keep.tile([128, 2, 8, 128], BF16, name="rows")
 
@@ -141,7 +141,7 @@ def tile_spectral_tikhonov_imaging_s8_kernel(
                 )
 
         def invert(un, j, th, give=True):
-            tiles["rw", un, j, th] = work.tile([128, 2, 128, 2], F32, name="rw", bufs=8)
+            tiles["rw", un, j, th] = work.tile([128, 2, 128, 2], F32, name="rw", bufs=6)
             nc.scalar.activation(
                 out=tiles["rw", un, j, th][:],
                 in_=tiles["wb", un, j, th][:].rearrange("q i e r -> q i r e"),
@@ -169,7 +169,7 @@ def tile_spectral_tikhonov_imaging_s8_kernel(
             give_bank("lb")
 
         def roots_of(un, j, th):
-            tiles["rt", un, j, th] = work.tile([128, 2, 128, 2], F32, name="rt", bufs=3)
+            tiles["rt", un, j, th] = work.tile([128, 2, 128, 2], F32, name="rt", bufs=2)
             for i in range(2):
                 place = 4 * j + 2 * th + i
                 nc.scalar.activation(
@@ -180,7 +180,7 @@ def tile_spectral_tikhonov_imaging_s8_kernel(
                 )
 
         def square_of(un, j, th, eng):
-            tiles["rw", un, j, th] = work.tile([128, 2, 128, 2], F32, name="rw", bufs=8)
+            tiles["rw", un, j, th] = work.tile([128, 2, 128, 2], F32, name="rw", bufs=6)
             root = tiles["rt", un, j, th]
             if eng == "S":
                 nc.scalar.activation(out=tiles["rw", un, j, th][:], in_=root[:], func=ACT.Square)
@@ -223,8 +223,8 @@ def tile_spectral_tikhonov_imaging_s8_kernel(
         def group_us(j, g, eng, lo, hi):
             if lo == 0:
                 tiles["ug", j, g] = work.tile([128, 2048], BF16, name="ug", align_bytes=64, bufs=3)
-            dst = tiles["ug", j, g][:].rearrange("p (t a b k) -> p a t b k", t=4, b=2, k=4)
-            src = raw_us[j, g][:].rearrange("p k (a b t) -> p a t b k", b=2, t=4)
+            dst = tiles["ug", j, g][:].rearrange("p (t a b k) -> p a k b t", t=4, b=2, k=4)
+            src = raw_us[j, g][:].rearrange("p k (a b t) -> p a k b t", b=2, t=4)
             copy_on[eng](out=dst[:, lo:hi], in_=src[:, lo:hi])
 
         def quantize_us(j, g):
@@ -261,8 +261,8 @@ def tile_spectral_tikhonov_imaging_s8_kernel(
         def group_h(un, j, eng):
             if j == 0:
                 tiles["ha", un] = work.tile([128, PM * 1024], BF16, name="ha", align_bytes=64)
-            dst = tiles["ha", un][:, 1024 * j : 1024 * j + 1024].rearrange("q (e a b t) -> q a e b t", e=2, b=4, t=4)
-            src = tiles["hn", un][:, 4 * j : 4 * j + 4, :].rearrange("q t (a b e) -> q a e b t", b=4, e=2)
+            dst = tiles["ha", un][:, 1024 * j : 1024 * j + 1024].rearrange("q (e a b t) -> q a t b e", e=2, b=4, t=4)
+            src = tiles["hn", un][:, 4 * j : 4 * j + 4, :].rearrange("q t (a b e) -> q a t b e", b=4, e=2)
             copy_on[eng](out=dst, in_=src)
 
         def quantize_h(un, lo, hi):
@@ -400,16 +400,16 @@ def tile_spectral_tikhonov_imaging_s8_kernel(
         prepare_us(0, 0, 64)
         turn_factors(0, "S")
         turn_factors(1, "S")
-        turn_unit(0)
+        both(paced_weights, 0, 0)
         quantize_us(0, 0)
         prepare_us(0, 1, 64)
-        quantize_meas(0, 0, 2)
+        turn_unit(0)
         quantize_us(0, 1)
         prepare_us(0, 2, 64)
-        both(paced_weights, 0, 0)
-        quantize_meas(0, 2, 3)
-        quantize_us(0, 2)
         both(paced_weights, 1, 0)
+        quantize_meas(0, 0, 2)
+        quantize_us(0, 2)
+        quantize_meas(0, 2, 3)
         turn_meas(1, 0, "S")
         square_sum(0, 1, 0, BANKS - 2)
         turn_meas(1, 1, "S")
@@ -449,6 +449,7 @@ def tile_spectral_tikhonov_imaging_s8_kernel(
         weigh(1, 1, 0)
         quantize_h(0, 0, 2)
         weigh(1, 1, 1)
+        spread_lam("S")
         both(project, 2, 0)
         group_h(1, 1, "V")
         image_banks(0, 0, 0, "SSSS")
@@ -470,7 +471,7 @@ def tile_spectral_tikhonov_imaging_s8_kernel(
         widen_basis(0)
         quantize_h(2, 0, 2)
         both(project, 3, 0)
-        both(weights, 3, 1)
+        slow_weights(3, 1, "SS")
         widen_basis(1)
         split_basis(0, "V")
         both(weigh, 3, 0)

@@ -193,12 +193,17 @@ def tile_spectral_tikhonov_imaging_s8_kernel(
             copy_on[eng](out=tiles["split", un][:], in_=src)
 
         def turn_meas(un, g, eng):
+            turn_meas_words(un, g)
+            empty_meas(un, g, eng)
+
+        def turn_meas_words(un, g):
             if g == 0:
                 tiles["mc", un] = keep.tile([128, PD, 256], U32, name="mc%d" % un, align_bytes=64)
                 tiles["ms", un] = keep.tile([128, PD, 256], U8, name="ms%d" % un, align_bytes=64)
                 tiles["mg", un] = work.tile([128, PD * 1024], BF16, name="mg", align_bytes=64)
             words = raw_meas[un][:].bitcast(F32)
-            bank = take_bank([128, 2, 2, 128], "mt")
+            bank = take_bank([128, 2, 2, 128], ("mt", g))
+            tiles["mt", g] = bank
             for e in range(2):
                 for w in range(2):
                     if ("split", un) in tiles:
@@ -206,9 +211,12 @@ def tile_spectral_tikhonov_imaging_s8_kernel(
                     else:
                         src = words[:, e, 256 * g + w : 256 * g + 256 : 2]
                     nc.tensor.transpose(bank[:, e, w, :], src, ident[:])
+
+        def empty_meas(un, g, eng):
+            bank = tiles["mt", g]
             dst = tiles["mg", un][:, 1024 * g : 1024 * g + 1024].bitcast(F32).rearrange("p (r e w) -> p r e w", e=2, w=2)
             copy_on[eng](out=dst, in_=bank[:].rearrange("p e w r -> p r e w"))
-            give_bank("mt")
+            give_bank(("mt", g))
 
         def quantize_meas(un, lo, hi):
             nc.vector.quantize_mx(
@@ -223,8 +231,8 @@ def tile_spectral_tikhonov_imaging_s8_kernel(
         def group_us(j, g, eng, lo, hi):
             if lo == 0:
                 tiles["ug", j, g] = work.tile([128, 2048], BF16, name="ug", align_bytes=64, bufs=3)
-            dst = tiles["ug", j, g][:].rearrange("p (t a b k) -> p a k b t", t=4, b=2, k=4)
-            src = raw_us[j, g][:].rearrange("p k (a b t) -> p a k b t", b=2, t=4)
+            dst = tiles["ug", j, g][:].rearrange("p (t a b k) -> p a t b k", t=4, b=2, k=4)
+            src = raw_us[j, g][:].rearrange("p k (a b t) -> p a t b k", b=2, t=4)
             copy_on[eng](out=dst[:, lo:hi], in_=src[:, lo:hi])
 
         def quantize_us(j, g):
@@ -251,7 +259,7 @@ def tile_spectral_tikhonov_imaging_s8_kernel(
             tiles["cb", un, j, th] = bank
 
         def weigh(un, j, th):
-            if (j, th) == (0, 0):
+            if ("hn", un) not in tiles:
                 tiles["hn", un] = keep.tile([128, PM * 4, 256], BF16, name="hn%d" % un)
             places = slice(4 * j + 2 * th, 4 * j + 2 * th + 2)
             weight = tiles["rw", un, j, th][:].rearrange("q i r e -> q i (r e)")
@@ -261,8 +269,8 @@ def tile_spectral_tikhonov_imaging_s8_kernel(
         def group_h(un, j, eng):
             if j == 0:
                 tiles["ha", un] = work.tile([128, PM * 1024], BF16, name="ha", align_bytes=64)
-            dst = tiles["ha", un][:, 1024 * j : 1024 * j + 1024].rearrange("q (e a b t) -> q a t b e", e=2, b=4, t=4)
-            src = tiles["hn", un][:, 4 * j : 4 * j + 4, :].rearrange("q t (a b e) -> q a t b e", b=4, e=2)
+            dst = tiles["ha", un][:, 1024 * j : 1024 * j + 1024].rearrange("q (e a b t) -> q a e b t", e=2, b=4, t=4)
+            src = tiles["hn", un][:, 4 * j : 4 * j + 4, :].rearrange("q t (a b e) -> q a e b t", b=4, e=2)
             copy_on[eng](out=dst, in_=src)
 
         def quantize_h(un, lo, hi):
@@ -277,11 +285,8 @@ def tile_spectral_tikhonov_imaging_s8_kernel(
 
         image_v = image.rearrange("(g p t) n -> g t p n", g=PF, p=128)
 
-        def image_part(un, e, n, eng):
-            if n % 2 == 0:
-                tiles["ob"] = stage.tile([128, 1024], F32, name="ob", tag="stage", bufs=7)
-            ob = tiles["ob"]
-            bank = take_bank([128, 512], "ib")
+        def image_bank(un, e, n):
+            bank = take_bank([128, 512], ("ib", n))
             for j in range(PM):
                 cols = slice(256 * j + 128 * e, 256 * j + 128 * e + 128)
                 nc.tensor.matmul_mx(
@@ -293,11 +298,15 @@ def tile_spectral_tikhonov_imaging_s8_kernel(
                     start=(j == 0),
                     stop=(j == PM - 1),
                 )
-            copy_on[eng](out=ob[:, 512 * (n % 2) : 512 * (n % 2) + 512], in_=bank[:])
-            give_bank("ib")
-            rows_out = image_v[un // 2, 2 * (un % 2) + e]
-            if n % 2 == 1:
-                nc.sync.dma_start(out=rows_out[:, 512 * n - 512 : 512 * n + 512], in_=ob[:])
+            return bank
+
+        def image_pair(un, e, half, engs):
+            banks = [image_bank(un, e, 2 * half + i) for i in range(2)]
+            ob = stage.tile([128, 1024], F32, name="ob", tag="stage", bufs=7)
+            for i in (1, 0) if engs[0] == engs[1] else (0, 1):
+                copy_on[engs[i]](out=ob[:, 512 * i : 512 * i + 512], in_=banks[i][:])
+                give_bank(("ib", 2 * half + i))
+            nc.sync.dma_start(out=image_v[un // 2, 2 * (un % 2) + e, :, 1024 * half : 1024 * half + 1024], in_=ob[:])
 
         bc = keep.tile([128, PF, R], U32, name="bc", align_bytes=64)
         bsc = keep.tile([128, PF, R], U8, name="bsc", align_bytes=64)
@@ -312,14 +321,18 @@ def tile_spectral_tikhonov_imaging_s8_kernel(
             tiles["bs", r] = keep.tile([128, 2, F // 4], F32, name="bs%d" % r)
             copy_on[eng](out=tiles["bs", r][:], in_=tiles["bw", r][:].bitcast(F32).rearrange("n (c w) -> n w c", w=2))
 
-        def turn_basis(g, h, eng):
-            bank = take_bank([128, 2, 2, 128], "bt")
+        def turn_basis(g, h):
+            bank = take_bank([128, 2, 2, 128], ("bt", g, h))
+            tiles["bt", g, h] = bank
             for r in range(2):
                 for w in range(2):
                     nc.tensor.transpose(bank[:, w, r, :], tiles["bs", 2 * h + r][:, w, 128 * g : 128 * g + 128], ident[:])
+
+        def empty_basis(g, h, eng):
+            bank = tiles["bt", g, h]
             dst = bg[:, 2048 * g + 1024 * h : 2048 * g + 1024 * h + 1024].bitcast(F32).rearrange("p (c w) -> p c w", w=2)
             copy_on[eng](out=dst, in_=bank[:].rearrange("p w r n -> p (r n) w"))
-            give_bank("bt")
+            give_bank(("bt", g, h))
 
         def quantize_basis():
             nc.vector.quantize_mx(
@@ -329,17 +342,21 @@ def tile_spectral_tikhonov_imaging_s8_kernel(
         ac = keep.tile([128, PF, M], U32, name="ac", align_bytes=64)
         asc = keep.tile([128, PF, M], U8, name="asc", align_bytes=64)
 
-        def turn_h(g, j, th, eng):
+        def turn_h(g, j, th):
             if (j, th) == (0, 0):
                 tiles["hb", g] = work.tile([128, PM * 2048], BF16, name="hb", align_bytes=64)
-            bank = take_bank([128, 2, 2, 128], "ht")
+            bank = take_bank([128, 2, 2, 128], ("ht", j, th))
+            tiles["ht", j, th] = bank
             for u in range(2):
                 words = tiles["hn", 2 * g + u][:].bitcast(F32)
                 for i in range(2):
                     nc.tensor.transpose(bank[:, u, i, :], words[:, 4 * j + 2 * th + i, :], ident[:])
+
+        def empty_h(g, j, th, eng):
+            bank = tiles["ht", j, th]
             dst = tiles["hb", g][:, 2048 * j + 1024 * th : 2048 * j + 1024 * th + 1024].bitcast(F32).rearrange("p (c u) -> p c u", u=2)
             copy_on[eng](out=dst, in_=bank[:].rearrange("p u i q -> p (i q) u"))
-            give_bank("ht")
+            give_bank(("ht", j, th))
 
         def quantize_hb(g, lo, hi):
             cols = slice(512 * lo, 512 * hi)
@@ -347,11 +364,8 @@ def tile_spectral_tikhonov_imaging_s8_kernel(
                 out=ac[:, g, cols].bitcast(FP8X4), scales=asc[:, g, cols], in_=tiles["hb", g][:, 2048 * lo : 2048 * hi]
             )
 
-        def comps_part(r, j, eng):
-            if j == 0:
-                tiles["co"] = stage.tile([128, M], F32, name="co", tag="stage", bufs=7)
-            co = tiles["co"]
-            bank = take_bank([128, 512], "kb")
+        def comps_bank(r, j):
+            bank = take_bank([128, 512], ("kb", j))
             cols = slice(512 * j, 512 * j + 512)
             for g in range(PF):
                 nc.tensor.matmul_mx(
@@ -363,25 +377,45 @@ def tile_spectral_tikhonov_imaging_s8_kernel(
                     start=(g == 0),
                     stop=(g == PF - 1),
                 )
-            copy_on[eng](out=co[:, cols].rearrange("p (q t) -> p q t", t=4), in_=bank[:].rearrange("p (t q) -> p q t", t=4))
-            give_bank("kb")
-            if r == 3:
-                nc.sync.dma_start(out=comps[128 * r : 128 * r + 128, cols], in_=co[:, cols])
-            elif j == PM - 1:
-                nc.sync.dma_start(out=comps[128 * r : 128 * r + 128, :], in_=co[:])
+            return bank
+
+        def comps_rows(r, engs, whole=True):
+            banks = [comps_bank(r, j) for j in range(PM)]
+            co = stage.tile([128, M], F32, name="co", tag="stage", bufs=7)
+            rows_out = comps[128 * r : 128 * r + 128, :]
+            for j in (1, 0) if engs[0] == engs[1] else (0, 1):
+                cols = slice(512 * j, 512 * j + 512)
+                copy_on[engs[j]](out=co[:, cols].rearrange("p (q t) -> p q t", t=4), in_=banks[j][:].rearrange("p (t q) -> p q t", t=4))
+                give_bank(("kb", j))
+                if not whole:
+                    nc.sync.dma_start(out=rows_out[:, cols], in_=co[:, cols])
+            if whole:
+                nc.sync.dma_start(out=rows_out, in_=co[:])
 
         def both(step, un, j):
             for th in range(2):
                 step(un, j, th)
 
-        def image_banks(un, e, first, engs):
-            for i, eng in enumerate(engs):
-                image_part(un, e, first + i, eng)
+        def back(step, un, j):
+            for th in (1, 0):
+                step(un, j, th)
 
         def prepare_us(j, g, split):
             group_us(j, g, "V", 0, split)
             if split < 64:
                 group_us(j, g, "S", split, 64)
+
+        def weights_of(un, j):
+            both(square_sum, un, j)
+            back(invert, un, j)
+
+        def turn_four(turn, empty, engs):
+            quarters = [(a, b) for a in range(2) for b in range(2)]
+            for a, b in quarters:
+                turn(a, b)
+            for a in range(2):
+                for b in (1, 0):
+                    empty(a, b, engs[a])
 
         def turn_unit(un):
             for g in range(PD):
@@ -421,27 +455,25 @@ def tile_spectral_tikhonov_imaging_s8_kernel(
         quantize_unit(1)
         quantize_us(1, 0)
         prepare_us(1, 1, 32)
-        project(1, 0, 0)
+        both(project, 1, 0)
+        weigh(0, 0, 1)
         quantize_us(1, 1)
         prepare_us(1, 2, 32)
         turn_meas(2, 0, "S")
         turn_meas(2, 1, "S")
-        project(1, 0, 1)
-        turn_meas(2, 2, "S")
         weigh(0, 0, 0)
-        square_sum(1, 1, 0)
+        both(square_sum, 1, 1)
+        turn_meas(2, 2, "S")
         quantize_us(1, 2)
-        weigh(0, 0, 1)
-        square_sum(1, 1, 1)
         both(project, 0, 1)
         group_h(0, 0, "S")
-        both(invert, 1, 1)
+        back(invert, 1, 1)
         quantize_meas(2, 0, 2)
         weigh(0, 1, 0)
         weigh(1, 0, 0)
         weigh(0, 1, 1)
         both(project, 1, 1)
-        both(weights, 2, 0)
+        weights_of(2, 0)
         weigh(1, 0, 1)
         group_h(1, 0, "S")
         quantize_meas(2, 2, 3)
@@ -452,60 +484,61 @@ def tile_spectral_tikhonov_imaging_s8_kernel(
         spread_lam("S")
         both(project, 2, 0)
         group_h(1, 1, "V")
-        image_banks(0, 0, 0, "SSSS")
-        weigh(2, 0, 0)
-        quantize_h(1, 0, 2)
-        weigh(2, 0, 1)
+        image_pair(0, 0, 0, "SS")
+        back(weigh, 2, 0)
+        image_pair(0, 0, 1, "SS")
         split_meas(3, "V")
-        both(weights, 2, 1)
+        quantize_h(1, 0, 2)
+        weights_of(2, 1)
         both(project, 2, 1)
-        image_banks(0, 1, 0, "SS")
         group_h(2, 0, "V")
-        turn_unit(3)
-        both(weigh, 2, 1)
-        image_banks(0, 1, 2, "VS")
-        quantize_unit(3)
-        both(weights, 3, 0)
+        image_pair(0, 1, 0, "SS")
+        back(weigh, 2, 1)
+        for g in range(PD):
+            turn_meas_words(3, g)
+        for g in (1, 0, 2):
+            empty_meas(3, g, "S")
         group_h(2, 1, "V")
-        image_banks(1, 0, 0, "SSSS")
-        widen_basis(0)
+        image_pair(0, 1, 1, "VV")
+        quantize_unit(3)
+        slow_weights(3, 0, "SS")
+        image_pair(1, 0, 0, "VV")
         quantize_h(2, 0, 2)
+        image_pair(1, 0, 1, "SS")
         both(project, 3, 0)
         slow_weights(3, 1, "SS")
+        widen_basis(0)
+        back(weigh, 3, 0)
+        image_pair(1, 1, 0, "SS")
         widen_basis(1)
-        split_basis(0, "V")
-        both(weigh, 3, 0)
-        image_banks(1, 1, 0, "SS")
-        split_basis(1, "V")
         both(project, 3, 1)
-        widen_basis(2)
-        image_banks(1, 1, 2, "SS")
-        both(weigh, 3, 1)
-        for j in range(PM):
-            for th in range(2):
-                turn_h(0, j, th, "S")
+        split_basis(0, "V")
+        image_pair(1, 1, 1, "SS")
+        back(weigh, 3, 1)
+        turn_four(lambda j, th: turn_h(0, j, th), lambda j, th, eng: empty_h(0, j, th, eng), "SS")
         group_h(3, 0, "V")
+        split_basis(1, "V")
         group_h(3, 1, "V")
-        widen_basis(3)
-        image_banks(2, 0, 0, "SSSS")
-        split_basis(2, "V")
+        widen_basis(2)
+        image_pair(2, 0, 0, "SS")
         quantize_h(3, 0, 2)
+        image_pair(2, 0, 1, "SS")
+        widen_basis(3)
+        split_basis(2, "V")
         split_basis(3, "V")
+        image_pair(2, 1, 0, "SS")
+        image_pair(2, 1, 1, "VV")
+        turn_four(lambda h, g: turn_basis(g, h), lambda h, g, eng: empty_basis(g, h, eng), "SV")
+        image_pair(3, 0, 0, "SS")
         quantize_hb(0, 0, 2)
-        image_banks(2, 1, 0, "SVSV")
-        for g in range(PF):
-            for h in range(2):
-                turn_basis(g, h, "SV"[h])
-        image_banks(3, 0, 0, "SS")
+        image_pair(3, 0, 1, "SS")
         quantize_basis()
-        image_banks(3, 0, 2, "SV")
-        for j in range(PM):
-            for th in range(2):
-                turn_h(1, j, th, "SV"[th])
+        turn_four(lambda j, th: turn_h(1, j, th), lambda j, th, eng: empty_h(1, j, th, eng), "VS")
         quantize_hb(1, 0, 1)
-        image_banks(3, 1, 0, "SS")
         quantize_hb(1, 1, 2)
-        image_banks(3, 1, 2, "SS")
-        for r in range(4):
-            for j in range(PM):
-                comps_part(r, j, "SV"[j])
+        image_pair(3, 1, 0, "SS")
+        image_pair(3, 1, 1, "VS")
+        comps_rows(0, "VS")
+        comps_rows(1, "VS")
+        comps_rows(2, "VS")
+        comps_rows(3, "VS", False)

@@ -48,6 +48,8 @@ def tile_spectral_tikhonov_imaging_s8_kernel(
         def give_bank(name):
             free_banks.append(held[name])
 
+        root_rows = keep.tile([128, 512], BF16, name="root_rows")
+        nc.vector.memset(root_rows[:], 0.0)
         factors = keep.tile([128, 2, 8, 128], BF16, name="factors")
         nc.vector.memset(factors[:], 0.0)
         vs = keep.tile([128, PM, P], U8, name="vs", align_bytes=64)
@@ -69,14 +71,13 @@ def tile_spectral_tikhonov_imaging_s8_kernel(
             raw_us[j, g] = stage.tile([128, 4, 512], BF16, name="raw_us", tag="stage", bufs=7)
             nc.sync.dma_start(out=raw_us[j, g][:], in_=us_v[g, :, :, 512 * j : 512 * j + 512])
 
-        roots = keep.tile([128, 2, 16], BF16, name="roots")
         for i, vec in enumerate((lam, sigma)):
-            nc.scalar.dma_start(out=roots[:, i, 0:8].rearrange("q (g t) -> q g t", t=4), in_=vec.rearrange("(g q t) -> q g t", q=128, t=4))
+            nc.scalar.dma_start(out=root_rows[2 * i : 2 * i + 2, :], in_=vec.rearrange("(g x) -> g x", g=2))
         nc.scalar.activation(out=factors[:, 1, :, 0:2], in_=factors[:, 1, :, 8:10], func=ACT.Abs_reciprocal_sqrt, bias=1.0)
         nc.scalar.activation(out=factors[:, 0, :, 4:8], in_=factors[:, 0, :, 8:12], func=ACT.Abs_reciprocal_sqrt, bias=1.0)
         load_us(0, 0)
-        load_us(0, 1)
         load_meas(0)
+        load_us(0, 1)
         load_us(0, 2)
         load_meas(1)
         load_us(1, 0)
@@ -96,22 +97,40 @@ def tile_spectral_tikhonov_imaging_s8_kernel(
         b_scale = keep.tile([128, F], F32, name="b_scale")
         nc.sync.dma_start(out=b_scale[:], in_=basis_scale.rearrange("o k -> (o k)").partition_broadcast(128))
 
+        roots = keep.tile([128, 2, 16], BF16, name="roots")
         squares = keep.tile([128, 2, 8], F32, name="squares")
-        nc.vector.tensor_tensor(out=squares[:], in0=roots[:, :, 0:8], in1=roots[:, :, 0:8], op=MULT)
-        nc.vector.tensor_copy(out=factors[:, 0, :, 2:4], in_=roots[:, 0, 0:8].unsqueeze(2).to_broadcast([128, 8, 2]))
         s4 = keep.tile([128, PM * 4], F32, name="s4")
-        nc.vector.tensor_tensor(out=s4[:], in0=squares[:, 1, :], in1=squares[:, 1, :], op=MULT)
-        nc.vector.tensor_copy(out=factors[:, 0, :, 0], in_=squares[:, 0, :])
-        nc.vector.tensor_scalar(out=factors[:, 1, :, 2], in0=squares[:, 1, :], scalar1=2.0, scalar2=None, op0=MULT)
-        nc.vector.tensor_copy(out=factors[:, 1, :, 4], in_=s4[:])
-        nc.vector.tensor_tensor(out=factors[:, 0, :, 1], in0=squares[:, 0, :], in1=factors[:, 0, :, 0], op=SUB)
-        nc.vector.scalar_tensor_tensor(
-            out=factors[:, 1, :, 3], in0=squares[:, 1, :], scalar=2.0, in1=factors[:, 1, :, 2], op0=MULT, op1=SUB
-        )
         rest = keep.tile([128, PM * 4], F32, name="rest")
-        nc.vector.tensor_tensor(out=rest[:], in0=s4[:], in1=factors[:, 1, :, 4], op=SUB)
-        nc.vector.tensor_tensor(out=factors[:, 1, :, 5], in0=s4[:], in1=factors[:, 1, :, 4], op=SUB)
-        nc.vector.tensor_tensor(out=factors[:, 1, :, 6], in0=rest[:], in1=factors[:, 1, :, 5], op=SUB)
+
+        def spread_roots():
+            root_bank = take_bank([128, 4, 4], "rb")
+            for t in range(4):
+                nc.tensor.matmul(out=root_bank[:, t, :], lhsT=root_rows[:, t:512:4], rhs=ident_b[:, 0:4], start=True, stop=True)
+            nc.vector.tensor_copy(
+                out=roots[:, :, 0:8].rearrange("q v (g t) -> q v g t", t=4), in_=root_bank[:].rearrange("q t (v g) -> q v g t", v=2)
+            )
+            give_bank("rb")
+
+        def factor_step(level):
+            if level == 0:
+                nc.vector.tensor_tensor(out=squares[:], in0=roots[:, :, 0:8], in1=roots[:, :, 0:8], op=MULT)
+                nc.vector.tensor_copy(out=factors[:, 0, :, 2:4], in_=roots[:, 0, 0:8].unsqueeze(2).to_broadcast([128, 8, 2]))
+            if level == 1:
+                nc.vector.tensor_tensor(out=s4[:], in0=squares[:, 1, :], in1=squares[:, 1, :], op=MULT)
+                nc.vector.tensor_copy(out=factors[:, 0, :, 0], in_=squares[:, 0, :])
+                nc.vector.tensor_scalar(out=factors[:, 1, :, 2], in0=squares[:, 1, :], scalar1=2.0, scalar2=None, op0=MULT)
+            if level == 2:
+                nc.vector.tensor_copy(out=factors[:, 1, :, 4], in_=s4[:])
+                nc.vector.tensor_tensor(out=factors[:, 0, :, 1], in0=squares[:, 0, :], in1=factors[:, 0, :, 0], op=SUB)
+                nc.vector.scalar_tensor_tensor(
+                    out=factors[:, 1, :, 3], in0=squares[:, 1, :], scalar=2.0, in1=factors[:, 1, :, 2], op0=MULT, op1=SUB
+                )
+            if level == 3:
+                nc.vector.tensor_tensor(out=rest[:], in0=s4[:], in1=factors[:, 1, :, 4], op=SUB)
+                nc.vector.tensor_tensor(out=factors[:, 1, :, 5], in0=s4[:], in1=factors[:, 1, :, 4], op=SUB)
+            if level == 4:
+                nc.vector.tensor_tensor(out=factors[:, 1, :, 6], in0=rest[:], in1=factors[:, 1, :, 5], op=SUB)
+
         rows = keep.tile([128, 2, 8, 128], BF16, name="rows")
 
         def turn_factors(i, eng):
@@ -120,6 +139,12 @@ def tile_spectral_tikhonov_imaging_s8_kernel(
                 nc.tensor.matmul(out=bank[:, c, :], lhsT=factors[:, i, c, :], rhs=ident_b[:], start=True, stop=True)
             copy_on[eng](out=rows[:, i], in_=bank[:])
             give_bank("ft")
+
+        def warm_up(src, count):
+            bank = take_bank([128, 512], "warm")
+            for i in range(count):
+                nc.tensor.matmul(out=bank[:], lhsT=src[:, 0:128], rhs=src, start=True, stop=True)
+            give_bank("warm")
 
         copy_on = {"S": nc.scalar.copy, "V": nc.vector.tensor_copy}
         tiles = {}
@@ -431,25 +456,33 @@ def tile_spectral_tikhonov_imaging_s8_kernel(
             for th in range(2):
                 square_of(un, j, th, engs[th])
 
-        prepare_us(0, 0, 64)
+        spread_roots()
+        warm_up(root_rows[:], 4)
+        factor_step(0)
+        for level in range(1, 5):
+            factor_step(level)
+            group_us(0, 0, "V", 16 * level - 16, 16 * level)
         turn_factors(0, "S")
+        turn_meas(0, 0, "S")
         turn_factors(1, "S")
+        turn_meas(0, 1, "S")
+        turn_meas(0, 2, "S")
         both(paced_weights, 0, 0)
+        weights_of(1, 0)
         quantize_us(0, 0)
         prepare_us(0, 1, 64)
-        turn_unit(0)
+        quantize_meas(0, 0, 2)
         quantize_us(0, 1)
         prepare_us(0, 2, 64)
-        both(paced_weights, 1, 0)
-        quantize_meas(0, 0, 2)
-        quantize_us(0, 2)
+        warm_up(raw_us[0, 2][:, 0, :], 3)
         quantize_meas(0, 2, 3)
+        quantize_us(0, 2)
         turn_meas(1, 0, "S")
         square_sum(0, 1, 0, BANKS - 2)
         turn_meas(1, 1, "S")
         square_sum(0, 1, 1, BANKS - 1)
         turn_meas(1, 2, "S")
-        both(invert, 0, 1)
+        back(invert, 0, 1)
         both(project, 0, 0)
         prepare_us(1, 0, 64)
         quantize_unit(1)

@@ -49,7 +49,7 @@ def tile_spectral_tikhonov_imaging_s8_kernel(
             free_banks.append(held[name])
 
         root_rows = keep.tile([128, 512], BF16, name="root_rows")
-        nc.vector.memset(root_rows[:], 0.0)
+        nc.vector.memset(root_rows[0:124, :], 0.0)
         factors = keep.tile([128, 2, 8, 128], BF16, name="factors")
         nc.vector.memset(factors[:], 0.0)
         vs = keep.tile([128, PM, P], U8, name="vs", align_bytes=64)
@@ -72,7 +72,7 @@ def tile_spectral_tikhonov_imaging_s8_kernel(
             nc.sync.dma_start(out=raw_us[j, g][:], in_=us_v[g, :, :, 512 * j : 512 * j + 512])
 
         for i, vec in enumerate((lam, sigma)):
-            nc.scalar.dma_start(out=root_rows[2 * i : 2 * i + 2, :], in_=vec.rearrange("(g x) -> g x", g=2))
+            nc.sync.dma_start(out=root_rows[124 + 2 * i : 126 + 2 * i, :], in_=vec.rearrange("(g x) -> g x", g=2))
         nc.scalar.activation(out=factors[:, 1, :, 0:2], in_=factors[:, 1, :, 8:10], func=ACT.Abs_reciprocal_sqrt, bias=1.0)
         nc.scalar.activation(out=factors[:, 0, :, 4:8], in_=factors[:, 0, :, 8:12], func=ACT.Abs_reciprocal_sqrt, bias=1.0)
         load_us(0, 0)
@@ -105,7 +105,7 @@ def tile_spectral_tikhonov_imaging_s8_kernel(
         def spread_roots():
             root_bank = take_bank([128, 4, 4], "rb")
             for t in range(4):
-                nc.tensor.matmul(out=root_bank[:, t, :], lhsT=root_rows[:, t:512:4], rhs=ident_b[:, 0:4], start=True, stop=True)
+                nc.tensor.matmul(out=root_bank[:, t, :], lhsT=root_rows[:, t:512:4], rhs=ident_b[:, 124:128], start=True, stop=True)
             nc.vector.tensor_copy(
                 out=roots[:, :, 0:8].rearrange("q v (g t) -> q v g t", t=4), in_=root_bank[:].rearrange("q t (v g) -> q v g t", v=2)
             )

@@ -14,15 +14,21 @@ I32 = mybir.dt.int32
 E4M3 = mybir.dt.float8_e4m3fn
 FP8X4 = mybir.dt.float8_e4m3fn_x4
 FP4X4 = mybir.dt.float4_e2m1fn_x4
-ACT = mybir.ActivationFunctionType
+RSQRT = mybir.ActivationFunctionType.Abs_reciprocal_sqrt
 MULT = mybir.AluOpType.mult
 SUB = mybir.AluOpType.subtract
 
 PD = D // 512
 PM = M // 512
 PF = F // 512
-UNITS = 4
 BANKS = 8
+ROOT_ROW = 124
+US_PARTS = 64
+H_PARTS = 32
+US_SHARE = 24
+H_SHARE = 20
+OUT_BUFS = 7
+WEIGHT_BUFS = 6
 
 
 def tile_spectral_tikhonov_imaging_s8_kernel(
@@ -32,546 +38,454 @@ def tile_spectral_tikhonov_imaging_s8_kernel(
     with ExitStack() as ctx:
         keep = ctx.enter_context(tc.tile_pool(name="keep", bufs=1))
         work = ctx.enter_context(tc.tile_pool(name="work", bufs=2))
-        stage = ctx.enter_context(tc.tile_pool(name="stage", bufs=7))
+        stage = ctx.enter_context(tc.tile_pool(name="stage", bufs=OUT_BUFS))
         psum = ctx.enter_context(tc.psum_pool(name="psum", bufs=1))
 
         ctx.enter_context(tc.manual_schedule())
 
-        free_banks = list(range(BANKS - 2))
+        copy_on = {"S": nc.scalar.copy, "V": nc.vector.tensor_copy}
+        tiles = {}
+
+        free_banks = list(range(BANKS))
         held = {}
 
-        def take_bank(shape, name, dtype=F32):
-            held[name] = free_banks[0]
-            free_banks.remove(held[name])
-            return psum.tile(shape, dtype, name="bank", tag="bank%d" % held[name], bufs=1)
+        def take_bank(key, shape, dtype=F32):
+            held[key] = free_banks[0]
+            free_banks.remove(held[key])
+            tiles[key] = psum.tile(shape, dtype, name="bank", tag="bank%d" % held[key], bufs=1)
+            return tiles[key]
 
-        def give_bank(name):
-            free_banks.append(held[name])
+        def give_bank(key):
+            free_banks.append(held[key])
 
         root_rows = keep.tile([128, 512], BF16, name="root_rows")
-        nc.vector.memset(root_rows[0:124, :], 0.0)
+        nc.vector.memset(root_rows[0:ROOT_ROW, :], 0.0)
         factors = keep.tile([128, 2, 8, 128], BF16, name="factors")
         nc.vector.memset(factors[:], 0.0)
-        vs = keep.tile([128, PM, P], U8, name="vs", align_bytes=64)
-        nc.vector.memset(vs[:].bitcast(I32), 0)
+        vt_scale = keep.tile([128, PM, P], U8, name="vt_scale", align_bytes=64)
+        nc.vector.memset(vt_scale[:].bitcast(I32), 0)
         ident = keep.tile([128, 128], F32, name="ident")
         make_identity(nc, ident[:])
         ident_b = keep.tile([128, 128], BF16, name="ident_b")
         nc.vector.tensor_copy(out=ident_b[:], in_=ident[:])
+        nc.scalar.activation(out=factors[:, 1, :, 0:2], in_=factors[:, 1, :, 8:10], func=RSQRT, bias=1.0)
+        nc.scalar.activation(out=factors[:, 0, :, 4:8], in_=factors[:, 0, :, 8:12], func=RSQRT, bias=1.0)
 
-        raw_meas, raw_us = {}, {}
         meas_v = meas.rearrange("(g p t) d -> g p t d", g=PF, p=128)
         us_v = us.rearrange("(g p k) m -> g p k m", p=128, k=4)
 
         def load_meas(un):
-            raw_meas[un] = work.tile([128, 2, D], BF16, name="raw_meas", tag="raw_meas", bufs=4)
-            nc.sync.dma_start(out=raw_meas[un][:], in_=meas_v[un // 2, :, 2 * (un % 2) : 2 * (un % 2) + 2, :])
+            tiles["meas", un] = work.tile([128, 2, D], BF16, name="raw_meas", tag="raw_meas", bufs=4)
+            nc.sync.dma_start(out=tiles["meas", un][:], in_=meas_v[un // 2, :, 2 * (un % 2) : 2 * (un % 2) + 2, :])
 
-        def load_us(j, g):
-            raw_us[j, g] = stage.tile([128, 4, 512], BF16, name="raw_us", tag="stage", bufs=7)
-            nc.sync.dma_start(out=raw_us[j, g][:], in_=us_v[g, :, :, 512 * j : 512 * j + 512])
+        def load_us(g):
+            tiles["us", g] = work.tile([128, 4, M], BF16, name="raw_us", tag="wide", bufs=3, align_bytes=64)
+            nc.sync.dma_start(out=tiles["us", g][:], in_=us_v[g])
 
-        for i, vec in enumerate((lam, sigma)):
-            nc.sync.dma_start(out=root_rows[124 + 2 * i : 126 + 2 * i, :], in_=vec.rearrange("(g x) -> g x", g=2))
-        nc.scalar.activation(out=factors[:, 1, :, 0:2], in_=factors[:, 1, :, 8:10], func=ACT.Abs_reciprocal_sqrt, bias=1.0)
-        nc.scalar.activation(out=factors[:, 0, :, 4:8], in_=factors[:, 0, :, 8:12], func=ACT.Abs_reciprocal_sqrt, bias=1.0)
-        load_us(0, 0)
+        for side, vec in enumerate((lam, sigma)):
+            first = ROOT_ROW + 2 * side
+            nc.sync.dma_start(out=root_rows[first : first + 2, :], in_=vec.rearrange("(g x) -> g x", g=2))
+        load_us(0)
         load_meas(0)
-        load_us(0, 1)
-        load_us(0, 2)
         load_meas(1)
-        load_us(1, 0)
-        load_us(1, 1)
+        load_us(1)
+        load_us(2)
         load_meas(2)
-        load_us(1, 2)
-        for q in range(4):
+        for quad in range(4):
             nc.sync.dma_start(
-                out=vs[32 * q : 32 * q + 4, :, :].bitcast(I32),
-                in_=vt_scales[:, 4 * q : 4 * q + 4, :].rearrange("g r n -> r g n").bitcast(I32),
+                out=vt_scale[32 * quad : 32 * quad + 4, :, :].bitcast(I32),
+                in_=vt_scales[:, 4 * quad : 4 * quad + 4, :].rearrange("g r n -> r g n").bitcast(I32),
             )
         vt = keep.tile([128, PM, 2 * P], U8, name="vt", align_bytes=64)
         nc.sync.dma_start(out=vt[:], in_=vt_words.rearrange("g p n -> p g n"))
         load_meas(3)
-        b_raw = keep.tile([128, 4, F], U8, name="b_raw")
-        nc.sync.dma_start(out=b_raw[:], in_=basis_bytes.rearrange("(r p) f -> p r f", p=128))
-        b_scale = keep.tile([128, F], F32, name="b_scale")
-        nc.sync.dma_start(out=b_scale[:], in_=basis_scale.rearrange("o k -> (o k)").partition_broadcast(128))
+        basis_raw = keep.tile([128, 4, F], U8, name="basis_raw")
+        nc.sync.dma_start(out=basis_raw[:], in_=basis_bytes.rearrange("(r p) f -> p r f", p=128))
+        basis_wide_scale = keep.tile([128, F], F32, name="basis_wide_scale")
+        nc.sync.dma_start(out=basis_wide_scale[:], in_=basis_scale.rearrange("o k -> (o k)").partition_broadcast(128))
 
-        roots = keep.tile([128, 2, 16], BF16, name="roots")
+        roots = keep.tile([128, 2, 8], BF16, name="roots")
         squares = keep.tile([128, 2, 8], F32, name="squares")
-        s4 = keep.tile([128, PM * 4], F32, name="s4")
-        rest = keep.tile([128, PM * 4], F32, name="rest")
-
-        def spread_roots():
-            root_bank = take_bank([128, 4, 4], "rb")
-            for t in range(4):
-                nc.tensor.matmul(out=root_bank[:, t, :], lhsT=root_rows[:, t:512:4], rhs=ident_b[:, 124:128], start=True, stop=True)
-            nc.vector.tensor_copy(
-                out=roots[:, :, 0:8].rearrange("q v (g t) -> q v g t", t=4), in_=root_bank[:].rearrange("q t (v g) -> q v g t", v=2)
-            )
-            give_bank("rb")
-
-        def factor_step(level):
-            if level == 0:
-                nc.vector.tensor_tensor(out=squares[:], in0=roots[:, :, 0:8], in1=roots[:, :, 0:8], op=MULT)
-                nc.vector.tensor_copy(out=factors[:, 0, :, 2:4], in_=roots[:, 0, 0:8].unsqueeze(2).to_broadcast([128, 8, 2]))
-            if level == 1:
-                nc.vector.tensor_tensor(out=s4[:], in0=squares[:, 1, :], in1=squares[:, 1, :], op=MULT)
-                nc.vector.tensor_copy(out=factors[:, 0, :, 0], in_=squares[:, 0, :])
-                nc.vector.tensor_scalar(out=factors[:, 1, :, 2], in0=squares[:, 1, :], scalar1=2.0, scalar2=None, op0=MULT)
-            if level == 2:
-                nc.vector.tensor_copy(out=factors[:, 1, :, 4], in_=s4[:])
-                nc.vector.tensor_tensor(out=factors[:, 0, :, 1], in0=squares[:, 0, :], in1=factors[:, 0, :, 0], op=SUB)
-                nc.vector.scalar_tensor_tensor(
-                    out=factors[:, 1, :, 3], in0=squares[:, 1, :], scalar=2.0, in1=factors[:, 1, :, 2], op0=MULT, op1=SUB
-                )
-            if level == 3:
-                nc.vector.tensor_tensor(out=rest[:], in0=s4[:], in1=factors[:, 1, :, 4], op=SUB)
-                nc.vector.tensor_tensor(out=factors[:, 1, :, 5], in0=s4[:], in1=factors[:, 1, :, 4], op=SUB)
-            if level == 4:
-                nc.vector.tensor_tensor(out=factors[:, 1, :, 6], in0=rest[:], in1=factors[:, 1, :, 5], op=SUB)
-
+        fourth = keep.tile([128, 8], F32, name="fourth")
+        rest = keep.tile([128, 8], F32, name="rest")
         rows = keep.tile([128, 2, 8, 128], BF16, name="rows")
 
-        def turn_factors(i, eng):
-            bank = take_bank([128, 8, 128], "ft", BF16)
-            for c in range(8):
-                nc.tensor.matmul(out=bank[:, c, :], lhsT=factors[:, i, c, :], rhs=ident_b[:], start=True, stop=True)
-            copy_on[eng](out=rows[:, i], in_=bank[:])
-            give_bank("ft")
-
-        def warm_up(src, count):
-            bank = take_bank([128, 512], "warm")
-            for i in range(count):
-                nc.tensor.matmul(out=bank[:], lhsT=src[:, 0:128], rhs=src, start=True, stop=True)
-            give_bank("warm")
-
-        copy_on = {"S": nc.scalar.copy, "V": nc.vector.tensor_copy}
-        tiles = {}
-
-        def square_sum(un, j, th, bank_no=None):
-            if bank_no is None:
-                bank = take_bank([128, 2, 2, 128], ("wb", un, j, th))
-            else:
-                held["wb", un, j, th] = bank_no
-                bank = psum.tile([128, 2, 2, 128], F32, name="bank", tag="bank%d" % bank_no, bufs=1)
-            tiles["wb", un, j, th] = bank
-            for i in range(2):
-                nc.tensor.matmul(
-                    out=bank[:, i].rearrange("q e r -> q (e r)"),
-                    lhsT=rows[:, 1, 4 * j + 2 * th + i, :],
-                    rhs=rows[:, 0, 2 * un : 2 * un + 2, :].rearrange("k e r -> k (e r)"),
-                    start=True,
-                    stop=True,
-                )
-
-        def invert(un, j, th, give=True):
-            tiles["rw", un, j, th] = work.tile([128, 2, 128, 2], F32, name="rw", bufs=6)
-            nc.scalar.activation(
-                out=tiles["rw", un, j, th][:],
-                in_=tiles["wb", un, j, th][:].rearrange("q i e r -> q i r e"),
-                func=ACT.Abs_reciprocal_sqrt,
-            )
-            if give:
-                give_bank(("wb", un, j, th))
-
-        def weights(un, j, th):
-            square_sum(un, j, th)
-            invert(un, j, th)
-
-        def paced_weights(un, j, th):
-            square_sum(un, j, th, BANKS - 2 + th)
-            invert(un, j, th, False)
-
-        lam_wide = keep.tile([128, 2, 128, 2], F32, name="lam_wide")
-
-        def spread_lam(eng):
-            bank = take_bank([128, 2, 2, 128], "lb")
+        def make_factors():
+            bank = take_bank("roots", [128, 4, 4])
             for t in range(4):
-                column = roots[:, 0, 4 + t : 5 + t].to_broadcast([128, 128])
-                nc.tensor.matmul(out=bank[:, t // 2, t % 2, :], lhsT=column, rhs=ident_b[:], start=True, stop=True)
-            copy_on[eng](out=lam_wide[:], in_=bank[:].rearrange("q u e r -> q u r e"))
-            give_bank("lb")
-
-        def roots_of(un, j, th):
-            tiles["rt", un, j, th] = work.tile([128, 2, 128, 2], F32, name="rt", bufs=2)
-            for i in range(2):
-                place = 4 * j + 2 * th + i
-                nc.scalar.activation(
-                    out=tiles["rt", un, j, th][:, i],
-                    in_=lam_wide[:, un % 2],
-                    func=ACT.Abs_reciprocal_sqrt,
-                    bias=squares[:, 1, place : place + 1],
+                nc.tensor.matmul(
+                    out=bank[:, t, :], lhsT=root_rows[:, t:512:4], rhs=ident_b[:, ROOT_ROW:128], start=True, stop=True
                 )
+            nc.vector.tensor_copy(
+                out=roots[:].rearrange("q v (g t) -> q v g t", t=4), in_=bank[:].rearrange("q t (v g) -> q v g t", v=2)
+            )
+            give_bank("roots")
+            lam_side, sigma_side = factors[:, 0], factors[:, 1]
+            nc.vector.tensor_tensor(out=squares[:], in0=roots[:], in1=roots[:], op=MULT)
+            nc.vector.tensor_copy(out=lam_side[:, :, 2:4], in_=roots[:, 0, :].unsqueeze(2).to_broadcast([128, 8, 2]))
+            nc.vector.tensor_tensor(out=fourth[:], in0=squares[:, 1, :], in1=squares[:, 1, :], op=MULT)
+            nc.vector.tensor_copy(out=lam_side[:, :, 0], in_=squares[:, 0, :])
+            nc.vector.tensor_scalar(out=sigma_side[:, :, 2], in0=squares[:, 1, :], scalar1=2.0, scalar2=None, op0=MULT)
+            nc.vector.tensor_copy(out=sigma_side[:, :, 4], in_=fourth[:])
+            nc.vector.tensor_tensor(out=lam_side[:, :, 1], in0=squares[:, 0, :], in1=lam_side[:, :, 0], op=SUB)
+            nc.vector.scalar_tensor_tensor(
+                out=sigma_side[:, :, 3], in0=squares[:, 1, :], scalar=2.0, in1=sigma_side[:, :, 2], op0=MULT, op1=SUB
+            )
+            nc.vector.tensor_tensor(out=rest[:], in0=fourth[:], in1=sigma_side[:, :, 4], op=SUB)
+            nc.vector.tensor_tensor(out=sigma_side[:, :, 5], in0=fourth[:], in1=sigma_side[:, :, 4], op=SUB)
+            nc.vector.tensor_tensor(out=sigma_side[:, :, 6], in0=rest[:], in1=sigma_side[:, :, 5], op=SUB)
 
-        def square_of(un, j, th, eng):
-            tiles["rw", un, j, th] = work.tile([128, 2, 128, 2], F32, name="rw", bufs=6)
-            root = tiles["rt", un, j, th]
-            if eng == "S":
-                nc.scalar.activation(out=tiles["rw", un, j, th][:], in_=root[:], func=ACT.Square)
-            else:
-                nc.vector.tensor_tensor(out=tiles["rw", un, j, th][:], in0=root[:], in1=root[:], op=MULT)
+        def turn_factors(side):
+            bank = take_bank("factors", [128, 8, 128], BF16)
+            for block in range(8):
+                nc.tensor.matmul(out=bank[:, block, :], lhsT=factors[:, side, block, :], rhs=ident_b[:], start=True, stop=True)
+            nc.vector.tensor_copy(out=rows[:, side], in_=bank[:])
+            give_bank("factors")
 
-        def split_meas(un, eng):
+        def square_sums(un, j):
+            for th in range(2):
+                bank = take_bank(("square", th), [128, 2, 2, 128])
+                for i in range(2):
+                    nc.tensor.matmul(
+                        out=bank[:, i].rearrange("q e r -> q (e r)"),
+                        lhsT=rows[:, 1, 4 * j + 2 * th + i, :],
+                        rhs=rows[:, 0, 2 * un : 2 * un + 2, :].rearrange("k e r -> k (e r)"),
+                        start=True,
+                        stop=True,
+                    )
+
+        def invert(un, j):
+            for th in (1, 0):
+                tiles["weight", un, j, th] = work.tile([128, 2, 128, 2], F32, name="weight", bufs=WEIGHT_BUFS)
+                nc.scalar.activation(
+                    out=tiles["weight", un, j, th][:], in_=tiles["square", th][:].rearrange("q i e r -> q i r e"), func=RSQRT
+                )
+                give_bank(("square", th))
+
+        def weights(un, j):
+            square_sums(un, j)
+            invert(un, j)
+
+        def split_meas(un):
             tiles["split", un] = work.tile([128, 2, 2, D // 4], F32, name="split", tag="raw_meas", bufs=4)
-            src = raw_meas[un][:].bitcast(F32).rearrange("r e (c w) -> r e w c", w=2)
-            copy_on[eng](out=tiles["split", un][:], in_=src)
+            words = tiles["meas", un][:].bitcast(F32)
+            nc.vector.tensor_copy(out=tiles["split", un][:], in_=words.rearrange("r e (c w) -> r e w c", w=2))
 
-        def turn_meas(un, g, eng):
-            turn_meas_words(un, g)
-            empty_meas(un, g, eng)
-
-        def turn_meas_words(un, g):
+        def turn_meas(un, g):
             if g == 0:
-                tiles["mc", un] = keep.tile([128, PD, 256], U32, name="mc%d" % un, align_bytes=64)
-                tiles["ms", un] = keep.tile([128, PD, 256], U8, name="ms%d" % un, align_bytes=64)
-                tiles["mg", un] = work.tile([128, PD * 1024], BF16, name="mg", align_bytes=64)
-            words = raw_meas[un][:].bitcast(F32)
-            bank = take_bank([128, 2, 2, 128], ("mt", g))
-            tiles["mt", g] = bank
+                tiles["meas_codes", un] = keep.tile([128, PD, 256], U32, name="meas_codes%d" % un, align_bytes=64)
+                tiles["meas_scales", un] = keep.tile([128, PD, 256], U8, name="meas_scales%d" % un, align_bytes=64)
+                tiles["meas_k", un] = work.tile([128, PD * 1024], BF16, name="meas_k", align_bytes=64)
+            bank = take_bank(("meas_turn", g), [128, 2, 2, 128])
             for e in range(2):
                 for w in range(2):
                     if ("split", un) in tiles:
                         src = tiles["split", un][:, e, w, 128 * g : 128 * g + 128]
                     else:
-                        src = words[:, e, 256 * g + w : 256 * g + 256 : 2]
+                        src = tiles["meas", un][:].bitcast(F32)[:, e, 256 * g + w : 256 * g + 256 : 2]
                     nc.tensor.transpose(bank[:, e, w, :], src, ident[:])
 
         def empty_meas(un, g, eng):
-            bank = tiles["mt", g]
-            dst = tiles["mg", un][:, 1024 * g : 1024 * g + 1024].bitcast(F32).rearrange("p (r e w) -> p r e w", e=2, w=2)
-            copy_on[eng](out=dst, in_=bank[:].rearrange("p e w r -> p r e w"))
-            give_bank(("mt", g))
+            dst = tiles["meas_k", un][:, 1024 * g : 1024 * g + 1024].bitcast(F32).rearrange("p (r e w) -> p r e w", e=2, w=2)
+            copy_on[eng](out=dst, in_=tiles["meas_turn", g][:].rearrange("p e w r -> p r e w"))
+            give_bank(("meas_turn", g))
 
-        def quantize_meas(un, lo, hi):
-            nc.vector.quantize_mx(
-                out=tiles["mc", un][:, lo:hi, :].rearrange("p g c -> p (g c)").bitcast(FP8X4),
-                scales=tiles["ms", un][:, lo:hi, :].rearrange("p g c -> p (g c)"),
-                in_=tiles["mg", un][:, 1024 * lo : 1024 * hi],
-            )
+        def turn_and_empty_meas(un, g, eng):
+            turn_meas(un, g)
+            empty_meas(un, g, eng)
 
-        uc = keep.tile([128, PD, M], U32, name="uc", align_bytes=64)
-        usc = keep.tile([128, PD, M], U8, name="usc", align_bytes=64)
+        def quantize_meas(un):
+            for lo, hi in ((0, 2), (2, 3)):
+                nc.vector.quantize_mx(
+                    out=tiles["meas_codes", un][:, lo:hi, :].rearrange("p g c -> p (g c)").bitcast(FP8X4),
+                    scales=tiles["meas_scales", un][:, lo:hi, :].rearrange("p g c -> p (g c)"),
+                    in_=tiles["meas_k", un][:, 1024 * lo : 1024 * hi],
+                )
 
-        def group_us(j, g, eng, lo, hi):
+        us_codes = keep.tile([128, PD, M], U32, name="us_codes", align_bytes=64)
+        us_scales = keep.tile([128, PD, M], U8, name="us_scales", align_bytes=64)
+
+        def group_us(j, g, eng, lo=0, hi=US_PARTS):
             if lo == 0:
-                tiles["ug", j, g] = work.tile([128, 2048], BF16, name="ug", align_bytes=64, bufs=3)
-            dst = tiles["ug", j, g][:].rearrange("p (t a b k) -> p a t b k", t=4, b=2, k=4)
-            src = raw_us[j, g][:].rearrange("p k (a b t) -> p a t b k", b=2, t=4)
+                tiles["us_k", j, g] = work.tile([128, 2048], BF16, name="us_k", align_bytes=64, bufs=3)
+            dst = tiles["us_k", j, g][:].rearrange("p (t a b k) -> p a t b k", t=4, b=2, k=4)
+            src = tiles["us", g][:, :, 512 * j : 512 * j + 512].rearrange("p k (a b t) -> p a t b k", b=2, t=4)
             copy_on[eng](out=dst[:, lo:hi], in_=src[:, lo:hi])
 
         def quantize_us(j, g):
-            nc.vector.quantize_mx(
-                out=uc[:, g, 512 * j : 512 * j + 512].bitcast(FP8X4),
-                scales=usc[:, g, 512 * j : 512 * j + 512],
-                in_=tiles["ug", j, g][:],
-            )
+            cols = slice(512 * j, 512 * j + 512)
+            nc.vector.quantize_mx(out=us_codes[:, g, cols].bitcast(FP8X4), scales=us_scales[:, g, cols], in_=tiles["us_k", j, g][:])
 
-        def project(un, j, th):
-            bank = take_bank([128, 2, 256], ("cb", un, j, th))
-            for i in range(2):
-                col = 512 * j + 128 * (2 * th + i)
-                for g in range(PD):
+        def project_pass(un, j, g, halves=(0, 1)):
+            for th in halves:
+                if g == 0:
+                    take_bank(("c", un, j, th), [128, 2, 256])
+                for i in range(2):
+                    col = 512 * j + 128 * (2 * th + i)
                     nc.tensor.matmul_mx(
-                        out=bank[:, i, :],
-                        lhsT=uc[:, g, col : col + 128].bitcast(FP8X4),
-                        lhsT_scale=usc[:, g, col : col + 128],
-                        rhs=tiles["mc", un][:, g, :].bitcast(FP8X4),
-                        rhs_scale=tiles["ms", un][:, g, :],
-                        start=(g == 0),
-                        stop=(g == PD - 1),
+                        out=tiles["c", un, j, th][:, i, :],
+                        lhsT=us_codes[:, g, col : col + 128].bitcast(FP8X4),
+                        lhsT_scale=us_scales[:, g, col : col + 128],
+                        rhs=tiles["meas_codes", un][:, g, :].bitcast(FP8X4),
+                        rhs_scale=tiles["meas_scales", un][:, g, :],
+                        start=((g, i) == (0, 0)),
+                        stop=((g, i) == (PD - 1, 1)),
                     )
-            tiles["cb", un, j, th] = bank
 
-        def weigh(un, j, th):
-            if ("hn", un) not in tiles:
-                tiles["hn", un] = keep.tile([128, PM * 4, 256], BF16, name="hn%d" % un)
-            places = slice(4 * j + 2 * th, 4 * j + 2 * th + 2)
-            weight = tiles["rw", un, j, th][:].rearrange("q i r e -> q i (r e)")
-            nc.vector.tensor_tensor(out=tiles["hn", un][:, places, :], in0=tiles["cb", un, j, th][:], in1=weight, op=MULT)
-            give_bank(("cb", un, j, th))
+        def project(un, j):
+            for th in range(2):
+                for g in range(PD):
+                    project_pass(un, j, g, (th,))
 
-        def group_h(un, j, eng):
+        def weigh(un, j):
             if j == 0:
-                tiles["ha", un] = work.tile([128, PM * 1024], BF16, name="ha", align_bytes=64)
-            dst = tiles["ha", un][:, 1024 * j : 1024 * j + 1024].rearrange("q (e a b t) -> q a e b t", e=2, b=4, t=4)
-            src = tiles["hn", un][:, 4 * j : 4 * j + 4, :].rearrange("q t (a b e) -> q a e b t", b=4, e=2)
-            copy_on[eng](out=dst, in_=src)
+                tiles["h", un] = keep.tile([128, PM * 4, 256], BF16, name="h%d" % un)
+            for th in (1, 0):
+                places = slice(4 * j + 2 * th, 4 * j + 2 * th + 2)
+                weight = tiles["weight", un, j, th][:].rearrange("q i r e -> q i (r e)")
+                nc.vector.tensor_tensor(out=tiles["h", un][:, places, :], in0=tiles["c", un, j, th][:], in1=weight, op=MULT)
+                give_bank(("c", un, j, th))
 
-        def quantize_h(un, lo, hi):
-            if lo == 0:
-                tiles["hc", un] = keep.tile([128, PM * 256], U32, name="hc%d" % un, align_bytes=64)
-                tiles["hs", un] = keep.tile([128, PM * 256], U8, name="hs%d" % un, align_bytes=64)
+        def group_h(un, j, eng, lo=0, hi=H_PARTS):
+            if ("h_modes", un) not in tiles:
+                tiles["h_modes", un] = work.tile([128, PM * 1024], BF16, name="h_modes", align_bytes=64)
+            dst = tiles["h_modes", un][:, 1024 * j : 1024 * j + 1024].rearrange("q (e a b t) -> q a e b t", e=2, b=4, t=4)
+            src = tiles["h", un][:, 4 * j : 4 * j + 4, :].rearrange("q t (a b e) -> q a e b t", b=4, e=2)
+            copy_on[eng](out=dst[:, lo:hi], in_=src[:, lo:hi])
+
+        def quantize_h_modes(un):
+            tiles["h_codes", un] = keep.tile([128, PM * 256], U32, name="h_codes%d" % un, align_bytes=64)
+            tiles["h_scales", un] = keep.tile([128, PM * 256], U8, name="h_scales%d" % un, align_bytes=64)
             nc.vector.quantize_mx(
-                out=tiles["hc", un][:, 256 * lo : 256 * hi].bitcast(FP8X4),
-                scales=tiles["hs", un][:, 256 * lo : 256 * hi],
-                in_=tiles["ha", un][:, 1024 * lo : 1024 * hi],
+                out=tiles["h_codes", un][:].bitcast(FP8X4), scales=tiles["h_scales", un][:], in_=tiles["h_modes", un][:]
             )
 
         image_v = image.rearrange("(g p t) n -> g t p n", g=PF, p=128)
 
-        def image_bank(un, e, n):
-            bank = take_bank([128, 512], ("ib", n))
-            for j in range(PM):
-                cols = slice(256 * j + 128 * e, 256 * j + 128 * e + 128)
-                nc.tensor.matmul_mx(
-                    out=bank[:],
-                    lhsT=tiles["hc", un][:, cols].bitcast(FP8X4),
-                    lhsT_scale=tiles["hs", un][:, cols],
-                    rhs=vt[:, j, 1024 * n : 1024 * n + 1024].bitcast(FP4X4),
-                    rhs_scale=vs[:, j, 512 * n : 512 * n + 512],
-                    start=(j == 0),
-                    stop=(j == PM - 1),
-                )
-            return bank
+        def emptying_order(engs):
+            return (1, 0) if engs[0] == engs[1] else (0, 1)
 
-        def image_pair(un, e, half, engs):
-            banks = [image_bank(un, e, 2 * half + i) for i in range(2)]
-            ob = stage.tile([128, 1024], F32, name="ob", tag="stage", bufs=7)
-            for i in (1, 0) if engs[0] == engs[1] else (0, 1):
-                copy_on[engs[i]](out=ob[:, 512 * i : 512 * i + 512], in_=banks[i][:])
-                give_bank(("ib", 2 * half + i))
-            nc.sync.dma_start(out=image_v[un // 2, 2 * (un % 2) + e, :, 1024 * half : 1024 * half + 1024], in_=ob[:])
+        def image_half(un, e, half, engs):
+            for i in range(2):
+                n = 2 * half + i
+                bank = take_bank(("image", i), [128, 512])
+                for j in range(PM):
+                    cols = slice(256 * j + 128 * e, 256 * j + 128 * e + 128)
+                    nc.tensor.matmul_mx(
+                        out=bank[:],
+                        lhsT=tiles["h_codes", un][:, cols].bitcast(FP8X4),
+                        lhsT_scale=tiles["h_scales", un][:, cols],
+                        rhs=vt[:, j, 1024 * n : 1024 * n + 1024].bitcast(FP4X4),
+                        rhs_scale=vt_scale[:, j, 512 * n : 512 * n + 512],
+                        start=(j == 0),
+                        stop=(j == PM - 1),
+                    )
+            result = stage.tile([128, 1024], F32, name="result", tag="result")
+            for i in emptying_order(engs):
+                copy_on[engs[i]](out=result[:, 512 * i : 512 * i + 512], in_=tiles["image", i][:])
+                give_bank(("image", i))
+            nc.sync.dma_start(out=image_v[un // 2, 2 * (un % 2) + e, :, 1024 * half : 1024 * half + 1024], in_=result[:])
 
-        bc = keep.tile([128, PF, R], U32, name="bc", align_bytes=64)
-        bsc = keep.tile([128, PF, R], U8, name="bsc", align_bytes=64)
+        basis_codes = keep.tile([128, PF * R], U32, name="basis_codes", align_bytes=64)
+        basis_scales = keep.tile([128, PF * R], U8, name="basis_scales", align_bytes=64)
 
-        bg = keep.tile([128, PF * 2048], BF16, name="bg", align_bytes=64)
+        def scale_basis(r):
+            tiles["basis", r] = work.tile([128, F], BF16, name="basis")
+            nc.vector.tensor_tensor(out=tiles["basis", r][:], in0=basis_raw[:, r, :].bitcast(E4M3), in1=basis_wide_scale[:], op=MULT)
 
-        def widen_basis(r):
-            tiles["bw", r] = work.tile([128, F], BF16, name="bw")
-            nc.vector.tensor_tensor(out=tiles["bw", r][:], in0=b_raw[:, r, :].bitcast(E4M3), in1=b_scale[:], op=MULT)
+        def split_basis(r):
+            tiles["basis_split", r] = keep.tile([128, 2, F // 4], F32, name="basis_split%d" % r)
+            words = tiles["basis", r][:].bitcast(F32)
+            nc.vector.tensor_copy(out=tiles["basis_split", r][:], in_=words.rearrange("n (c w) -> n w c", w=2))
 
-        def split_basis(r, eng):
-            tiles["bs", r] = keep.tile([128, 2, F // 4], F32, name="bs%d" % r)
-            copy_on[eng](out=tiles["bs", r][:], in_=tiles["bw", r][:].bitcast(F32).rearrange("n (c w) -> n w c", w=2))
-
-        def turn_basis(g, h):
-            bank = take_bank([128, 2, 2, 128], ("bt", g, h))
-            tiles["bt", g, h] = bank
-            for r in range(2):
-                for w in range(2):
-                    nc.tensor.transpose(bank[:, w, r, :], tiles["bs", 2 * h + r][:, w, 128 * g : 128 * g + 128], ident[:])
-
-        def empty_basis(g, h, eng):
-            bank = tiles["bt", g, h]
-            dst = bg[:, 2048 * g + 1024 * h : 2048 * g + 1024 * h + 1024].bitcast(F32).rearrange("p (c w) -> p c w", w=2)
-            copy_on[eng](out=dst, in_=bank[:].rearrange("p w r n -> p (r n) w"))
-            give_bank(("bt", g, h))
+        def turn_basis(engs):
+            tiles["basis_k"] = work.tile([128, PF * 2048], BF16, name="basis_k", tag="wide", bufs=3, align_bytes=64)
+            for half in range(2):
+                for g in range(PF):
+                    bank = take_bank(("basis_turn", half, g), [128, 2, 2, 128])
+                    for i in range(2):
+                        for w in range(2):
+                            src = tiles["basis_split", 2 * half + i][:, w, 128 * g : 128 * g + 128]
+                            nc.tensor.transpose(bank[:, w, i, :], src, ident[:])
+            for half in range(2):
+                for g in (1, 0):
+                    first = 2048 * g + 1024 * half
+                    dst = tiles["basis_k"][:, first : first + 1024].bitcast(F32).rearrange("p (c w) -> p c w", w=2)
+                    copy_on[engs[half]](out=dst, in_=tiles["basis_turn", half, g][:].rearrange("p w i n -> p (i n) w"))
+                    give_bank(("basis_turn", half, g))
 
         def quantize_basis():
-            nc.vector.quantize_mx(
-                out=bc[:].rearrange("p g r -> p (g r)").bitcast(FP8X4), scales=bsc[:].rearrange("p g r -> p (g r)"), in_=bg[:]
-            )
+            nc.vector.quantize_mx(out=basis_codes[:].bitcast(FP8X4), scales=basis_scales[:], in_=tiles["basis_k"][:])
 
-        ac = keep.tile([128, PF, M], U32, name="ac", align_bytes=64)
-        asc = keep.tile([128, PF, M], U8, name="asc", align_bytes=64)
+        frame_codes = keep.tile([128, PF, M], U32, name="frame_codes", align_bytes=64)
+        frame_scales = keep.tile([128, PF, M], U8, name="frame_scales", align_bytes=64)
 
-        def turn_h(g, j, th):
-            if (j, th) == (0, 0):
-                tiles["hb", g] = work.tile([128, PM * 2048], BF16, name="hb", align_bytes=64)
-            bank = take_bank([128, 2, 2, 128], ("ht", j, th))
-            tiles["ht", j, th] = bank
-            for u in range(2):
-                words = tiles["hn", 2 * g + u][:].bitcast(F32)
-                for i in range(2):
-                    nc.tensor.transpose(bank[:, u, i, :], words[:, 4 * j + 2 * th + i, :], ident[:])
+        def turn_h(g, engs):
+            tiles["h_frames", g] = work.tile([128, PM * 2048], BF16, name="h_frames", tag="wide", bufs=3, align_bytes=64)
+            for j in range(PM):
+                for th in range(2):
+                    bank = take_bank(("h_turn", j, th), [128, 2, 2, 128])
+                    for u in range(2):
+                        words = tiles["h", 2 * g + u][:].bitcast(F32)
+                        for i in range(2):
+                            nc.tensor.transpose(bank[:, u, i, :], words[:, 4 * j + 2 * th + i, :], ident[:])
+            for j in range(PM):
+                for th in (1, 0):
+                    first = 2048 * j + 1024 * th
+                    dst = tiles["h_frames", g][:, first : first + 1024].bitcast(F32).rearrange("p (c u) -> p c u", u=2)
+                    copy_on[engs[j]](out=dst, in_=tiles["h_turn", j, th][:].rearrange("p u i q -> p (i q) u"))
+                    give_bank(("h_turn", j, th))
 
-        def empty_h(g, j, th, eng):
-            bank = tiles["ht", j, th]
-            dst = tiles["hb", g][:, 2048 * j + 1024 * th : 2048 * j + 1024 * th + 1024].bitcast(F32).rearrange("p (c u) -> p c u", u=2)
-            copy_on[eng](out=dst, in_=bank[:].rearrange("p u i q -> p (i q) u"))
-            give_bank(("ht", j, th))
-
-        def quantize_hb(g, lo, hi):
+        def quantize_h_frames(g, lo, hi):
             cols = slice(512 * lo, 512 * hi)
             nc.vector.quantize_mx(
-                out=ac[:, g, cols].bitcast(FP8X4), scales=asc[:, g, cols], in_=tiles["hb", g][:, 2048 * lo : 2048 * hi]
+                out=frame_codes[:, g, cols].bitcast(FP8X4),
+                scales=frame_scales[:, g, cols],
+                in_=tiles["h_frames", g][:, 2048 * lo : 2048 * hi],
             )
 
-        def comps_bank(r, j):
-            bank = take_bank([128, 512], ("kb", j))
-            cols = slice(512 * j, 512 * j + 512)
-            for g in range(PF):
-                nc.tensor.matmul_mx(
-                    out=bank[:],
-                    lhsT=bc[:, g, 128 * r : 128 * r + 128].bitcast(FP8X4),
-                    lhsT_scale=bsc[:, g, 128 * r : 128 * r + 128],
-                    rhs=ac[:, g, cols].bitcast(FP8X4),
-                    rhs_scale=asc[:, g, cols],
-                    start=(g == 0),
-                    stop=(g == PF - 1),
-                )
-            return bank
-
-        def comps_rows(r, engs, whole=True):
-            banks = [comps_bank(r, j) for j in range(PM)]
-            co = stage.tile([128, M], F32, name="co", tag="stage", bufs=7)
-            rows_out = comps[128 * r : 128 * r + 128, :]
-            for j in (1, 0) if engs[0] == engs[1] else (0, 1):
+        def comps_rows(r, engs, store_by_bank):
+            for j in range(PM):
+                bank = take_bank(("comps", j), [128, 512])
                 cols = slice(512 * j, 512 * j + 512)
-                copy_on[engs[j]](out=co[:, cols].rearrange("p (q t) -> p q t", t=4), in_=banks[j][:].rearrange("p (t q) -> p q t", t=4))
-                give_bank(("kb", j))
-                if not whole:
-                    nc.sync.dma_start(out=rows_out[:, cols], in_=co[:, cols])
-            if whole:
-                nc.sync.dma_start(out=rows_out, in_=co[:])
+                for g in range(PF):
+                    stationary = slice(R * g + 128 * r, R * g + 128 * r + 128)
+                    nc.tensor.matmul_mx(
+                        out=bank[:],
+                        lhsT=basis_codes[:, stationary].bitcast(FP8X4),
+                        lhsT_scale=basis_scales[:, stationary],
+                        rhs=frame_codes[:, g, cols].bitcast(FP8X4),
+                        rhs_scale=frame_scales[:, g, cols],
+                        start=(g == 0),
+                        stop=(g == PF - 1),
+                    )
+            result = stage.tile([128, M], F32, name="result", tag="result")
+            rows_out = comps[128 * r : 128 * r + 128, :]
+            for j in range(PM):
+                cols = slice(512 * j, 512 * j + 512)
+                copy_on[engs[j]](
+                    out=result[:, cols].rearrange("p (q t) -> p q t", t=4),
+                    in_=tiles["comps", j][:].rearrange("p (t q) -> p q t", t=4),
+                )
+                give_bank(("comps", j))
+                if store_by_bank:
+                    nc.sync.dma_start(out=rows_out[:, cols], in_=result[:, cols])
+            if not store_by_bank:
+                nc.sync.dma_start(out=rows_out, in_=result[:])
 
-        def both(step, un, j):
-            for th in range(2):
-                step(un, j, th)
-
-        def back(step, un, j):
-            for th in (1, 0):
-                step(un, j, th)
-
-        def prepare_us(j, g, split):
-            group_us(j, g, "V", 0, split)
-            if split < 64:
-                group_us(j, g, "S", split, 64)
-
-        def weights_of(un, j):
-            both(square_sum, un, j)
-            back(invert, un, j)
-
-        def turn_four(turn, empty, engs):
-            quarters = [(a, b) for a in range(2) for b in range(2)]
-            for a, b in quarters:
-                turn(a, b)
-            for a in range(2):
-                for b in (1, 0):
-                    empty(a, b, engs[a])
-
-        def turn_unit(un):
-            for g in range(PD):
-                turn_meas(un, g, "S")
-
-        def quantize_unit(un):
-            quantize_meas(un, 0, 2)
-            quantize_meas(un, 2, 3)
-
-        def slow_weights(un, j, engs):
-            for th in range(2):
-                roots_of(un, j, th)
-            for th in range(2):
-                square_of(un, j, th, engs[th])
-
-        spread_roots()
-        warm_up(root_rows[:], 4)
-        factor_step(0)
-        for level in range(1, 5):
-            factor_step(level)
-            group_us(0, 0, "V", 16 * level - 16, 16 * level)
-        turn_factors(0, "S")
-        turn_meas(0, 0, "S")
-        turn_factors(1, "S")
-        turn_meas(0, 1, "S")
-        turn_meas(0, 2, "S")
-        both(paced_weights, 0, 0)
-        weights_of(1, 0)
+        group_us(1, 0, "S")
+        make_factors()
+        group_us(0, 0, "V")
+        turn_factors(0)
         quantize_us(0, 0)
-        prepare_us(0, 1, 64)
-        quantize_meas(0, 0, 2)
-        quantize_us(0, 1)
-        prepare_us(0, 2, 64)
-        warm_up(raw_us[0, 2][:, 0, :], 3)
-        quantize_meas(0, 2, 3)
-        quantize_us(0, 2)
-        turn_meas(1, 0, "S")
-        square_sum(0, 1, 0, BANKS - 2)
-        turn_meas(1, 1, "S")
-        square_sum(0, 1, 1, BANKS - 1)
-        turn_meas(1, 2, "S")
-        back(invert, 0, 1)
-        both(project, 0, 0)
-        prepare_us(1, 0, 64)
-        quantize_unit(1)
-        quantize_us(1, 0)
-        prepare_us(1, 1, 32)
-        both(project, 1, 0)
-        weigh(0, 0, 1)
-        quantize_us(1, 1)
-        prepare_us(1, 2, 32)
-        turn_meas(2, 0, "S")
-        turn_meas(2, 1, "S")
-        weigh(0, 0, 0)
-        both(square_sum, 1, 1)
-        turn_meas(2, 2, "S")
-        quantize_us(1, 2)
-        both(project, 0, 1)
-        group_h(0, 0, "S")
-        back(invert, 1, 1)
-        quantize_meas(2, 0, 2)
-        weigh(0, 1, 0)
-        weigh(1, 0, 0)
-        weigh(0, 1, 1)
-        both(project, 1, 1)
-        weights_of(2, 0)
-        weigh(1, 0, 1)
-        group_h(1, 0, "S")
-        quantize_meas(2, 2, 3)
-        group_h(0, 1, "V")
-        weigh(1, 1, 0)
-        quantize_h(0, 0, 2)
-        weigh(1, 1, 1)
-        spread_lam("S")
-        both(project, 2, 0)
-        group_h(1, 1, "V")
-        image_pair(0, 0, 0, "SS")
-        back(weigh, 2, 0)
-        image_pair(0, 0, 1, "SS")
-        split_meas(3, "V")
-        quantize_h(1, 0, 2)
-        weights_of(2, 1)
-        both(project, 2, 1)
-        group_h(2, 0, "V")
-        image_pair(0, 1, 0, "SS")
-        back(weigh, 2, 1)
+        turn_factors(1)
         for g in range(PD):
-            turn_meas_words(3, g)
+            turn_and_empty_meas(0, g, "S")
+        quantize_us(1, 0)
+        for g in range(PD):
+            turn_and_empty_meas(1, g, "S")
+        weights(0, 0)
+        quantize_meas(0)
+        group_us(0, 1, "V")
+        project_pass(0, 0, 0)
+        project_pass(0, 1, 0)
+        group_us(1, 1, "S")
+        quantize_meas(1)
+        quantize_us(0, 1)
+        project_pass(1, 0, 0)
+        project_pass(0, 0, 1)
+        square_sums(0, 1)
+        project_pass(1, 0, 1)
+        group_us(0, 2, "V")
+        group_us(1, 2, "V", 0, US_SHARE)
+        group_us(1, 2, "S", US_SHARE, US_PARTS)
+        invert(0, 1)
+        quantize_us(1, 1)
+        quantize_us(0, 2)
+        project_pass(0, 1, 1)
+        project_pass(0, 0, 2)
+        quantize_us(1, 2)
+        project_pass(0, 1, 2)
+        project_pass(1, 0, 2)
+
+        weigh(0, 0)
+        project(1, 1)
+        group_h(0, 0, "S")
+        square_sums(1, 0)
+        weigh(0, 1)
+        group_h(0, 1, "V", 0, H_SHARE)
+        group_h(0, 1, "S", H_SHARE, H_PARTS)
+        invert(1, 0)
+        quantize_h_modes(0)
+        turn_and_empty_meas(2, 0, "V")
+        turn_and_empty_meas(2, 1, "S")
+        weigh(1, 0)
+        turn_and_empty_meas(2, 2, "S")
+        square_sums(1, 1)
+
+        image_half(0, 0, 0, "VS")
+        invert(1, 1)
+        quantize_meas(2)
+        image_half(0, 0, 1, "SS")
+        weigh(1, 1)
+        weights(2, 0)
+        group_h(1, 1, "V")
+        split_meas(3)
+        project(2, 0)
+        weights(2, 1)
+        group_h(1, 0, "S")
+        weigh(2, 0)
+        quantize_h_modes(1)
+        project(2, 1)
+        image_half(0, 1, 0, "SS")
+        group_h(2, 0, "V")
+        weigh(2, 1)
+        for g in range(PD):
+            turn_meas(3, g)
         for g in (1, 0, 2):
             empty_meas(3, g, "S")
+        image_half(0, 1, 1, "VV")
+        quantize_meas(3)
         group_h(2, 1, "V")
-        image_pair(0, 1, 1, "VV")
-        quantize_unit(3)
-        slow_weights(3, 0, "SS")
-        image_pair(1, 0, 0, "VV")
-        quantize_h(2, 0, 2)
-        image_pair(1, 0, 1, "SS")
-        both(project, 3, 0)
-        slow_weights(3, 1, "SS")
-        widen_basis(0)
-        back(weigh, 3, 0)
-        image_pair(1, 1, 0, "SS")
-        widen_basis(1)
-        both(project, 3, 1)
-        split_basis(0, "V")
-        image_pair(1, 1, 1, "SS")
-        back(weigh, 3, 1)
-        turn_four(lambda j, th: turn_h(0, j, th), lambda j, th, eng: empty_h(0, j, th, eng), "SS")
+
+        weights(3, 0)
+        image_half(1, 0, 0, "SS")
+        quantize_h_modes(2)
+        scale_basis(0)
+        image_half(1, 0, 1, "SS")
+        project(3, 0)
+        weights(3, 1)
+        scale_basis(1)
+        split_basis(0)
+        weigh(3, 0)
+        image_half(1, 1, 0, "SS")
+        split_basis(1)
+        project(3, 1)
+        scale_basis(2)
+        image_half(1, 1, 1, "SS")
+        weigh(3, 1)
+
+        turn_h(0, "SS")
         group_h(3, 0, "V")
-        split_basis(1, "V")
+        split_basis(2)
         group_h(3, 1, "V")
-        widen_basis(2)
-        image_pair(2, 0, 0, "SS")
-        quantize_h(3, 0, 2)
-        image_pair(2, 0, 1, "SS")
-        widen_basis(3)
-        split_basis(2, "V")
-        split_basis(3, "V")
-        image_pair(2, 1, 0, "SS")
-        image_pair(2, 1, 1, "VV")
-        turn_four(lambda h, g: turn_basis(g, h), lambda h, g, eng: empty_basis(g, h, eng), "SV")
-        image_pair(3, 0, 0, "SS")
-        quantize_hb(0, 0, 2)
-        image_pair(3, 0, 1, "SS")
+        scale_basis(3)
+        image_half(2, 0, 0, "SS")
+        quantize_h_modes(3)
+        image_half(2, 0, 1, "SS")
+        split_basis(3)
+        quantize_h_frames(0, 0, 2)
+        image_half(2, 1, 0, "SS")
+        image_half(2, 1, 1, "VV")
+        turn_basis("SV")
+        image_half(3, 0, 0, "SS")
         quantize_basis()
-        turn_four(lambda j, th: turn_h(1, j, th), lambda j, th, eng: empty_h(1, j, th, eng), "VS")
-        quantize_hb(1, 0, 1)
-        quantize_hb(1, 1, 2)
-        image_pair(3, 1, 0, "SS")
-        image_pair(3, 1, 1, "VS")
-        comps_rows(0, "VS")
-        comps_rows(1, "VS")
-        comps_rows(2, "VS")
-        comps_rows(3, "VS", False)
+        image_half(3, 0, 1, "VS")
+        turn_h(1, "VS")
+        quantize_h_frames(1, 0, 1)
+        quantize_h_frames(1, 1, 2)
+        image_half(3, 1, 0, "SS")
+        image_half(3, 1, 1, "VS")
+
+        for r in range(R // 128):
+            comps_rows(r, "VS", store_by_bank=(r == R // 128 - 1))

@@ -262,10 +262,7 @@ def tile_spectral_tikhonov_imaging_s8_kernel(
 
         image_v = image.rearrange("(g p t) n -> g t p n", g=PF, p=128)
 
-        def emptying_order(engs):
-            return (1, 0) if engs[0] == engs[1] else (0, 1)
-
-        def image_half(un, e, half, engs):
+        def image_half(un, e, half, engs, order=(1, 0)):
             for i in range(2):
                 n = 2 * half + i
                 bank = take_bank(("image", i), [128, 512])
@@ -281,7 +278,7 @@ def tile_spectral_tikhonov_imaging_s8_kernel(
                         stop=(j == PM - 1),
                     )
             result = stage.tile([128, 1024], F32, name="result", tag="result")
-            for i in emptying_order(engs):
+            for i in order:
                 copy_on[engs[i]](out=result[:, 512 * i : 512 * i + 512], in_=tiles["image", i][:])
                 give_bank(("image", i))
             nc.sync.dma_start(out=image_v[un // 2, 2 * (un % 2) + e, :, 1024 * half : 1024 * half + 1024], in_=result[:])
@@ -293,10 +290,10 @@ def tile_spectral_tikhonov_imaging_s8_kernel(
             tiles["basis", r] = work.tile([128, F], BF16, name="basis")
             nc.vector.tensor_tensor(out=tiles["basis", r][:], in0=basis_raw[:, r, :].bitcast(E4M3), in1=basis_wide_scale[:], op=MULT)
 
-        def split_basis(r):
+        def split_basis(r, eng):
             tiles["basis_split", r] = keep.tile([128, 2, F // 4], F32, name="basis_split%d" % r)
             words = tiles["basis", r][:].bitcast(F32)
-            nc.vector.tensor_copy(out=tiles["basis_split", r][:], in_=words.rearrange("n (c w) -> n w c", w=2))
+            copy_on[eng](out=tiles["basis_split", r][:], in_=words.rearrange("n (c w) -> n w c", w=2))
 
         def turn_basis(engs):
             tiles["basis_k"] = work.tile([128, PF * 2048], BF16, name="basis_k", tag="wide", bufs=3, align_bytes=64)
@@ -320,21 +317,20 @@ def tile_spectral_tikhonov_imaging_s8_kernel(
         frame_codes = keep.tile([128, PF, M], U32, name="frame_codes", align_bytes=64)
         frame_scales = keep.tile([128, PF, M], U8, name="frame_scales", align_bytes=64)
 
-        def turn_h(g, engs):
-            tiles["h_frames", g] = work.tile([128, PM * 2048], BF16, name="h_frames", tag="wide", bufs=3, align_bytes=64)
-            for j in range(PM):
-                for th in range(2):
-                    bank = take_bank(("h_turn", j, th), [128, 2, 2, 128])
-                    for u in range(2):
-                        words = tiles["h", 2 * g + u][:].bitcast(F32)
-                        for i in range(2):
-                            nc.tensor.transpose(bank[:, u, i, :], words[:, 4 * j + 2 * th + i, :], ident[:])
-            for j in range(PM):
-                for th in (1, 0):
-                    first = 2048 * j + 1024 * th
-                    dst = tiles["h_frames", g][:, first : first + 1024].bitcast(F32).rearrange("p (c u) -> p c u", u=2)
-                    copy_on[engs[j]](out=dst, in_=tiles["h_turn", j, th][:].rearrange("p u i q -> p (i q) u"))
-                    give_bank(("h_turn", j, th))
+        def turn_h(g, j, eng):
+            if j == 0:
+                tiles["h_frames", g] = work.tile([128, PM * 2048], BF16, name="h_frames", tag="wide", bufs=3, align_bytes=64)
+            for th in range(2):
+                bank = take_bank(("h_turn", th), [128, 2, 2, 128])
+                for u in range(2):
+                    words = tiles["h", 2 * g + u][:].bitcast(F32)
+                    for i in range(2):
+                        nc.tensor.transpose(bank[:, u, i, :], words[:, 4 * j + 2 * th + i, :], ident[:])
+            for th in (1, 0):
+                first = 2048 * j + 1024 * th
+                dst = tiles["h_frames", g][:, first : first + 1024].bitcast(F32).rearrange("p (c u) -> p c u", u=2)
+                copy_on[eng](out=dst, in_=tiles["h_turn", th][:].rearrange("p u i q -> p (i q) u"))
+                give_bank(("h_turn", th))
 
         def quantize_h_frames(g, lo, hi):
             cols = slice(512 * lo, 512 * hi)
@@ -423,7 +419,7 @@ def tile_spectral_tikhonov_imaging_s8_kernel(
         turn_and_empty_meas(2, 2, "S")
         square_sums(1, 1)
 
-        image_half(0, 0, 0, "VS")
+        image_half(0, 0, 0, "VS", (0, 1))
         invert(1, 1)
         quantize_meas(2)
         image_half(0, 0, 1, "SS")
@@ -435,6 +431,7 @@ def tile_spectral_tikhonov_imaging_s8_kernel(
         weights(2, 1)
         group_h(1, 0, "S")
         weigh(2, 0)
+        scale_basis(0)
         quantize_h_modes(1)
         project(2, 1)
         image_half(0, 1, 0, "SS")
@@ -451,41 +448,42 @@ def tile_spectral_tikhonov_imaging_s8_kernel(
         weights(3, 0)
         image_half(1, 0, 0, "SS")
         quantize_h_modes(2)
-        scale_basis(0)
+        scale_basis(1)
         image_half(1, 0, 1, "SS")
         project(3, 0)
+        split_basis(0, "S")
         weights(3, 1)
-        scale_basis(1)
-        split_basis(0)
+        split_basis(1, "V")
+        scale_basis(2)
         weigh(3, 0)
         image_half(1, 1, 0, "SS")
-        split_basis(1)
+        split_basis(2, "S")
         project(3, 1)
-        scale_basis(2)
+        scale_basis(3)
         image_half(1, 1, 1, "SS")
         weigh(3, 1)
 
-        turn_h(0, "SS")
+        turn_h(0, 0, "S")
+        turn_h(0, 1, "S")
         group_h(3, 0, "V")
-        split_basis(2)
+        split_basis(3, "V")
         group_h(3, 1, "V")
-        scale_basis(3)
         image_half(2, 0, 0, "SS")
         quantize_h_modes(3)
         image_half(2, 0, 1, "SS")
-        split_basis(3)
-        quantize_h_frames(0, 0, 2)
+        turn_basis("VV")
         image_half(2, 1, 0, "SS")
-        image_half(2, 1, 1, "VV")
-        turn_basis("SV")
-        image_half(3, 0, 0, "SS")
         quantize_basis()
-        image_half(3, 0, 1, "VS")
-        turn_h(1, "VS")
+        image_half(2, 1, 1, "SS")
+        quantize_h_frames(0, 0, 2)
+        image_half(3, 0, 0, "SS")
+        turn_h(1, 0, "V")
         quantize_h_frames(1, 0, 1)
+        image_half(3, 0, 1, "SS", (0, 1))
+        turn_h(1, 1, "V")
         quantize_h_frames(1, 1, 2)
-        image_half(3, 1, 0, "SS")
-        image_half(3, 1, 1, "VS")
+        image_half(3, 1, 0, "SS", (0, 1))
+        image_half(3, 1, 1, "SS", (0, 1))
 
         for r in range(R // 128):
             comps_rows(r, "VS", store_by_bank=(r == R // 128 - 1))

@@ -24,9 +24,9 @@ PF = F // 512
 BANKS = 8
 ROOT_ROW = 124
 US_PARTS = 64
-H_PARTS = 32
+H_PARTS = 64
 US_SHARE = 24
-H_SHARE = 20
+H_SHARE = 40
 OUT_BUFS = 7
 WEIGHT_BUFS = 6
 
@@ -155,7 +155,7 @@ def tile_spectral_tikhonov_imaging_s8_kernel(
                     )
 
         def invert(un, j):
-            for th in (1, 0):
+            for th in (0, 1):
                 tiles["weight", un, j, th] = work.tile([128, 2, 128, 2], F32, name="weight", bufs=WEIGHT_BUFS)
                 nc.scalar.activation(
                     out=tiles["weight", un, j, th][:], in_=tiles["square", th][:].rearrange("q i e r -> q i r e"), func=RSQRT
@@ -240,7 +240,7 @@ def tile_spectral_tikhonov_imaging_s8_kernel(
         def weigh(un, j):
             if j == 0:
                 tiles["h", un] = keep.tile([128, PM * 4, 256], BF16, name="h%d" % un)
-            for th in (1, 0):
+            for th in (0, 1):
                 places = slice(4 * j + 2 * th, 4 * j + 2 * th + 2)
                 weight = tiles["weight", un, j, th][:].rearrange("q i r e -> q i (r e)")
                 nc.vector.tensor_tensor(out=tiles["h", un][:, places, :], in0=tiles["c", un, j, th][:], in1=weight, op=MULT)
@@ -249,8 +249,8 @@ def tile_spectral_tikhonov_imaging_s8_kernel(
         def group_h(un, j, eng, lo=0, hi=H_PARTS):
             if ("h_modes", un) not in tiles:
                 tiles["h_modes", un] = work.tile([128, PM * 1024], BF16, name="h_modes", align_bytes=64)
-            dst = tiles["h_modes", un][:, 1024 * j : 1024 * j + 1024].rearrange("q (e a b t) -> q a e b t", e=2, b=4, t=4)
-            src = tiles["h", un][:, 4 * j : 4 * j + 4, :].rearrange("q t (a b e) -> q a e b t", b=4, e=2)
+            dst = tiles["h_modes", un][:, 1024 * j : 1024 * j + 1024].rearrange("q (e a b t) -> q a t b e", e=2, b=2, t=4)
+            src = tiles["h", un][:, 4 * j : 4 * j + 4, :].rearrange("q t (a b e) -> q a t b e", b=2, e=2)
             copy_on[eng](out=dst[:, lo:hi], in_=src[:, lo:hi])
 
         def quantize_h_modes(un):
@@ -262,7 +262,7 @@ def tile_spectral_tikhonov_imaging_s8_kernel(
 
         image_v = image.rearrange("(g p t) n -> g t p n", g=PF, p=128)
 
-        def image_half(un, e, half, engs, order=(1, 0)):
+        def image_half(un, e, half, engs, order=(0, 1)):
             for i in range(2):
                 n = 2 * half + i
                 bank = take_bank(("image", i), [128, 512])
@@ -305,7 +305,7 @@ def tile_spectral_tikhonov_imaging_s8_kernel(
                             src = tiles["basis_split", 2 * half + i][:, w, 128 * g : 128 * g + 128]
                             nc.tensor.transpose(bank[:, w, i, :], src, ident[:])
             for half in range(2):
-                for g in (1, 0):
+                for g in (0, 1):
                     first = 2048 * g + 1024 * half
                     dst = tiles["basis_k"][:, first : first + 1024].bitcast(F32).rearrange("p (c w) -> p c w", w=2)
                     copy_on[engs[half]](out=dst, in_=tiles["basis_turn", half, g][:].rearrange("p w i n -> p (i n) w"))
@@ -326,7 +326,7 @@ def tile_spectral_tikhonov_imaging_s8_kernel(
                     words = tiles["h", 2 * g + u][:].bitcast(F32)
                     for i in range(2):
                         nc.tensor.transpose(bank[:, u, i, :], words[:, 4 * j + 2 * th + i, :], ident[:])
-            for th in (1, 0):
+            for th in (0, 1):
                 first = 2048 * j + 1024 * th
                 dst = tiles["h_frames", g][:, first : first + 1024].bitcast(F32).rearrange("p (c u) -> p c u", u=2)
                 copy_on[eng](out=dst, in_=tiles["h_turn", th][:].rearrange("p u i q -> p (i q) u"))
@@ -419,7 +419,7 @@ def tile_spectral_tikhonov_imaging_s8_kernel(
         turn_and_empty_meas(2, 2, "S")
         square_sums(1, 1)
 
-        image_half(0, 0, 0, "VS", (0, 1))
+        image_half(0, 0, 0, "VS")
         invert(1, 1)
         quantize_meas(2)
         image_half(0, 0, 1, "SS")
@@ -439,7 +439,7 @@ def tile_spectral_tikhonov_imaging_s8_kernel(
         weigh(2, 1)
         for g in range(PD):
             turn_meas(3, g)
-        for g in (1, 0, 2):
+        for g in range(PD):
             empty_meas(3, g, "S")
         image_half(0, 1, 1, "VV")
         quantize_meas(3)
@@ -479,11 +479,11 @@ def tile_spectral_tikhonov_imaging_s8_kernel(
         image_half(3, 0, 0, "SS")
         turn_h(1, 0, "V")
         quantize_h_frames(1, 0, 1)
-        image_half(3, 0, 1, "SS", (0, 1))
+        image_half(3, 0, 1, "SS")
         turn_h(1, 1, "V")
         quantize_h_frames(1, 1, 2)
-        image_half(3, 1, 0, "SS", (0, 1))
-        image_half(3, 1, 1, "SS", (0, 1))
+        image_half(3, 1, 0, "SS")
+        image_half(3, 1, 1, "SS")
 
         for r in range(R // 128):
             comps_rows(r, "VS", store_by_bank=(r == R // 128 - 1))

@@ -14,9 +14,10 @@ I32 = mybir.dt.int32
 E4M3 = mybir.dt.float8_e4m3fn
 FP8X4 = mybir.dt.float8_e4m3fn_x4
 FP4X4 = mybir.dt.float4_e2m1fn_x4
-RSQRT = mybir.ActivationFunctionType.Abs_reciprocal_sqrt
+LN = mybir.ActivationFunctionType.Ln
+SIGMOID = mybir.ActivationFunctionType.Sigmoid
 MULT = mybir.AluOpType.mult
-SUB = mybir.AluOpType.subtract
+ADD = mybir.AluOpType.add
 
 PD = D // 512
 PM = M // 512
@@ -28,7 +29,8 @@ H_PARTS = 64
 US_SHARE = 24
 H_SHARE = 40
 OUT_BUFS = 7
-WEIGHT_BUFS = 6
+WEIGHT_BUFS = 4
+TINY = 1e-30
 
 
 def tile_spectral_tikhonov_imaging_s8_kernel(
@@ -60,16 +62,16 @@ def tile_spectral_tikhonov_imaging_s8_kernel(
 
         root_rows = keep.tile([128, 512], BF16, name="root_rows")
         nc.vector.memset(root_rows[0:ROOT_ROW, :], 0.0)
-        factors = keep.tile([128, 2, 8, 128], BF16, name="factors")
-        nc.vector.memset(factors[:], 0.0)
+        root_rows_zero = keep.tile([128, 1], F32, name="zero")
+        nc.vector.memset(root_rows_zero[:], 0.0)
         vt_scale = keep.tile([128, PM, P], U8, name="vt_scale", align_bytes=64)
         nc.vector.memset(vt_scale[:].bitcast(I32), 0)
         ident = keep.tile([128, 128], F32, name="ident")
         make_identity(nc, ident[:])
         ident_b = keep.tile([128, 128], BF16, name="ident_b")
         nc.vector.tensor_copy(out=ident_b[:], in_=ident[:])
-        nc.scalar.activation(out=factors[:, 1, :, 0:2], in_=factors[:, 1, :, 8:10], func=RSQRT, bias=1.0)
-        nc.scalar.activation(out=factors[:, 0, :, 4:8], in_=factors[:, 0, :, 8:12], func=RSQRT, bias=1.0)
+        tiny = keep.tile([128, 1], F32, name="tiny")
+        nc.vector.tensor_scalar(out=tiny[:], in0=root_rows_zero[:], scalar1=TINY, scalar2=None, op0=ADD)
 
         meas_v = meas.rearrange("(g p t) d -> g p t d", g=PF, p=128)
         us_v = us.rearrange("(g p k) m -> g p k m", p=128, k=4)
@@ -91,6 +93,7 @@ def tile_spectral_tikhonov_imaging_s8_kernel(
         load_us(1)
         load_us(2)
         load_meas(2)
+        load_meas(3)
         for quad in range(4):
             nc.sync.dma_start(
                 out=vt_scale[32 * quad : 32 * quad + 4, :, :].bitcast(I32),
@@ -98,73 +101,59 @@ def tile_spectral_tikhonov_imaging_s8_kernel(
             )
         vt = keep.tile([128, PM, 2 * P], U8, name="vt", align_bytes=64)
         nc.sync.dma_start(out=vt[:], in_=vt_words.rearrange("g p n -> p g n"))
-        load_meas(3)
         basis_raw = keep.tile([128, 4, F], U8, name="basis_raw")
         nc.sync.dma_start(out=basis_raw[:], in_=basis_bytes.rearrange("(r p) f -> p r f", p=128))
         basis_wide_scale = keep.tile([128, F], F32, name="basis_wide_scale")
         nc.sync.dma_start(out=basis_wide_scale[:], in_=basis_scale.rearrange("o k -> (o k)").partition_broadcast(128))
 
-        roots = keep.tile([128, 2, 8], BF16, name="roots")
-        squares = keep.tile([128, 2, 8], F32, name="squares")
-        fourth = keep.tile([128, 8], F32, name="fourth")
-        rest = keep.tile([128, 8], F32, name="rest")
-        rows = keep.tile([128, 2, 8, 128], BF16, name="rows")
+        square = keep.tile([128, PM, 4], F32, name="square")
+        log_square = keep.tile([128, PM * 4], F32, name="log_square")
+        inverse = keep.tile([128, PM * 4], F32, name="inverse")
+        log_lam = keep.tile([128, PF, 2, 256], F32, name="log_lam")
 
-        def make_factors():
-            bank = take_bank("roots", [128, 4, 4])
+        def spread_roots():
+            bank = take_bank("sigma", [128, 4, 2])
             for t in range(4):
                 nc.tensor.matmul(
-                    out=bank[:, t, :], lhsT=root_rows[:, t:512:4], rhs=ident_b[:, ROOT_ROW:128], start=True, stop=True
+                    out=bank[:, t, :], lhsT=root_rows[:, t:512:4], rhs=ident_b[:, ROOT_ROW + 2 : 128], start=True, stop=True
                 )
-            nc.vector.tensor_copy(
-                out=roots[:].rearrange("q v (g t) -> q v g t", t=4), in_=bank[:].rearrange("q t (v g) -> q v g t", v=2)
-            )
-            give_bank("roots")
-            lam_side, sigma_side = factors[:, 0], factors[:, 1]
-            nc.vector.tensor_tensor(out=squares[:], in0=roots[:], in1=roots[:], op=MULT)
-            nc.vector.tensor_copy(out=lam_side[:, :, 2:4], in_=roots[:, 0, :].unsqueeze(2).to_broadcast([128, 8, 2]))
-            nc.vector.tensor_tensor(out=fourth[:], in0=squares[:, 1, :], in1=squares[:, 1, :], op=MULT)
-            nc.vector.tensor_copy(out=lam_side[:, :, 0], in_=squares[:, 0, :])
-            nc.vector.tensor_scalar(out=sigma_side[:, :, 2], in0=squares[:, 1, :], scalar1=2.0, scalar2=None, op0=MULT)
-            nc.vector.tensor_copy(out=sigma_side[:, :, 4], in_=fourth[:])
-            nc.vector.tensor_tensor(out=lam_side[:, :, 1], in0=squares[:, 0, :], in1=lam_side[:, :, 0], op=SUB)
-            nc.vector.scalar_tensor_tensor(
-                out=sigma_side[:, :, 3], in0=squares[:, 1, :], scalar=2.0, in1=sigma_side[:, :, 2], op0=MULT, op1=SUB
-            )
-            nc.vector.tensor_tensor(out=rest[:], in0=fourth[:], in1=sigma_side[:, :, 4], op=SUB)
-            nc.vector.tensor_tensor(out=sigma_side[:, :, 5], in0=fourth[:], in1=sigma_side[:, :, 4], op=SUB)
-            nc.vector.tensor_tensor(out=sigma_side[:, :, 6], in0=rest[:], in1=sigma_side[:, :, 5], op=SUB)
+            for g in range(PF):
+                bank = take_bank(("lam", g), [128, 512])
+                row = ident_b[:, ROOT_ROW + g : ROOT_ROW + g + 1].to_broadcast([128, 128])
+                nc.tensor.matmul(out=bank[:], lhsT=row, rhs=root_rows[:], start=True, stop=True)
 
-        def turn_factors(side):
-            bank = take_bank("factors", [128, 8, 128], BF16)
-            for block in range(8):
-                nc.tensor.matmul(out=bank[:, block, :], lhsT=factors[:, side, block, :], rhs=ident_b[:], start=True, stop=True)
-            nc.vector.tensor_copy(out=rows[:, side], in_=bank[:])
-            give_bank("factors")
-
-        def square_sums(un, j):
-            for th in range(2):
-                bank = take_bank(("square", th), [128, 2, 2, 128])
-                for i in range(2):
-                    nc.tensor.matmul(
-                        out=bank[:, i].rearrange("q e r -> q (e r)"),
-                        lhsT=rows[:, 1, 4 * j + 2 * th + i, :],
-                        rhs=rows[:, 0, 2 * un : 2 * un + 2, :].rearrange("k e r -> k (e r)"),
-                        start=True,
-                        stop=True,
-                    )
-
-        def invert(un, j):
-            for th in (0, 1):
-                tiles["weight", un, j, th] = work.tile([128, 2, 128, 2], F32, name="weight", bufs=WEIGHT_BUFS)
+        def logarithms():
+            root = keep.tile([128, PM, 4], F32, name="root")
+            nc.vector.tensor_copy(out=root[:], in_=tiles["sigma"][:].rearrange("q t j -> q j t"))
+            give_bank("sigma")
+            nc.vector.tensor_tensor(out=square[:], in0=root[:], in1=root[:], op=MULT)
+            for g in range(PF):
                 nc.scalar.activation(
-                    out=tiles["weight", un, j, th][:], in_=tiles["square", th][:].rearrange("q i e r -> q i r e"), func=RSQRT
+                    out=log_lam[:, g].rearrange("p u (r e) -> p u r e", e=2),
+                    in_=tiles["lam", g][:].rearrange("p (r u e) -> p u r e", u=2, e=2),
+                    func=LN,
+                    bias=tiny[:],
                 )
-                give_bank(("square", th))
+                give_bank(("lam", g))
+            nc.scalar.activation(out=log_square[:], in_=square[:].rearrange("q j t -> q (j t)"), func=LN, bias=tiny[:])
+
+        def invert_squares():
+            shifted = keep.tile([128, PM * 4], F32, name="shifted")
+            nc.vector.tensor_scalar(
+                out=shifted[:], in0=square[:].rearrange("q j t -> q (j t)"), scalar1=TINY, scalar2=None, op0=ADD
+            )
+            nc.vector.reciprocal(out=inverse[:], in_=shifted[:])
 
         def weights(un, j):
-            square_sums(un, j)
-            invert(un, j)
+            tiles["weight", un, j] = work.tile([128, 4, 256], F32, name="weight", bufs=WEIGHT_BUFS)
+            for t in range(4):
+                nc.scalar.activation(
+                    out=tiles["weight", un, j][:, t, :],
+                    in_=log_lam[:, un // 2, un % 2, :],
+                    func=SIGMOID,
+                    scale=-1.0,
+                    bias=log_square[:, 4 * j + t : 4 * j + t + 1],
+                )
 
         def split_meas(un):
             tiles["split", un] = work.tile([128, 2, 2, D // 4], F32, name="split", tag="raw_meas", bufs=4)
@@ -194,8 +183,8 @@ def tile_spectral_tikhonov_imaging_s8_kernel(
             turn_meas(un, g)
             empty_meas(un, g, eng)
 
-        def quantize_meas(un):
-            for lo, hi in ((0, 2), (2, 3)):
+        def quantize_meas(un, spans=((0, 2), (2, 3))):
+            for lo, hi in spans:
                 nc.vector.quantize_mx(
                     out=tiles["meas_codes", un][:, lo:hi, :].rearrange("p g c -> p (g c)").bitcast(FP8X4),
                     scales=tiles["meas_scales", un][:, lo:hi, :].rearrange("p g c -> p (g c)"),
@@ -241,9 +230,16 @@ def tile_spectral_tikhonov_imaging_s8_kernel(
             if j == 0:
                 tiles["h", un] = keep.tile([128, PM * 4, 256], BF16, name="h%d" % un)
             for th in (0, 1):
-                places = slice(4 * j + 2 * th, 4 * j + 2 * th + 2)
-                weight = tiles["weight", un, j, th][:].rearrange("q i r e -> q i (r e)")
-                nc.vector.tensor_tensor(out=tiles["h", un][:, places, :], in0=tiles["c", un, j, th][:], in1=weight, op=MULT)
+                for i in range(2):
+                    place = 4 * j + 2 * th + i
+                    nc.vector.scalar_tensor_tensor(
+                        out=tiles["h", un][:, place, :],
+                        in0=tiles["c", un, j, th][:, i, :],
+                        scalar=inverse[:, place : place + 1],
+                        in1=tiles["weight", un, j][:, 2 * th + i, :],
+                        op0=MULT,
+                        op1=MULT,
+                    )
                 give_bank(("c", un, j, th))
 
         def group_h(un, j, eng, lo=0, hi=H_PARTS):
@@ -253,11 +249,15 @@ def tile_spectral_tikhonov_imaging_s8_kernel(
             src = tiles["h", un][:, 4 * j : 4 * j + 4, :].rearrange("q t (a b e) -> q a t b e", b=2, e=2)
             copy_on[eng](out=dst[:, lo:hi], in_=src[:, lo:hi])
 
-        def quantize_h_modes(un):
-            tiles["h_codes", un] = keep.tile([128, PM * 256], U32, name="h_codes%d" % un, align_bytes=64)
-            tiles["h_scales", un] = keep.tile([128, PM * 256], U8, name="h_scales%d" % un, align_bytes=64)
+        def quantize_h_modes(un, lo=0, hi=PM):
+            if lo == 0:
+                tiles["h_codes", un] = keep.tile([128, PM * 256], U32, name="h_codes%d" % un, align_bytes=64)
+                tiles["h_scales", un] = keep.tile([128, PM * 256], U8, name="h_scales%d" % un, align_bytes=64)
+            cols = slice(256 * lo, 256 * hi)
             nc.vector.quantize_mx(
-                out=tiles["h_codes", un][:].bitcast(FP8X4), scales=tiles["h_scales", un][:], in_=tiles["h_modes", un][:]
+                out=tiles["h_codes", un][:, cols].bitcast(FP8X4),
+                scales=tiles["h_scales", un][:, cols],
+                in_=tiles["h_modes", un][:, 1024 * lo : 1024 * hi],
             )
 
         image_v = image.rearrange("(g p t) n -> g t p n", g=PF, p=128)
@@ -369,121 +369,129 @@ def tile_spectral_tikhonov_imaging_s8_kernel(
             if not store_by_bank:
                 nc.sync.dma_start(out=rows_out, in_=result[:])
 
-        group_us(1, 0, "S")
-        make_factors()
+        spread_roots()
+        logarithms()
+        invert_squares()
         group_us(0, 0, "V")
-        turn_factors(0)
-        quantize_us(0, 0)
-        turn_factors(1)
-        for g in range(PD):
-            turn_and_empty_meas(0, g, "S")
-        quantize_us(1, 0)
-        for g in range(PD):
-            turn_and_empty_meas(1, g, "S")
+        group_us(1, 0, "V")
         weights(0, 0)
+        quantize_us(0, 0)
+        for g in range(PD):
+            turn_meas(0, g)
+        empty_meas(0, 0, "S")
+        quantize_us(1, 0)
+        empty_meas(0, 1, "S")
+        empty_meas(0, 2, "V")
+        weights(0, 1)
+        for g in range(PD):
+            turn_meas(1, g)
         quantize_meas(0)
-        group_us(0, 1, "V")
+        empty_meas(1, 0, "S")
+        empty_meas(1, 1, "V")
+        empty_meas(1, 2, "S")
+        group_us(0, 1, "V", 0, 48)
+        group_us(0, 1, "S", 48, 64)
         project_pass(0, 0, 0)
         project_pass(0, 1, 0)
-        group_us(1, 1, "S")
         quantize_meas(1)
+        group_us(1, 1, "S", 0, 32)
         quantize_us(0, 1)
+        group_us(1, 1, "V", 32, 64)
         project_pass(1, 0, 0)
+        project_pass(1, 1, 0)
+        group_us(0, 2, "S", 0, 32)
         project_pass(0, 0, 1)
-        square_sums(0, 1)
         project_pass(1, 0, 1)
-        group_us(0, 2, "V")
-        group_us(1, 2, "V", 0, US_SHARE)
-        group_us(1, 2, "S", US_SHARE, US_PARTS)
-        invert(0, 1)
+        group_us(0, 2, "V", 32, 48)
         quantize_us(1, 1)
-        quantize_us(0, 2)
+        group_us(0, 2, "V", 48, 64)
+        group_us(1, 2, "S", 0, 48)
         project_pass(0, 1, 1)
+        project_pass(1, 1, 1)
+        group_us(1, 2, "V", 48, 64)
+        quantize_us(0, 2)
         project_pass(0, 0, 2)
-        quantize_us(1, 2)
-        project_pass(0, 1, 2)
         project_pass(1, 0, 2)
-
+        quantize_us(1, 2)
+        weights(1, 0)
         weigh(0, 0)
-        project(1, 1)
+        project_pass(0, 1, 2)
         group_h(0, 0, "S")
-        square_sums(1, 0)
         weigh(0, 1)
-        group_h(0, 1, "V", 0, H_SHARE)
-        group_h(0, 1, "S", H_SHARE, H_PARTS)
-        invert(1, 0)
-        quantize_h_modes(0)
-        turn_and_empty_meas(2, 0, "V")
-        turn_and_empty_meas(2, 1, "S")
+        turn_meas(2, 0)
+        turn_meas(2, 1)
+        project_pass(1, 1, 2)
+        turn_meas(2, 2)
+        group_h(0, 1, "V", 0, 40)
+        group_h(0, 1, "S", 40, 64)
+        quantize_h_modes(0, 0, 1)
+        quantize_h_modes(0, 1, 2)
+        empty_meas(2, 0, "S")
         weigh(1, 0)
-        turn_and_empty_meas(2, 2, "S")
-        square_sums(1, 1)
-
+        empty_meas(2, 1, "S")
+        empty_meas(2, 2, "S")
+        weights(1, 1)
         image_half(0, 0, 0, "VS")
-        invert(1, 1)
         quantize_meas(2)
-        image_half(0, 0, 1, "SS")
         weigh(1, 1)
+        image_half(0, 0, 1, "SS")
+        group_h(1, 0, "V")
         weights(2, 0)
-        group_h(1, 1, "V")
-        split_meas(3)
-        project(2, 0)
-        weights(2, 1)
-        group_h(1, 0, "S")
-        weigh(2, 0)
-        scale_basis(0)
-        quantize_h_modes(1)
-        project(2, 1)
         image_half(0, 1, 0, "SS")
-        group_h(2, 0, "V")
-        weigh(2, 1)
+        group_h(1, 1, "V")
+        project(2, 0)
+        split_meas(3)
+        quantize_h_modes(1)
+        weights(2, 1)
+        weigh(2, 0)
+        image_half(0, 1, 1, "SS")
+        project(2, 1)
+        scale_basis(0)
         for g in range(PD):
             turn_meas(3, g)
+        weigh(2, 1)
         for g in range(PD):
             empty_meas(3, g, "S")
-        image_half(0, 1, 1, "VV")
+        split_basis(0, "V")
+        image_half(1, 0, 0, "VS")
         quantize_meas(3)
-        group_h(2, 1, "V")
-
         weights(3, 0)
-        image_half(1, 0, 0, "SS")
-        quantize_h_modes(2)
-        scale_basis(1)
+        group_h(2, 0, "V")
         image_half(1, 0, 1, "SS")
+        group_h(2, 1, "V")
+        image_half(1, 1, 0, "SS")
+        scale_basis(1)
         project(3, 0)
-        split_basis(0, "S")
+        quantize_h_modes(2)
         weights(3, 1)
+        weigh(3, 0)
+        image_half(1, 1, 1, "SS")
+        project(3, 1)
         split_basis(1, "V")
         scale_basis(2)
-        weigh(3, 0)
-        image_half(1, 1, 0, "SS")
-        split_basis(2, "S")
-        project(3, 1)
-        scale_basis(3)
-        image_half(1, 1, 1, "SS")
-        weigh(3, 1)
-
         turn_h(0, 0, "S")
         turn_h(0, 1, "S")
+        weigh(3, 1)
+        split_basis(2, "V")
+        scale_basis(3)
+        image_half(2, 0, 0, "SS")
         group_h(3, 0, "V")
         split_basis(3, "V")
-        group_h(3, 1, "V")
-        image_half(2, 0, 0, "SS")
-        quantize_h_modes(3)
         image_half(2, 0, 1, "SS")
-        turn_basis("VV")
-        image_half(2, 1, 0, "SS")
-        quantize_basis()
-        image_half(2, 1, 1, "SS")
+        group_h(3, 1, "V")
         quantize_h_frames(0, 0, 2)
-        image_half(3, 0, 0, "SS")
+        image_half(2, 1, 0, "SS")
+        turn_basis("VS")
+        quantize_h_modes(3)
+        image_half(2, 1, 1, "SS")
+        quantize_basis()
+        image_half(3, 0, 0, "VS")
         turn_h(1, 0, "V")
-        quantize_h_frames(1, 0, 1)
         image_half(3, 0, 1, "SS")
+        quantize_h_frames(1, 0, 1)
         turn_h(1, 1, "V")
-        quantize_h_frames(1, 1, 2)
         image_half(3, 1, 0, "SS")
-        image_half(3, 1, 1, "SS")
-
+        quantize_h_frames(1, 1, 2)
+        image_half(3, 1, 1, "SV")
         for r in range(R // 128):
-            comps_rows(r, "VS", store_by_bank=(r == R // 128 - 1))
+            comps_rows(r, "SV", store_by_bank=(r == R // 128 - 1))

@@ -18,19 +18,18 @@ LN = mybir.ActivationFunctionType.Ln
 SIGMOID = mybir.ActivationFunctionType.Sigmoid
 MULT = mybir.AluOpType.mult
 ADD = mybir.AluOpType.add
+MAX = mybir.AluOpType.max
 
 PD = D // 512
 PM = M // 512
 PF = F // 512
 BANKS = 8
 ROOT_ROW = 124
-US_PARTS = 64
-H_PARTS = 64
-US_SHARE = 24
-H_SHARE = 40
+PARTS = 64
 OUT_BUFS = 7
 WEIGHT_BUFS = 4
-TINY = 1e-30
+BASIS_BUFS = 2
+TINY = 1e-18
 
 
 def tile_spectral_tikhonov_imaging_s8_kernel(
@@ -62,16 +61,16 @@ def tile_spectral_tikhonov_imaging_s8_kernel(
 
         root_rows = keep.tile([128, 512], BF16, name="root_rows")
         nc.vector.memset(root_rows[0:ROOT_ROW, :], 0.0)
-        root_rows_zero = keep.tile([128, 1], F32, name="zero")
-        nc.vector.memset(root_rows_zero[:], 0.0)
+        zero = keep.tile([128, 1], F32, name="zero")
+        nc.vector.memset(zero[:], 0.0)
         vt_scale = keep.tile([128, PM, P], U8, name="vt_scale", align_bytes=64)
         nc.vector.memset(vt_scale[:].bitcast(I32), 0)
         ident = keep.tile([128, 128], F32, name="ident")
         make_identity(nc, ident[:])
+        tiny = keep.tile([128, 1], F32, name="tiny")
+        nc.vector.tensor_scalar(out=tiny[:], in0=zero[:], scalar1=TINY, scalar2=None, op0=ADD)
         ident_b = keep.tile([128, 128], BF16, name="ident_b")
         nc.vector.tensor_copy(out=ident_b[:], in_=ident[:])
-        tiny = keep.tile([128, 1], F32, name="tiny")
-        nc.vector.tensor_scalar(out=tiny[:], in0=root_rows_zero[:], scalar1=TINY, scalar2=None, op0=ADD)
 
         meas_v = meas.rearrange("(g p t) d -> g p t d", g=PF, p=128)
         us_v = us.rearrange("(g p k) m -> g p k m", p=128, k=4)
@@ -106,54 +105,44 @@ def tile_spectral_tikhonov_imaging_s8_kernel(
         basis_wide_scale = keep.tile([128, F], F32, name="basis_wide_scale")
         nc.sync.dma_start(out=basis_wide_scale[:], in_=basis_scale.rearrange("o k -> (o k)").partition_broadcast(128))
 
-        square = keep.tile([128, PM, 4], F32, name="square")
-        log_square = keep.tile([128, PM * 4], F32, name="log_square")
-        inverse = keep.tile([128, PM * 4], F32, name="inverse")
-        log_lam = keep.tile([128, PF, 2, 256], F32, name="log_lam")
+        log_sigma = keep.tile([128, M], F32, name="log_sigma")
+        log_lam = keep.tile([128, PF, 4], F32, name="log_lam")
+        inverse = keep.tile([128, PF * 4], F32, name="inverse")
 
         def spread_roots():
-            bank = take_bank("sigma", [128, 4, 2])
+            size = keep.tile([128, 512], BF16, name="size")
+            nc.vector.scalar_tensor_tensor(out=size[:], in0=root_rows[:], scalar=-1.0, in1=root_rows[:], op0=MULT, op1=MAX)
+            bank = take_bank("lam", [128, 4, 2])
             for t in range(4):
                 nc.tensor.matmul(
-                    out=bank[:, t, :], lhsT=root_rows[:, t:512:4], rhs=ident_b[:, ROOT_ROW + 2 : 128], start=True, stop=True
+                    out=bank[:, t, :], lhsT=root_rows[:, t:512:4], rhs=ident_b[:, ROOT_ROW : ROOT_ROW + 2], start=True, stop=True
                 )
-            for g in range(PF):
-                bank = take_bank(("lam", g), [128, 512])
-                row = ident_b[:, ROOT_ROW + g : ROOT_ROW + g + 1].to_broadcast([128, 128])
-                nc.tensor.matmul(out=bank[:], lhsT=row, rhs=root_rows[:], start=True, stop=True)
+            for j in range(PM):
+                bank = take_bank(("sigma", j), [128, 512])
+                row = ident_b[:, ROOT_ROW + 2 + j : ROOT_ROW + 3 + j].to_broadcast([128, 128])
+                nc.tensor.matmul(out=bank[:], lhsT=row, rhs=size[:], start=True, stop=True)
 
         def logarithms():
-            root = keep.tile([128, PM, 4], F32, name="root")
-            nc.vector.tensor_copy(out=root[:], in_=tiles["sigma"][:].rearrange("q t j -> q j t"))
-            give_bank("sigma")
-            nc.vector.tensor_tensor(out=square[:], in0=root[:], in1=root[:], op=MULT)
-            for g in range(PF):
+            lam_columns = tiles["lam"][:].rearrange("p t g -> p g t")
+            nc.scalar.activation(out=log_lam[:], in_=lam_columns, func=LN, bias=tiny[:])
+            shifted = keep.tile([128, PF, 4], F32, name="shifted")
+            nc.vector.tensor_scalar(out=shifted[:], in0=lam_columns, scalar1=TINY, scalar2=None, op0=ADD)
+            give_bank("lam")
+            nc.vector.reciprocal(out=inverse[:], in_=shifted[:].rearrange("p g t -> p (g t)"))
+            for j in range(PM):
                 nc.scalar.activation(
-                    out=log_lam[:, g].rearrange("p u (r e) -> p u r e", e=2),
-                    in_=tiles["lam", g][:].rearrange("p (r u e) -> p u r e", u=2, e=2),
+                    out=log_sigma[:, 512 * j : 512 * j + 512].rearrange("p (w q e) -> p w q e", w=2, e=2),
+                    in_=tiles["sigma", j][:].rearrange("p (q w e) -> p w q e", w=2, e=2),
                     func=LN,
                     bias=tiny[:],
                 )
-                give_bank(("lam", g))
-            nc.scalar.activation(out=log_square[:], in_=square[:].rearrange("q j t -> q (j t)"), func=LN, bias=tiny[:])
+                give_bank(("sigma", j))
 
-        def invert_squares():
-            shifted = keep.tile([128, PM * 4], F32, name="shifted")
-            nc.vector.tensor_scalar(
-                out=shifted[:], in0=square[:].rearrange("q j t -> q (j t)"), scalar1=TINY, scalar2=None, op0=ADD
+        def weights(s):
+            tiles["weight", s] = work.tile([128, M], F32, name="weight", bufs=WEIGHT_BUFS)
+            nc.scalar.activation(
+                out=tiles["weight", s][:], in_=log_sigma[:], func=SIGMOID, scale=-2.0, bias=log_lam[:, s // 4, s % 4 : s % 4 + 1]
             )
-            nc.vector.reciprocal(out=inverse[:], in_=shifted[:])
-
-        def weights(un, j):
-            tiles["weight", un, j] = work.tile([128, 4, 256], F32, name="weight", bufs=WEIGHT_BUFS)
-            for t in range(4):
-                nc.scalar.activation(
-                    out=tiles["weight", un, j][:, t, :],
-                    in_=log_lam[:, un // 2, un % 2, :],
-                    func=SIGMOID,
-                    scale=-1.0,
-                    bias=log_square[:, 4 * j + t : 4 * j + t + 1],
-                )
 
         def split_meas(un):
             tiles["split", un] = work.tile([128, 2, 2, D // 4], F32, name="split", tag="raw_meas", bufs=4)
@@ -165,7 +154,7 @@ def tile_spectral_tikhonov_imaging_s8_kernel(
                 tiles["meas_codes", un] = keep.tile([128, PD, 256], U32, name="meas_codes%d" % un, align_bytes=64)
                 tiles["meas_scales", un] = keep.tile([128, PD, 256], U8, name="meas_scales%d" % un, align_bytes=64)
                 tiles["meas_k", un] = work.tile([128, PD * 1024], BF16, name="meas_k", align_bytes=64)
-            bank = take_bank(("meas_turn", g), [128, 2, 2, 128])
+            bank = take_bank(("meas_turn", un, g), [128, 2, 2, 128])
             for e in range(2):
                 for w in range(2):
                     if ("split", un) in tiles:
@@ -175,16 +164,12 @@ def tile_spectral_tikhonov_imaging_s8_kernel(
                     nc.tensor.transpose(bank[:, e, w, :], src, ident[:])
 
         def empty_meas(un, g, eng):
-            dst = tiles["meas_k", un][:, 1024 * g : 1024 * g + 1024].bitcast(F32).rearrange("p (r e w) -> p r e w", e=2, w=2)
-            copy_on[eng](out=dst, in_=tiles["meas_turn", g][:].rearrange("p e w r -> p r e w"))
-            give_bank(("meas_turn", g))
+            dst = tiles["meas_k", un][:, 1024 * g : 1024 * g + 1024].bitcast(F32).rearrange("p (e r w) -> p e r w", e=2, w=2)
+            copy_on[eng](out=dst, in_=tiles["meas_turn", un, g][:].rearrange("p e w r -> p e r w"))
+            give_bank(("meas_turn", un, g))
 
-        def turn_and_empty_meas(un, g, eng):
-            turn_meas(un, g)
-            empty_meas(un, g, eng)
-
-        def quantize_meas(un, spans=((0, 2), (2, 3))):
-            for lo, hi in spans:
+        def quantize_meas(un):
+            for lo, hi in ((0, 2), (2, 3)):
                 nc.vector.quantize_mx(
                     out=tiles["meas_codes", un][:, lo:hi, :].rearrange("p g c -> p (g c)").bitcast(FP8X4),
                     scales=tiles["meas_scales", un][:, lo:hi, :].rearrange("p g c -> p (g c)"),
@@ -194,100 +179,105 @@ def tile_spectral_tikhonov_imaging_s8_kernel(
         us_codes = keep.tile([128, PD, M], U32, name="us_codes", align_bytes=64)
         us_scales = keep.tile([128, PD, M], U8, name="us_scales", align_bytes=64)
 
-        def group_us(j, g, eng, lo=0, hi=US_PARTS):
+        def group_us(j, g, eng, lo=0, hi=PARTS):
             if lo == 0:
                 tiles["us_k", j, g] = work.tile([128, 2048], BF16, name="us_k", align_bytes=64, bufs=3)
-            dst = tiles["us_k", j, g][:].rearrange("p (t a b k) -> p a t b k", t=4, b=2, k=4)
-            src = tiles["us", g][:, :, 512 * j : 512 * j + 512].rearrange("p k (a b t) -> p a t b k", b=2, t=4)
-            copy_on[eng](out=dst[:, lo:hi], in_=src[:, lo:hi])
+            dst = tiles["us_k", j, g][:].rearrange("p (w q e k) -> p q k w e", w=2, e=2, k=4)
+            src = tiles["us", g][:, :, 512 * j : 512 * j + 512].rearrange("p k (q w e) -> p q k w e", w=2, e=2)
+            copy_on[eng](out=dst[:, 2 * lo : 2 * hi], in_=src[:, 2 * lo : 2 * hi])
 
         def quantize_us(j, g):
             cols = slice(512 * j, 512 * j + 512)
             nc.vector.quantize_mx(out=us_codes[:, g, cols].bitcast(FP8X4), scales=us_scales[:, g, cols], in_=tiles["us_k", j, g][:])
 
-        def project_pass(un, j, g, halves=(0, 1)):
-            for th in halves:
-                if g == 0:
-                    take_bank(("c", un, j, th), [128, 2, 256])
-                for i in range(2):
-                    col = 512 * j + 128 * (2 * th + i)
-                    nc.tensor.matmul_mx(
-                        out=tiles["c", un, j, th][:, i, :],
-                        lhsT=us_codes[:, g, col : col + 128].bitcast(FP8X4),
-                        lhsT_scale=us_scales[:, g, col : col + 128],
-                        rhs=tiles["meas_codes", un][:, g, :].bitcast(FP8X4),
-                        rhs_scale=tiles["meas_scales", un][:, g, :],
-                        start=((g, i) == (0, 0)),
-                        stop=((g, i) == (PD - 1, 1)),
-                    )
+        def project_pass(s, j, g):
+            if g == 0:
+                take_bank(("c", s, j), [128, 512])
+            frames = slice(128 * (s % 2), 128 * (s % 2) + 128)
+            cols = slice(512 * j, 512 * j + 512)
+            nc.tensor.matmul_mx(
+                out=tiles["c", s, j][:],
+                lhsT=tiles["meas_codes", s // 2][:, g, frames].bitcast(FP8X4),
+                lhsT_scale=tiles["meas_scales", s // 2][:, g, frames],
+                rhs=us_codes[:, g, cols].bitcast(FP8X4),
+                rhs_scale=us_scales[:, g, cols],
+                start=(g == 0),
+                stop=(g == PD - 1),
+            )
 
-        def project(un, j):
-            for th in range(2):
+        def project(s, passes=range(PM)):
+            for j in passes:
                 for g in range(PD):
-                    project_pass(un, j, g, (th,))
+                    project_pass(s, j, g)
 
-        def weigh(un, j):
-            if j == 0:
-                tiles["h", un] = keep.tile([128, PM * 4, 256], BF16, name="h%d" % un)
-            for th in (0, 1):
-                for i in range(2):
-                    place = 4 * j + 2 * th + i
-                    nc.vector.scalar_tensor_tensor(
-                        out=tiles["h", un][:, place, :],
-                        in0=tiles["c", un, j, th][:, i, :],
-                        scalar=inverse[:, place : place + 1],
-                        in1=tiles["weight", un, j][:, 2 * th + i, :],
-                        op0=MULT,
-                        op1=MULT,
-                    )
-                give_bank(("c", un, j, th))
+        def weigh(s, j):
+            if ("h", s // 4) not in tiles:
+                tiles["h", s // 4] = keep.tile([128, 4, M], BF16, name="h%d" % (s // 4))
+            cols = slice(512 * j, 512 * j + 512)
+            nc.vector.scalar_tensor_tensor(
+                out=tiles["h", s // 4][:, s % 4, cols],
+                in0=tiles["c", s, j][:],
+                scalar=inverse[:, s : s + 1],
+                in1=tiles["weight", s][:, cols],
+                op0=MULT,
+                op1=MULT,
+            )
+            give_bank(("c", s, j))
 
-        def group_h(un, j, eng, lo=0, hi=H_PARTS):
-            if ("h_modes", un) not in tiles:
-                tiles["h_modes", un] = work.tile([128, PM * 1024], BF16, name="h_modes", align_bytes=64)
-            dst = tiles["h_modes", un][:, 1024 * j : 1024 * j + 1024].rearrange("q (e a b t) -> q a t b e", e=2, b=2, t=4)
-            src = tiles["h", un][:, 4 * j : 4 * j + 4, :].rearrange("q t (a b e) -> q a t b e", b=2, e=2)
-            copy_on[eng](out=dst[:, lo:hi], in_=src[:, lo:hi])
+        def turn_h(s):
+            bank = take_bank(("h_turn", s), [128, PM, 2, 128])
+            words = tiles["h", s // 4][:, s % 4, :].bitcast(F32)
+            for j in range(PM):
+                for w in range(2):
+                    first = 256 * j + 128 * w
+                    nc.tensor.transpose(bank[:, j, w, :], words[:, first : first + 128], ident[:])
 
-        def quantize_h_modes(un, lo=0, hi=PM):
+        def empty_h(s, eng):
+            if s % 2 == 0:
+                tiles["h_modes", s // 2] = work.tile([128, 2, 1024], BF16, name="h_modes", align_bytes=64)
+            dst = tiles["h_modes", s // 2][:, s % 2, :].bitcast(F32).rearrange("q (j r w) -> q j r w", j=PM, w=2)
+            copy_on[eng](out=dst, in_=tiles["h_turn", s][:].rearrange("q j w r -> q j r w"))
+            give_bank(("h_turn", s))
+
+        def quantize_h_modes(un, lo=0, hi=2):
             if lo == 0:
-                tiles["h_codes", un] = keep.tile([128, PM * 256], U32, name="h_codes%d" % un, align_bytes=64)
-                tiles["h_scales", un] = keep.tile([128, PM * 256], U8, name="h_scales%d" % un, align_bytes=64)
+                tiles["h_codes", un] = keep.tile([128, 512], U32, name="h_codes%d" % un, align_bytes=64)
+                tiles["h_scales", un] = keep.tile([128, 512], U8, name="h_scales%d" % un, align_bytes=64)
             cols = slice(256 * lo, 256 * hi)
             nc.vector.quantize_mx(
                 out=tiles["h_codes", un][:, cols].bitcast(FP8X4),
                 scales=tiles["h_scales", un][:, cols],
-                in_=tiles["h_modes", un][:, 1024 * lo : 1024 * hi],
+                in_=tiles["h_modes", un][:, lo:hi, :].rearrange("q e c -> q (e c)"),
             )
 
         image_v = image.rearrange("(g p t) n -> g t p n", g=PF, p=128)
 
-        def image_half(un, e, half, engs, order=(0, 1)):
+        def image_half(s, half, engs):
             for i in range(2):
                 n = 2 * half + i
                 bank = take_bank(("image", i), [128, 512])
                 for j in range(PM):
-                    cols = slice(256 * j + 128 * e, 256 * j + 128 * e + 128)
+                    first = 256 * (s % 2) + 128 * j
                     nc.tensor.matmul_mx(
                         out=bank[:],
-                        lhsT=tiles["h_codes", un][:, cols].bitcast(FP8X4),
-                        lhsT_scale=tiles["h_scales", un][:, cols],
+                        lhsT=tiles["h_codes", s // 2][:, first : first + 128].bitcast(FP8X4),
+                        lhsT_scale=tiles["h_scales", s // 2][:, first : first + 128],
                         rhs=vt[:, j, 1024 * n : 1024 * n + 1024].bitcast(FP4X4),
                         rhs_scale=vt_scale[:, j, 512 * n : 512 * n + 512],
                         start=(j == 0),
                         stop=(j == PM - 1),
                     )
             result = stage.tile([128, 1024], F32, name="result", tag="result")
-            for i in order:
+            for i in range(2):
                 copy_on[engs[i]](out=result[:, 512 * i : 512 * i + 512], in_=tiles["image", i][:])
                 give_bank(("image", i))
-            nc.sync.dma_start(out=image_v[un // 2, 2 * (un % 2) + e, :, 1024 * half : 1024 * half + 1024], in_=result[:])
+            nc.sync.dma_start(out=image_v[s // 4, s % 4, :, 1024 * half : 1024 * half + 1024], in_=result[:])
 
         basis_codes = keep.tile([128, PF * R], U32, name="basis_codes", align_bytes=64)
         basis_scales = keep.tile([128, PF * R], U8, name="basis_scales", align_bytes=64)
 
         def scale_basis(r):
-            tiles["basis", r] = work.tile([128, F], BF16, name="basis")
+            tiles["basis", r] = work.tile([128, F], BF16, name="basis", bufs=BASIS_BUFS)
             nc.vector.tensor_tensor(out=tiles["basis", r][:], in0=basis_raw[:, r, :].bitcast(E4M3), in1=basis_wide_scale[:], op=MULT)
 
         def split_basis(r, eng):
@@ -295,21 +285,25 @@ def tile_spectral_tikhonov_imaging_s8_kernel(
             words = tiles["basis", r][:].bitcast(F32)
             copy_on[eng](out=tiles["basis_split", r][:], in_=words.rearrange("n (c w) -> n w c", w=2))
 
-        def turn_basis(engs):
-            tiles["basis_k"] = work.tile([128, PF * 2048], BF16, name="basis_k", tag="wide", bufs=3, align_bytes=64)
-            for half in range(2):
-                for g in range(PF):
-                    bank = take_bank(("basis_turn", half, g), [128, 2, 2, 128])
-                    for i in range(2):
-                        for w in range(2):
+        def turn_basis(half):
+            if half == 0:
+                tiles["basis_k"] = work.tile([128, PF * 2048], BF16, name="basis_k", tag="wide", bufs=3, align_bytes=64)
+            for g in range(PF):
+                bank = take_bank(("basis_turn", half, g), [128, 2, 2, 128])
+                for i in range(2):
+                    for w in range(2):
+                        if ("basis_split", 2 * half + i) in tiles:
                             src = tiles["basis_split", 2 * half + i][:, w, 128 * g : 128 * g + 128]
-                            nc.tensor.transpose(bank[:, w, i, :], src, ident[:])
-            for half in range(2):
-                for g in (0, 1):
-                    first = 2048 * g + 1024 * half
-                    dst = tiles["basis_k"][:, first : first + 1024].bitcast(F32).rearrange("p (c w) -> p c w", w=2)
-                    copy_on[engs[half]](out=dst, in_=tiles["basis_turn", half, g][:].rearrange("p w i n -> p (i n) w"))
-                    give_bank(("basis_turn", half, g))
+                        else:
+                            src = tiles["basis", 2 * half + i][:].bitcast(F32)[:, 256 * g + w : 256 * g + 256 : 2]
+                        nc.tensor.transpose(bank[:, w, i, :], src, ident[:])
+
+        def empty_basis(half, engs):
+            for g in range(PF):
+                first = 2048 * g + 1024 * half
+                dst = tiles["basis_k"][:, first : first + 1024].bitcast(F32).rearrange("p (c w) -> p c w", w=2)
+                copy_on[engs[g]](out=dst, in_=tiles["basis_turn", half, g][:].rearrange("p w i n -> p (i n) w"))
+                give_bank(("basis_turn", half, g))
 
         def quantize_basis():
             nc.vector.quantize_mx(out=basis_codes[:].bitcast(FP8X4), scales=basis_scales[:], in_=tiles["basis_k"][:])
@@ -317,22 +311,14 @@ def tile_spectral_tikhonov_imaging_s8_kernel(
         frame_codes = keep.tile([128, PF, M], U32, name="frame_codes", align_bytes=64)
         frame_scales = keep.tile([128, PF, M], U8, name="frame_scales", align_bytes=64)
 
-        def turn_h(g, j, eng):
+        def group_h(g, j, eng):
             if j == 0:
                 tiles["h_frames", g] = work.tile([128, PM * 2048], BF16, name="h_frames", tag="wide", bufs=3, align_bytes=64)
-            for th in range(2):
-                bank = take_bank(("h_turn", th), [128, 2, 2, 128])
-                for u in range(2):
-                    words = tiles["h", 2 * g + u][:].bitcast(F32)
-                    for i in range(2):
-                        nc.tensor.transpose(bank[:, u, i, :], words[:, 4 * j + 2 * th + i, :], ident[:])
-            for th in (0, 1):
-                first = 2048 * j + 1024 * th
-                dst = tiles["h_frames", g][:, first : first + 1024].bitcast(F32).rearrange("p (c u) -> p c u", u=2)
-                copy_on[eng](out=dst, in_=tiles["h_turn", th][:].rearrange("p u i q -> p (i q) u"))
-                give_bank(("h_turn", th))
+            dst = tiles["h_frames", g][:, 2048 * j : 2048 * j + 2048].rearrange("p (a i t) -> p a t i", i=4, t=4)
+            src = tiles["h", g][:, :, 512 * j : 512 * j + 512].rearrange("p t (a i) -> p a t i", i=4)
+            copy_on[eng](out=dst, in_=src)
 
-        def quantize_h_frames(g, lo, hi):
+        def quantize_h_frames(g, lo=0, hi=PM):
             cols = slice(512 * lo, 512 * hi)
             nc.vector.quantize_mx(
                 out=frame_codes[:, g, cols].bitcast(FP8X4),
@@ -340,41 +326,40 @@ def tile_spectral_tikhonov_imaging_s8_kernel(
                 in_=tiles["h_frames", g][:, 2048 * lo : 2048 * hi],
             )
 
-        def comps_rows(r, engs, store_by_bank):
-            for j in range(PM):
-                bank = take_bank(("comps", j), [128, 512])
-                cols = slice(512 * j, 512 * j + 512)
+        comps_v = comps.rearrange("(h i p) m -> h p i m", i=2, p=128)
+
+        def comps_half(j, half, engs, store_by_bank=False):
+            cols = slice(512 * j, 512 * j + 512)
+            for i in range(2):
+                bank = take_bank(("comps", i), [128, 512])
                 for g in range(PF):
-                    stationary = slice(R * g + 128 * r, R * g + 128 * r + 128)
+                    first = R * g + 256 * half + 128 * i
                     nc.tensor.matmul_mx(
                         out=bank[:],
-                        lhsT=basis_codes[:, stationary].bitcast(FP8X4),
-                        lhsT_scale=basis_scales[:, stationary],
+                        lhsT=basis_codes[:, first : first + 128].bitcast(FP8X4),
+                        lhsT_scale=basis_scales[:, first : first + 128],
                         rhs=frame_codes[:, g, cols].bitcast(FP8X4),
                         rhs_scale=frame_scales[:, g, cols],
                         start=(g == 0),
                         stop=(g == PF - 1),
                     )
-            result = stage.tile([128, M], F32, name="result", tag="result")
-            rows_out = comps[128 * r : 128 * r + 128, :]
-            for j in range(PM):
-                cols = slice(512 * j, 512 * j + 512)
-                copy_on[engs[j]](
-                    out=result[:, cols].rearrange("p (q t) -> p q t", t=4),
-                    in_=tiles["comps", j][:].rearrange("p (t q) -> p q t", t=4),
+            result = stage.tile([128, 2, 512], F32, name="result", tag="result")
+            for i in range(2):
+                copy_on[engs[i]](
+                    out=result[:, i, :].rearrange("p (q w e) -> p q w e", w=2, e=2),
+                    in_=tiles["comps", i][:].rearrange("p (w q e) -> p q w e", w=2, e=2),
                 )
-                give_bank(("comps", j))
+                give_bank(("comps", i))
                 if store_by_bank:
-                    nc.sync.dma_start(out=rows_out[:, cols], in_=result[:, cols])
+                    nc.sync.dma_start(out=comps_v[half, :, i, cols], in_=result[:, i, :])
             if not store_by_bank:
-                nc.sync.dma_start(out=rows_out, in_=result[:])
+                nc.sync.dma_start(out=comps_v[half, :, :, cols], in_=result[:])
 
         spread_roots()
         logarithms()
-        invert_squares()
         group_us(0, 0, "V")
         group_us(1, 0, "V")
-        weights(0, 0)
+        weights(0)
         quantize_us(0, 0)
         for g in range(PD):
             turn_meas(0, g)
@@ -382,7 +367,7 @@ def tile_spectral_tikhonov_imaging_s8_kernel(
         quantize_us(1, 0)
         empty_meas(0, 1, "S")
         empty_meas(0, 2, "V")
-        weights(0, 1)
+        weights(1)
         for g in range(PD):
             turn_meas(1, g)
         quantize_meas(0)
@@ -391,107 +376,134 @@ def tile_spectral_tikhonov_imaging_s8_kernel(
         empty_meas(1, 2, "S")
         group_us(0, 1, "V", 0, 48)
         group_us(0, 1, "S", 48, 64)
-        project_pass(0, 0, 0)
-        project_pass(0, 1, 0)
+        for j in range(PM):
+            for s in (0, 1):
+                project_pass(s, j, 0)
         quantize_meas(1)
         group_us(1, 1, "S", 0, 32)
-        quantize_us(0, 1)
         group_us(1, 1, "V", 32, 64)
-        project_pass(1, 0, 0)
-        project_pass(1, 1, 0)
+        quantize_us(0, 1)
+        for j in range(PM):
+            for s in (2, 3):
+                project_pass(s, j, 0)
         group_us(0, 2, "S", 0, 32)
-        project_pass(0, 0, 1)
-        project_pass(1, 0, 1)
-        group_us(0, 2, "V", 32, 48)
+        for s in range(4):
+            project_pass(s, 0, 1)
         quantize_us(1, 1)
-        group_us(0, 2, "V", 48, 64)
+        group_us(0, 2, "V", 32, 64)
         group_us(1, 2, "S", 0, 48)
-        project_pass(0, 1, 1)
-        project_pass(1, 1, 1)
+        for s in range(4):
+            project_pass(s, 1, 1)
         group_us(1, 2, "V", 48, 64)
         quantize_us(0, 2)
-        project_pass(0, 0, 2)
-        project_pass(1, 0, 2)
+        for s in range(4):
+            project_pass(s, 0, 2)
         quantize_us(1, 2)
-        weights(1, 0)
+        weights(2)
         weigh(0, 0)
         project_pass(0, 1, 2)
-        group_h(0, 0, "S")
-        weigh(0, 1)
-        turn_meas(2, 0)
-        turn_meas(2, 1)
         project_pass(1, 1, 2)
-        turn_meas(2, 2)
-        group_h(0, 1, "V", 0, 40)
-        group_h(0, 1, "S", 40, 64)
-        quantize_h_modes(0, 0, 1)
-        quantize_h_modes(0, 1, 2)
-        empty_meas(2, 0, "S")
+        weigh(0, 1)
+        weights(3)
+        turn_meas(2, 0)
+        turn_h(0)
         weigh(1, 0)
-        empty_meas(2, 1, "S")
-        empty_meas(2, 2, "S")
-        weights(1, 1)
-        image_half(0, 0, 0, "VS")
-        quantize_meas(2)
+        turn_meas(2, 1)
         weigh(1, 1)
-        image_half(0, 0, 1, "SS")
-        group_h(1, 0, "V")
-        weights(2, 0)
-        image_half(0, 1, 0, "SS")
-        group_h(1, 1, "V")
-        project(2, 0)
-        split_meas(3)
-        quantize_h_modes(1)
-        weights(2, 1)
+        project_pass(2, 1, 2)
+        project_pass(3, 1, 2)
+        empty_meas(2, 0, "S")
+        empty_h(0, "S")
         weigh(2, 0)
-        image_half(0, 1, 1, "SS")
-        project(2, 1)
-        scale_basis(0)
+        turn_h(1)
+        turn_meas(2, 2)
+        quantize_h_modes(0, 0, 1)
+        empty_meas(2, 1, "S")
+        weigh(2, 1)
+        empty_h(1, "S")
+        weigh(3, 0)
+        empty_meas(2, 2, "S")
+        weigh(3, 1)
+        quantize_h_modes(0, 1, 2)
+        split_meas(3)
+        image_half(0, 0, "SS")
+        quantize_meas(2)
+        image_half(0, 1, "SS")
+        turn_h(2)
+        turn_h(3)
         for g in range(PD):
             turn_meas(3, g)
-        weigh(2, 1)
-        for g in range(PD):
-            empty_meas(3, g, "S")
-        split_basis(0, "V")
-        image_half(1, 0, 0, "VS")
+        empty_h(2, "V")
+        weights(4)
+        empty_h(3, "V")
+        empty_meas(3, 0, "S")
+        empty_meas(3, 1, "S")
+        empty_meas(3, 2, "S")
+        scale_basis(0)
+        image_half(1, 0, "SS")
+        quantize_h_modes(1)
         quantize_meas(3)
-        weights(3, 0)
-        group_h(2, 0, "V")
-        image_half(1, 0, 1, "SS")
-        group_h(2, 1, "V")
-        image_half(1, 1, 0, "SS")
+        project(4)
+        weights(5)
         scale_basis(1)
-        project(3, 0)
-        quantize_h_modes(2)
-        weights(3, 1)
-        weigh(3, 0)
-        image_half(1, 1, 1, "SS")
-        project(3, 1)
+        image_half(1, 1, "SS")
+        weigh(4, 0)
+        weigh(4, 1)
+        split_basis(0, "V")
+        image_half(2, 0, "SS")
         split_basis(1, "V")
+        group_h(0, 0, "V")
+        project(5)
+        weights(6)
+        image_half(2, 1, "SS")
+        weigh(5, 0)
+        weigh(5, 1)
+        turn_h(4)
+        turn_basis(0)
+        turn_h(5)
         scale_basis(2)
-        turn_h(0, 0, "S")
-        turn_h(0, 1, "S")
-        weigh(3, 1)
+        empty_h(4, "S")
+        weights(7)
+        empty_basis(0, "VV")
         split_basis(2, "V")
         scale_basis(3)
-        image_half(2, 0, 0, "SS")
-        group_h(3, 0, "V")
+        empty_h(5, "S")
+        image_half(3, 0, "SS")
+        quantize_h_modes(2)
         split_basis(3, "V")
-        image_half(2, 0, 1, "SS")
-        group_h(3, 1, "V")
-        quantize_h_frames(0, 0, 2)
-        image_half(2, 1, 0, "SS")
-        turn_basis("VS")
-        quantize_h_modes(3)
-        image_half(2, 1, 1, "SS")
+        project(6, (0,))
+        project(7, (0,))
+        image_half(3, 1, "SS")
+        weigh(6, 0)
+        weigh(7, 0)
+        project(6, (1,))
+        weigh(6, 1)
+        group_h(0, 1, "V")
+        image_half(4, 0, "SS")
+        turn_basis(1)
+        turn_h(6)
+        group_h(1, 0, "V")
+        empty_basis(1, "SS")
+        empty_h(6, "V")
+        image_half(4, 1, "SS")
+        image_half(5, 0, "SS")
+        quantize_h_modes(3, 0, 1)
         quantize_basis()
-        image_half(3, 0, 0, "VS")
-        turn_h(1, 0, "V")
-        image_half(3, 0, 1, "SS")
+        image_half(5, 1, "SS")
+        quantize_h_frames(0)
+        image_half(6, 0, "SS")
         quantize_h_frames(1, 0, 1)
-        turn_h(1, 1, "V")
-        image_half(3, 1, 0, "SS")
+        project(7, (1,))
+        weigh(7, 1)
+        image_half(6, 1, "SS")
+        turn_h(7)
+        group_h(1, 1, "V")
+        empty_h(7, "S")
+        quantize_h_modes(3, 1, 2)
+        comps_half(0, 0, "SV")
         quantize_h_frames(1, 1, 2)
-        image_half(3, 1, 1, "SV")
-        for r in range(R // 128):
-            comps_rows(r, "SV", store_by_bank=(r == R // 128 - 1))
+        comps_half(0, 1, "SV")
+        image_half(7, 0, "SV")
+        image_half(7, 1, "SV")
+        comps_half(1, 0, "SV")
+        comps_half(1, 1, "SV", store_by_bank=True)

@@ -252,7 +252,7 @@ def tile_spectral_tikhonov_imaging_s8_kernel(
 
         image_v = image.rearrange("(g p t) n -> g t p n", g=PF, p=128)
 
-        def image_half(s, half, engs):
+        def image_half(s, half, engs, store_by_bank=False):
             for i in range(2):
                 n = 2 * half + i
                 bank = take_bank(("image", i), [128, 512])
@@ -268,10 +268,14 @@ def tile_spectral_tikhonov_imaging_s8_kernel(
                         stop=(j == PM - 1),
                     )
             result = stage.tile([128, 1024], F32, name="result", tag="result")
+            rows_out = image_v[s // 4, s % 4, :, 1024 * half : 1024 * half + 1024]
             for i in range(2):
                 copy_on[engs[i]](out=result[:, 512 * i : 512 * i + 512], in_=tiles["image", i][:])
                 give_bank(("image", i))
-            nc.sync.dma_start(out=image_v[s // 4, s % 4, :, 1024 * half : 1024 * half + 1024], in_=result[:])
+                if store_by_bank:
+                    nc.sync.dma_start(out=rows_out[:, 512 * i : 512 * i + 512], in_=result[:, 512 * i : 512 * i + 512])
+            if not store_by_bank:
+                nc.sync.dma_start(out=rows_out, in_=result[:])
 
         basis_codes = keep.tile([128, PF * R], U32, name="basis_codes", align_bytes=64)
         basis_scales = keep.tile([128, PF * R], U8, name="basis_scales", align_bytes=64)
@@ -396,26 +400,27 @@ def tile_spectral_tikhonov_imaging_s8_kernel(
             project_pass(s, 1, 1)
         group_us(1, 2, "V", 48, 64)
         quantize_us(0, 2)
-        for s in range(4):
+        for s in range(3):
             project_pass(s, 0, 2)
         quantize_us(1, 2)
         weights(2)
         weigh(0, 0)
         project_pass(0, 1, 2)
         project_pass(1, 1, 2)
+        project_pass(3, 0, 2)
         weigh(0, 1)
         weights(3)
         turn_meas(2, 0)
         turn_h(0)
         weigh(1, 0)
-        turn_meas(2, 1)
         weigh(1, 1)
         project_pass(2, 1, 2)
         project_pass(3, 1, 2)
+        turn_meas(2, 1)
+        turn_h(1)
         empty_meas(2, 0, "S")
         empty_h(0, "S")
         weigh(2, 0)
-        turn_h(1)
         turn_meas(2, 2)
         quantize_h_modes(0, 0, 1)
         empty_meas(2, 1, "S")
@@ -496,14 +501,14 @@ def tile_spectral_tikhonov_imaging_s8_kernel(
         project(7, (1,))
         weigh(7, 1)
         image_half(6, 1, "SS")
-        turn_h(7)
         group_h(1, 1, "V")
-        empty_h(7, "S")
-        quantize_h_modes(3, 1, 2)
-        comps_half(0, 0, "SV")
+        comps_half(0, 0, "SS")
         quantize_h_frames(1, 1, 2)
         comps_half(0, 1, "SV")
-        image_half(7, 0, "SV")
-        image_half(7, 1, "SV")
+        turn_h(7)
+        empty_h(7, "V")
+        quantize_h_modes(3, 1, 2)
         comps_half(1, 0, "SV")
-        comps_half(1, 1, "SV", store_by_bank=True)
+        comps_half(1, 1, "SV")
+        image_half(7, 0, "SV")
+        image_half(7, 1, "SV", store_by_bank=True)

@@ -28,7 +28,6 @@ ROOT_ROW = 124
 PARTS = 64
 OUT_BUFS = 7
 WEIGHT_BUFS = 4
-BASIS_BUFS = 2
 TINY = 1e-18
 
 
@@ -63,6 +62,8 @@ def tile_spectral_tikhonov_imaging_s8_kernel(
         nc.vector.memset(root_rows[0:ROOT_ROW, :], 0.0)
         zero = keep.tile([128, 1], F32, name="zero")
         nc.vector.memset(zero[:], 0.0)
+        one = keep.tile([128, 1], F32, name="one")
+        nc.vector.memset(one[:], 1.0)
         vt_scale = keep.tile([128, PM, P], U8, name="vt_scale", align_bytes=64)
         nc.vector.memset(vt_scale[:].bitcast(I32), 0)
         ident = keep.tile([128, 128], F32, name="ident")
@@ -102,8 +103,8 @@ def tile_spectral_tikhonov_imaging_s8_kernel(
         nc.sync.dma_start(out=vt[:], in_=vt_words.rearrange("g p n -> p g n"))
         basis_raw = keep.tile([128, 4, F], U8, name="basis_raw")
         nc.sync.dma_start(out=basis_raw[:], in_=basis_bytes.rearrange("(r p) f -> p r f", p=128))
-        basis_wide_scale = keep.tile([128, F], F32, name="basis_wide_scale")
-        nc.sync.dma_start(out=basis_wide_scale[:], in_=basis_scale.rearrange("o k -> (o k)").partition_broadcast(128))
+        frame_scale = keep.tile([128, PF, 4], F32, name="frame_scale")
+        nc.sync.dma_start(out=frame_scale[:], in_=basis_scale.rearrange("o (g p t) -> p (o g) t", p=128, t=4))
 
         log_sigma = keep.tile([128, M], F32, name="log_sigma")
         log_lam = keep.tile([128, PF, 4], F32, name="log_lam")
@@ -280,14 +281,15 @@ def tile_spectral_tikhonov_imaging_s8_kernel(
         basis_codes = keep.tile([128, PF * R], U32, name="basis_codes", align_bytes=64)
         basis_scales = keep.tile([128, PF * R], U8, name="basis_scales", align_bytes=64)
 
-        def scale_basis(r):
-            tiles["basis", r] = work.tile([128, F], BF16, name="basis", bufs=BASIS_BUFS)
-            nc.vector.tensor_tensor(out=tiles["basis", r][:], in0=basis_raw[:, r, :].bitcast(E4M3), in1=basis_wide_scale[:], op=MULT)
-
-        def split_basis(r, eng):
-            tiles["basis_split", r] = keep.tile([128, 2, F // 4], F32, name="basis_split%d" % r)
-            words = tiles["basis", r][:].bitcast(F32)
-            copy_on[eng](out=tiles["basis_split", r][:], in_=words.rearrange("n (c w) -> n w c", w=2))
+        def widen_basis(half):
+            tiles["basis", half] = work.tile([128, 2, 2, F // 4], F32, name="basis")
+            nc.vector.tensor_scalar(
+                out=tiles["basis", half][:].bitcast(BF16).rearrange("n w i (c e) -> n (i c) w e", e=2),
+                in0=basis_raw[:, 2 * half : 2 * half + 2, :].bitcast(E4M3).rearrange("n i (c w e) -> n (i c) w e", w=2, e=2),
+                scalar1=one[:],
+                scalar2=None,
+                op0=MULT,
+            )
 
         def turn_basis(half):
             if half == 0:
@@ -296,21 +298,23 @@ def tile_spectral_tikhonov_imaging_s8_kernel(
                 bank = take_bank(("basis_turn", half, g), [128, 2, 2, 128])
                 for i in range(2):
                     for w in range(2):
-                        if ("basis_split", 2 * half + i) in tiles:
-                            src = tiles["basis_split", 2 * half + i][:, w, 128 * g : 128 * g + 128]
-                        else:
-                            src = tiles["basis", 2 * half + i][:].bitcast(F32)[:, 256 * g + w : 256 * g + 256 : 2]
-                        nc.tensor.transpose(bank[:, w, i, :], src, ident[:])
+                        nc.tensor.transpose(bank[:, w, i, :], tiles["basis", half][:, w, i, 128 * g : 128 * g + 128], ident[:])
 
-        def empty_basis(half, engs):
-            for g in range(PF):
-                first = 2048 * g + 1024 * half
-                dst = tiles["basis_k"][:, first : first + 1024].bitcast(F32).rearrange("p (c w) -> p c w", w=2)
-                copy_on[engs[g]](out=dst, in_=tiles["basis_turn", half, g][:].rearrange("p w i n -> p (i n) w"))
-                give_bank(("basis_turn", half, g))
+        def scale_basis(half, g):
+            first = 2048 * half + 1024 * g
+            nc.vector.tensor_tensor(
+                out=tiles["basis_k"][:, first : first + 1024].rearrange("p (c w e) -> p c w e", w=2, e=2),
+                in0=tiles["basis_turn", half, g][:].bitcast(BF16).rearrange("p w i (n e) -> p (i n) w e", e=2),
+                in1=frame_scale[:, g, :].rearrange("p (w e) -> p w e", e=2).unsqueeze(1).to_broadcast([128, 256, 2, 2]),
+                op=MULT,
+            )
+            give_bank(("basis_turn", half, g))
 
-        def quantize_basis():
-            nc.vector.quantize_mx(out=basis_codes[:].bitcast(FP8X4), scales=basis_scales[:], in_=tiles["basis_k"][:])
+        def quantize_basis(lo=0, hi=2):
+            cols = slice(512 * lo, 512 * hi)
+            nc.vector.quantize_mx(
+                out=basis_codes[:, cols].bitcast(FP8X4), scales=basis_scales[:, cols], in_=tiles["basis_k"][:, 2048 * lo : 2048 * hi]
+            )
 
         frame_codes = keep.tile([128, PF, M], U32, name="frame_codes", align_bytes=64)
         frame_scales = keep.tile([128, PF, M], U8, name="frame_scales", align_bytes=64)
@@ -337,7 +341,7 @@ def tile_spectral_tikhonov_imaging_s8_kernel(
             for i in range(2):
                 bank = take_bank(("comps", i), [128, 512])
                 for g in range(PF):
-                    first = R * g + 256 * half + 128 * i
+                    first = 512 * half + 256 * g + 128 * i
                     nc.tensor.matmul_mx(
                         out=bank[:],
                         lhsT=basis_codes[:, first : first + 128].bitcast(FP8X4),
@@ -371,45 +375,43 @@ def tile_spectral_tikhonov_imaging_s8_kernel(
         quantize_us(1, 0)
         empty_meas(0, 1, "S")
         empty_meas(0, 2, "V")
-        weights(1)
         for g in range(PD):
             turn_meas(1, g)
         quantize_meas(0)
-        empty_meas(1, 0, "S")
-        empty_meas(1, 1, "V")
-        empty_meas(1, 2, "S")
-        group_us(0, 1, "V", 0, 48)
-        group_us(0, 1, "S", 48, 64)
+        for g in range(PD):
+            empty_meas(1, g, "S")
+        group_us(0, 1, "V", 0, 64)
+
         for j in range(PM):
             for s in (0, 1):
                 project_pass(s, j, 0)
+        group_us(1, 1, "S", 0, 40)
         quantize_meas(1)
-        group_us(1, 1, "S", 0, 32)
-        group_us(1, 1, "V", 32, 64)
         quantize_us(0, 1)
+        group_us(1, 1, "V", 40, 64)
         for j in range(PM):
             for s in (2, 3):
                 project_pass(s, j, 0)
-        group_us(0, 2, "S", 0, 32)
+        group_us(0, 2, "S", 0, 40)
         for s in range(4):
             project_pass(s, 0, 1)
+        group_us(0, 2, "V", 40, 64)
         quantize_us(1, 1)
-        group_us(0, 2, "V", 32, 64)
-        group_us(1, 2, "S", 0, 48)
+        group_us(1, 2, "S", 0, 40)
         for s in range(4):
             project_pass(s, 1, 1)
-        group_us(1, 2, "V", 48, 64)
+        group_us(1, 2, "V", 40, 64)
         quantize_us(0, 2)
         for s in range(3):
             project_pass(s, 0, 2)
         quantize_us(1, 2)
-        weights(2)
+        weights(1)
         weigh(0, 0)
         project_pass(0, 1, 2)
         project_pass(1, 1, 2)
         project_pass(3, 0, 2)
         weigh(0, 1)
-        weights(3)
+        weights(2)
         turn_meas(2, 0)
         turn_h(0)
         weigh(1, 0)
@@ -418,14 +420,15 @@ def tile_spectral_tikhonov_imaging_s8_kernel(
         project_pass(3, 1, 2)
         turn_meas(2, 1)
         turn_h(1)
-        empty_meas(2, 0, "S")
+        weights(3)
         empty_h(0, "S")
+        empty_meas(2, 0, "S")
         weigh(2, 0)
         turn_meas(2, 2)
         quantize_h_modes(0, 0, 1)
-        empty_meas(2, 1, "S")
         weigh(2, 1)
         empty_h(1, "S")
+        empty_meas(2, 1, "S")
         weigh(3, 0)
         empty_meas(2, 2, "S")
         weigh(3, 1)
@@ -444,20 +447,18 @@ def tile_spectral_tikhonov_imaging_s8_kernel(
         empty_meas(3, 0, "S")
         empty_meas(3, 1, "S")
         empty_meas(3, 2, "S")
-        scale_basis(0)
+        widen_basis(0)
         image_half(1, 0, "SS")
         quantize_h_modes(1)
         quantize_meas(3)
         project(4)
         weights(5)
-        scale_basis(1)
+        group_h(0, 0, "V")
         image_half(1, 1, "SS")
         weigh(4, 0)
         weigh(4, 1)
-        split_basis(0, "V")
         image_half(2, 0, "SS")
-        split_basis(1, "V")
-        group_h(0, 0, "V")
+        group_h(0, 1, "V")
         project(5)
         weights(6)
         image_half(2, 1, "SS")
@@ -466,49 +467,48 @@ def tile_spectral_tikhonov_imaging_s8_kernel(
         turn_h(4)
         turn_basis(0)
         turn_h(5)
-        scale_basis(2)
-        empty_h(4, "S")
+        empty_h(4, "V")
         weights(7)
-        empty_basis(0, "VV")
-        split_basis(2, "V")
-        scale_basis(3)
+        scale_basis(0, 0)
         empty_h(5, "S")
+        scale_basis(0, 1)
         image_half(3, 0, "SS")
         quantize_h_modes(2)
-        split_basis(3, "V")
         project(6, (0,))
-        project(7, (0,))
         image_half(3, 1, "SS")
         weigh(6, 0)
-        weigh(7, 0)
+        widen_basis(1)
         project(6, (1,))
         weigh(6, 1)
-        group_h(0, 1, "V")
-        image_half(4, 0, "SS")
-        turn_basis(1)
-        turn_h(6)
-        group_h(1, 0, "V")
-        empty_basis(1, "SS")
-        empty_h(6, "V")
-        image_half(4, 1, "SS")
-        image_half(5, 0, "SS")
-        quantize_h_modes(3, 0, 1)
-        quantize_basis()
-        image_half(5, 1, "SS")
         quantize_h_frames(0)
+        image_half(4, 0, "SS")
+        quantize_basis(0, 1)
+        image_half(4, 1, "SS")
+        turn_h(6)
+        turn_basis(1)
+        empty_h(6, "S")
+        scale_basis(1, 0)
+        image_half(5, 0, "SS")
+        scale_basis(1, 1)
+        project(7, (0,))
+        quantize_h_modes(3, 0, 1)
+        weigh(7, 0)
+        image_half(5, 1, "SS")
+        quantize_basis(1, 2)
+        group_h(1, 0, "V")
         image_half(6, 0, "SS")
-        quantize_h_frames(1, 0, 1)
         project(7, (1,))
+        quantize_h_frames(1, 0, 1)
         weigh(7, 1)
         image_half(6, 1, "SS")
         group_h(1, 1, "V")
         comps_half(0, 0, "SS")
         quantize_h_frames(1, 1, 2)
-        comps_half(0, 1, "SV")
+        comps_half(0, 1, "SS")
         turn_h(7)
         empty_h(7, "V")
         quantize_h_modes(3, 1, 2)
-        comps_half(1, 0, "SV")
-        comps_half(1, 1, "SV")
-        image_half(7, 0, "SV")
+        comps_half(1, 0, "SV", store_by_bank=True)
+        comps_half(1, 1, "SV", store_by_bank=True)
+        image_half(7, 0, "SV", store_by_bank=True)
         image_half(7, 1, "SV", store_by_bank=True)

@@ -334,14 +334,12 @@ def tile_spectral_tikhonov_imaging_s8_kernel(
                 in_=tiles["h_frames", g][:, 2048 * lo : 2048 * hi],
             )
 
-        comps_v = comps.rearrange("(h i p) m -> h p i m", i=2, p=128)
-
-        def comps_half(j, half, engs, store_by_bank=False):
-            cols = slice(512 * j, 512 * j + 512)
-            for i in range(2):
-                bank = take_bank(("comps", i), [128, 512])
+        def comps_rows(r, engs, store_by_bank=False):
+            for j in range(PM):
+                bank = take_bank(("comps", j), [128, 512])
+                cols = slice(512 * j, 512 * j + 512)
                 for g in range(PF):
-                    first = 512 * half + 256 * g + 128 * i
+                    first = 512 * (r // 2) + 256 * g + 128 * (r % 2)
                     nc.tensor.matmul_mx(
                         out=bank[:],
                         lhsT=basis_codes[:, first : first + 128].bitcast(FP8X4),
@@ -351,17 +349,19 @@ def tile_spectral_tikhonov_imaging_s8_kernel(
                         start=(g == 0),
                         stop=(g == PF - 1),
                     )
-            result = stage.tile([128, 2, 512], F32, name="result", tag="result")
-            for i in range(2):
-                copy_on[engs[i]](
-                    out=result[:, i, :].rearrange("p (q w e) -> p q w e", w=2, e=2),
-                    in_=tiles["comps", i][:].rearrange("p (w q e) -> p q w e", w=2, e=2),
+            result = stage.tile([128, M], F32, name="result", tag="result")
+            rows_out = comps[128 * r : 128 * r + 128, :]
+            for j in range(PM):
+                cols = slice(512 * j, 512 * j + 512)
+                copy_on[engs[j]](
+                    out=result[:, cols].rearrange("p (q w e) -> p q w e", w=2, e=2),
+                    in_=tiles["comps", j][:].rearrange("p (w q e) -> p q w e", w=2, e=2),
                 )
-                give_bank(("comps", i))
+                give_bank(("comps", j))
                 if store_by_bank:
-                    nc.sync.dma_start(out=comps_v[half, :, i, cols], in_=result[:, i, :])
+                    nc.sync.dma_start(out=rows_out[:, cols], in_=result[:, cols])
             if not store_by_bank:
-                nc.sync.dma_start(out=comps_v[half, :, :, cols], in_=result[:])
+                nc.sync.dma_start(out=rows_out, in_=result[:])
 
         spread_roots()
         logarithms()
@@ -464,51 +464,50 @@ def tile_spectral_tikhonov_imaging_s8_kernel(
         image_half(2, 1, "SS")
         weigh(5, 0)
         weigh(5, 1)
-        turn_h(4)
-        turn_basis(0)
-        turn_h(5)
-        empty_h(4, "V")
-        weights(7)
-        scale_basis(0, 0)
-        empty_h(5, "S")
-        scale_basis(0, 1)
-        image_half(3, 0, "SS")
-        quantize_h_modes(2)
-        project(6, (0,))
-        image_half(3, 1, "SS")
-        weigh(6, 0)
-        widen_basis(1)
-        project(6, (1,))
-        weigh(6, 1)
         quantize_h_frames(0)
-        image_half(4, 0, "SS")
-        quantize_basis(0, 1)
-        image_half(4, 1, "SS")
+        project(6)
+        weights(7)
+        weigh(6, 0)
+        weigh(6, 1)
+        image_half(3, 0, "SS")
+        turn_h(4)
+        turn_h(5)
+        turn_basis(0)
         turn_h(6)
-        turn_basis(1)
+        empty_h(4, "V")
+        empty_h(5, "S")
+        scale_basis(0, 0)
+        image_half(3, 1, "SS")
+        quantize_h_modes(2)
+        scale_basis(0, 1)
         empty_h(6, "S")
-        scale_basis(1, 0)
-        image_half(5, 0, "SS")
-        scale_basis(1, 1)
         project(7, (0,))
-        quantize_h_modes(3, 0, 1)
+        image_half(4, 0, "SS")
         weigh(7, 0)
-        image_half(5, 1, "SS")
-        quantize_basis(1, 2)
+        quantize_basis(0, 1)
+        widen_basis(1)
+        image_half(4, 1, "SS")
         group_h(1, 0, "V")
-        image_half(6, 0, "SS")
+        image_half(5, 0, "SS")
+        quantize_h_modes(3, 0, 1)
+        image_half(5, 1, "SV")
         project(7, (1,))
-        quantize_h_frames(1, 0, 1)
         weigh(7, 1)
-        image_half(6, 1, "SS")
+        quantize_h_frames(1, 0, 1)
+        image_half(6, 0, "SS")
         group_h(1, 1, "V")
-        comps_half(0, 0, "SS")
-        quantize_h_frames(1, 1, 2)
-        comps_half(0, 1, "SS")
+        image_half(6, 1, "SS")
         turn_h(7)
-        empty_h(7, "V")
+        turn_basis(1)
+        quantize_h_frames(1, 1, 2)
+        empty_h(7, "S")
+        scale_basis(1, 0)
+        comps_rows(0, "SS")
         quantize_h_modes(3, 1, 2)
-        comps_half(1, 0, "SV", store_by_bank=True)
-        comps_half(1, 1, "SV", store_by_bank=True)
-        image_half(7, 0, "SV", store_by_bank=True)
-        image_half(7, 1, "SV", store_by_bank=True)
+        scale_basis(1, 1)
+        comps_rows(1, "SS")
+        image_half(7, 0, "SS")
+        quantize_basis(1, 2)
+        image_half(7, 1, "VS")
+        comps_rows(2, "VS")
+        comps_rows(3, "VS")

@@ -64,7 +64,7 @@ def tile_spectral_tikhonov_imaging_s8_kernel(
         nc.vector.memset(zero[:], 0.0)
         one = keep.tile([128, 1], F32, name="one")
         nc.vector.memset(one[:], 1.0)
-        vt_scale = keep.tile([128, PM, P], U8, name="vt_scale", align_bytes=64)
+        vt_scale = keep.tile([128, PM, P], U8, name="vt_scale", align_bytes=256)
         nc.vector.memset(vt_scale[:].bitcast(I32), 0)
         ident = keep.tile([128, 128], F32, name="ident")
         make_identity(nc, ident[:])
@@ -99,7 +99,7 @@ def tile_spectral_tikhonov_imaging_s8_kernel(
                 out=vt_scale[32 * quad : 32 * quad + 4, :, :].bitcast(I32),
                 in_=vt_scales[:, 4 * quad : 4 * quad + 4, :].rearrange("g r n -> r g n").bitcast(I32),
             )
-        vt = keep.tile([128, PM, 2 * P], U8, name="vt", align_bytes=64)
+        vt = keep.tile([128, PM, 2 * P], U8, name="vt", align_bytes=256)
         nc.sync.dma_start(out=vt[:], in_=vt_words.rearrange("g p n -> p g n"))
         basis_raw = keep.tile([128, 4, F], U8, name="basis_raw")
         nc.sync.dma_start(out=basis_raw[:], in_=basis_bytes.rearrange("(r p) f -> p r f", p=128))
@@ -152,8 +152,8 @@ def tile_spectral_tikhonov_imaging_s8_kernel(
 
         def turn_meas(un, g):
             if g == 0:
-                tiles["meas_codes", un] = keep.tile([128, PD, 256], U32, name="meas_codes%d" % un, align_bytes=64)
-                tiles["meas_scales", un] = keep.tile([128, PD, 256], U8, name="meas_scales%d" % un, align_bytes=64)
+                tiles["meas_codes", un] = keep.tile([128, PD, 256], U32, name="meas_codes%d" % un, align_bytes=256)
+                tiles["meas_scales", un] = keep.tile([128, PD, 256], U8, name="meas_scales%d" % un, align_bytes=256)
                 tiles["meas_k", un] = work.tile([128, PD * 1024], BF16, name="meas_k", align_bytes=64)
             bank = take_bank(("meas_turn", un, g), [128, 2, 2, 128])
             for e in range(2):
@@ -177,8 +177,8 @@ def tile_spectral_tikhonov_imaging_s8_kernel(
                     in_=tiles["meas_k", un][:, 1024 * lo : 1024 * hi],
                 )
 
-        us_codes = keep.tile([128, PD, M], U32, name="us_codes", align_bytes=64)
-        us_scales = keep.tile([128, PD, M], U8, name="us_scales", align_bytes=64)
+        us_codes = keep.tile([128, PD, M], U32, name="us_codes", align_bytes=256)
+        us_scales = keep.tile([128, PD, M], U8, name="us_scales", align_bytes=256)
 
         def group_us(j, g, eng, lo=0, hi=PARTS):
             if lo == 0:
@@ -242,8 +242,8 @@ def tile_spectral_tikhonov_imaging_s8_kernel(
 
         def quantize_h_modes(un, lo=0, hi=2):
             if lo == 0:
-                tiles["h_codes", un] = keep.tile([128, 512], U32, name="h_codes%d" % un, align_bytes=64)
-                tiles["h_scales", un] = keep.tile([128, 512], U8, name="h_scales%d" % un, align_bytes=64)
+                tiles["h_codes", un] = keep.tile([128, 512], U32, name="h_codes%d" % un, align_bytes=256)
+                tiles["h_scales", un] = keep.tile([128, 512], U8, name="h_scales%d" % un, align_bytes=256)
             cols = slice(256 * lo, 256 * hi)
             nc.vector.quantize_mx(
                 out=tiles["h_codes", un][:, cols].bitcast(FP8X4),
@@ -278,8 +278,8 @@ def tile_spectral_tikhonov_imaging_s8_kernel(
             if not store_by_bank:
                 nc.sync.dma_start(out=rows_out, in_=result[:])
 
-        basis_codes = keep.tile([128, PF * R], U32, name="basis_codes", align_bytes=64)
-        basis_scales = keep.tile([128, PF * R], U8, name="basis_scales", align_bytes=64)
+        basis_codes = keep.tile([128, PF * R], U32, name="basis_codes", align_bytes=256)
+        basis_scales = keep.tile([128, PF * R], U8, name="basis_scales", align_bytes=256)
 
         def widen_basis(half):
             tiles["basis", half] = work.tile([128, 2, 2, F // 4], F32, name="basis")
@@ -316,8 +316,8 @@ def tile_spectral_tikhonov_imaging_s8_kernel(
                 out=basis_codes[:, cols].bitcast(FP8X4), scales=basis_scales[:, cols], in_=tiles["basis_k"][:, 2048 * lo : 2048 * hi]
             )
 
-        frame_codes = keep.tile([128, PF, M], U32, name="frame_codes", align_bytes=64)
-        frame_scales = keep.tile([128, PF, M], U8, name="frame_scales", align_bytes=64)
+        frame_codes = keep.tile([128, PF, M], U32, name="frame_codes", align_bytes=256)
+        frame_scales = keep.tile([128, PF, M], U8, name="frame_scales", align_bytes=256)
 
         def group_h(g, j, eng):
             if j == 0:

@@ -410,21 +410,21 @@ def tile_spectral_tikhonov_imaging_s8_kernel(
         project_pass(0, 1, 2)
         project_pass(1, 1, 2)
         project_pass(3, 0, 2)
-        weigh(0, 1)
-        weights(2)
-        turn_meas(2, 0)
-        turn_h(0)
-        weigh(1, 0)
-        weigh(1, 1)
         project_pass(2, 1, 2)
         project_pass(3, 1, 2)
+        weigh(0, 1)
+        weights(2)
+        turn_h(0)
+        turn_meas(2, 0)
+        weigh(1, 0)
+        weigh(1, 1)
         turn_meas(2, 1)
         turn_h(1)
         weights(3)
         empty_h(0, "S")
+        turn_meas(2, 2)
         empty_meas(2, 0, "S")
         weigh(2, 0)
-        turn_meas(2, 2)
         quantize_h_modes(0, 0, 1)
         weigh(2, 1)
         empty_h(1, "S")

@@ -40,12 +40,10 @@ def tile_spectral_tikhonov_imaging_s8_kernel(
         work = ctx.enter_context(tc.tile_pool(name="work", bufs=2))
         stage = ctx.enter_context(tc.tile_pool(name="stage", bufs=OUT_BUFS))
         psum = ctx.enter_context(tc.psum_pool(name="psum", bufs=1))
-
         ctx.enter_context(tc.manual_schedule())
 
         copy_on = {"S": nc.scalar.copy, "V": nc.vector.tensor_copy}
         tiles = {}
-
         free_banks = list(range(BANKS))
         held = {}
 
@@ -58,53 +56,56 @@ def tile_spectral_tikhonov_imaging_s8_kernel(
         def give_bank(key):
             free_banks.append(held[key])
 
+        ident = keep.tile([128, 128], F32, name="ident")
+        make_identity(nc, ident[:])
         root_rows = keep.tile([128, 512], BF16, name="root_rows")
         nc.vector.memset(root_rows[0:ROOT_ROW, :], 0.0)
         zero = keep.tile([128, 1], F32, name="zero")
         nc.vector.memset(zero[:], 0.0)
         one = keep.tile([128, 1], F32, name="one")
         nc.vector.memset(one[:], 1.0)
-        vt_scale = keep.tile([128, PM, P], U8, name="vt_scale", align_bytes=256)
-        nc.vector.memset(vt_scale[:].bitcast(I32), 0)
-        ident = keep.tile([128, 128], F32, name="ident")
-        make_identity(nc, ident[:])
         tiny = keep.tile([128, 1], F32, name="tiny")
         nc.vector.tensor_scalar(out=tiny[:], in0=zero[:], scalar1=TINY, scalar2=None, op0=ADD)
         ident_b = keep.tile([128, 128], BF16, name="ident_b")
         nc.vector.tensor_copy(out=ident_b[:], in_=ident[:])
+        vt_scale = keep.tile([128, PM, P], U8, name="vt_scale", align_bytes=256)
 
         meas_v = meas.rearrange("(g p t) d -> g p t d", g=PF, p=128)
         us_v = us.rearrange("(g p k) m -> g p k m", p=128, k=4)
+
+        def load_roots():
+            for side, vec in enumerate((lam, sigma)):
+                first = ROOT_ROW + 2 * side
+                nc.sync.dma_start(out=root_rows[first : first + 2, :], in_=vec.rearrange("(g x) -> g x", g=2))
 
         def load_meas(un):
             tiles["meas", un] = work.tile([128, 2, D], BF16, name="raw_meas", tag="raw_meas", bufs=4)
             nc.sync.dma_start(out=tiles["meas", un][:], in_=meas_v[un // 2, :, 2 * (un % 2) : 2 * (un % 2) + 2, :])
 
         def load_us(g):
-            tiles["us", g] = work.tile([128, 4, M], BF16, name="raw_us", tag="wide", bufs=3, align_bytes=64)
-            nc.sync.dma_start(out=tiles["us", g][:], in_=us_v[g])
+            whole = work.tile([128, 4, M], BF16, name="raw_us", tag="wide", bufs=3, align_bytes=64)
+            nc.sync.dma_start(out=whole[:], in_=us_v[g])
+            for j in range(PM):
+                tiles["us", g, j] = whole[:, :, 512 * j : 512 * j + 512]
 
-        for side, vec in enumerate((lam, sigma)):
-            first = ROOT_ROW + 2 * side
-            nc.sync.dma_start(out=root_rows[first : first + 2, :], in_=vec.rearrange("(g x) -> g x", g=2))
-        load_us(0)
-        load_meas(0)
-        load_meas(1)
-        load_us(1)
-        load_us(2)
-        load_meas(2)
-        load_meas(3)
-        for quad in range(4):
-            nc.sync.dma_start(
-                out=vt_scale[32 * quad : 32 * quad + 4, :, :].bitcast(I32),
-                in_=vt_scales[:, 4 * quad : 4 * quad + 4, :].rearrange("g r n -> r g n").bitcast(I32),
-            )
         vt = keep.tile([128, PM, 2 * P], U8, name="vt", align_bytes=256)
-        nc.sync.dma_start(out=vt[:], in_=vt_words.rearrange("g p n -> p g n"))
         basis_raw = keep.tile([128, 4, F], U8, name="basis_raw")
-        nc.sync.dma_start(out=basis_raw[:], in_=basis_bytes.rearrange("(r p) f -> p r f", p=128))
         frame_scale = keep.tile([128, PF, 4], F32, name="frame_scale")
-        nc.sync.dma_start(out=frame_scale[:], in_=basis_scale.rearrange("o (g p t) -> p (o g) t", p=128, t=4))
+
+        def clear_vt_scale():
+            nc.vector.memset(vt_scale[:].bitcast(I32), 0)
+
+        def load_vt():
+            for quad in range(4):
+                nc.sync.dma_start(
+                    out=vt_scale[32 * quad : 32 * quad + 4, :, :].bitcast(I32),
+                    in_=vt_scales[:, 4 * quad : 4 * quad + 4, :].rearrange("g r n -> r g n").bitcast(I32),
+                )
+            nc.sync.dma_start(out=vt[:], in_=vt_words.rearrange("g p n -> p g n"))
+
+        def load_basis():
+            nc.sync.dma_start(out=basis_raw[:], in_=basis_bytes.rearrange("(r p) f -> p r f", p=128))
+            nc.sync.dma_start(out=frame_scale[:], in_=basis_scale.rearrange("o (g p t) -> p (o g) t", p=128, t=4))
 
         log_sigma = keep.tile([128, M], F32, name="log_sigma")
         log_lam = keep.tile([128, PF, 4], F32, name="log_lam")
@@ -129,7 +130,6 @@ def tile_spectral_tikhonov_imaging_s8_kernel(
             shifted = keep.tile([128, PF, 4], F32, name="shifted")
             nc.vector.tensor_scalar(out=shifted[:], in0=lam_columns, scalar1=TINY, scalar2=None, op0=ADD)
             give_bank("lam")
-            nc.vector.reciprocal(out=inverse[:], in_=shifted[:].rearrange("p g t -> p (g t)"))
             for j in range(PM):
                 nc.scalar.activation(
                     out=log_sigma[:, 512 * j : 512 * j + 512].rearrange("p (w q e) -> p w q e", w=2, e=2),
@@ -138,17 +138,26 @@ def tile_spectral_tikhonov_imaging_s8_kernel(
                     bias=tiny[:],
                 )
                 give_bank(("sigma", j))
+            tiles["shifted"] = shifted
 
-        def weights(s):
-            tiles["weight", s] = work.tile([128, M], F32, name="weight", bufs=WEIGHT_BUFS)
+        def invert_lam():
+            nc.vector.reciprocal(out=inverse[:], in_=tiles["shifted"][:].rearrange("p g t -> p (g t)"))
+
+        def weights(s, lo=0, hi=M):
+            if lo == 0:
+                tiles["weight", s] = work.tile([128, M], F32, name="weight", bufs=WEIGHT_BUFS)
             nc.scalar.activation(
-                out=tiles["weight", s][:], in_=log_sigma[:], func=SIGMOID, scale=-2.0, bias=log_lam[:, s // 4, s % 4 : s % 4 + 1]
+                out=tiles["weight", s][:, lo:hi],
+                in_=log_sigma[:, lo:hi],
+                func=SIGMOID,
+                scale=-2.0,
+                bias=log_lam[:, s // 4, s % 4 : s % 4 + 1],
             )
 
-        def split_meas(un):
+        def split_meas(un, eng="V"):
             tiles["split", un] = work.tile([128, 2, 2, D // 4], F32, name="split", tag="raw_meas", bufs=4)
             words = tiles["meas", un][:].bitcast(F32)
-            nc.vector.tensor_copy(out=tiles["split", un][:], in_=words.rearrange("r e (c w) -> r e w c", w=2))
+            copy_on[eng](out=tiles["split", un][:], in_=words.rearrange("r e (c w) -> r e w c", w=2))
 
         def turn_meas(un, g):
             if g == 0:
@@ -169,23 +178,42 @@ def tile_spectral_tikhonov_imaging_s8_kernel(
             copy_on[eng](out=dst, in_=tiles["meas_turn", un, g][:].rearrange("p e w r -> p e r w"))
             give_bank(("meas_turn", un, g))
 
-        def quantize_meas(un):
-            for lo, hi in ((0, 2), (2, 3)):
-                nc.vector.quantize_mx(
-                    out=tiles["meas_codes", un][:, lo:hi, :].rearrange("p g c -> p (g c)").bitcast(FP8X4),
-                    scales=tiles["meas_scales", un][:, lo:hi, :].rearrange("p g c -> p (g c)"),
-                    in_=tiles["meas_k", un][:, 1024 * lo : 1024 * hi],
-                )
+        def quantize_meas(un, lo, hi):
+            nc.vector.quantize_mx(
+                out=tiles["meas_codes", un][:, lo:hi, :].rearrange("p g c -> p (g c)").bitcast(FP8X4),
+                scales=tiles["meas_scales", un][:, lo:hi, :].rearrange("p g c -> p (g c)"),
+                in_=tiles["meas_k", un][:, 1024 * lo : 1024 * hi],
+            )
 
         us_codes = keep.tile([128, PD, M], U32, name="us_codes", align_bytes=256)
         us_scales = keep.tile([128, PD, M], U8, name="us_scales", align_bytes=256)
 
+        def us_k(j, g):
+            if ("us_k", j, g) not in tiles:
+                tiles["us_k", j, g] = work.tile([128, 2048], BF16, name="us_k", align_bytes=64, bufs=4)
+            return tiles["us_k", j, g]
+
         def group_us(j, g, eng, lo=0, hi=PARTS):
-            if lo == 0:
-                tiles["us_k", j, g] = work.tile([128, 2048], BF16, name="us_k", align_bytes=64, bufs=3)
-            dst = tiles["us_k", j, g][:].rearrange("p (w q e k) -> p q k w e", w=2, e=2, k=4)
-            src = tiles["us", g][:, :, 512 * j : 512 * j + 512].rearrange("p k (q w e) -> p q k w e", w=2, e=2)
+            dst = us_k(j, g)[:].rearrange("p (w q e k) -> p q k w e", w=2, e=2, k=4)
+            src = tiles["us", g, j].rearrange("p k (q w e) -> p q k w e", w=2, e=2)
             copy_on[eng](out=dst[:, 2 * lo : 2 * hi], in_=src[:, 2 * lo : 2 * hi])
+
+        def weave_us(j, g, half):
+            bank = take_bank(("weave", j, g, half), [128, 2, 512], BF16)
+            src = tiles["us", g, j].rearrange("p k (q w e) -> p w q e k", w=2, e=2)
+            for w in range(2):
+                nc.tensor.matmul(
+                    out=bank[:, w, :].rearrange("p (q e k) -> p q e k", e=2, k=4),
+                    lhsT=ident_b[:],
+                    rhs=src[:, w, 64 * half : 64 * half + 64],
+                    start=True,
+                    stop=True,
+                )
+
+        def empty_weave(j, g, half, eng):
+            dst = us_k(j, g)[:].rearrange("p (w c) -> p w c", w=2)[:, :, 512 * half : 512 * half + 512]
+            copy_on[eng](out=dst, in_=tiles["weave", j, g, half][:])
+            give_bank(("weave", j, g, half))
 
         def quantize_us(j, g):
             cols = slice(512 * j, 512 * j + 512)
@@ -206,10 +234,9 @@ def tile_spectral_tikhonov_imaging_s8_kernel(
                 stop=(g == PD - 1),
             )
 
-        def project(s, passes=range(PM)):
-            for j in passes:
-                for g in range(PD):
-                    project_pass(s, j, g)
+        def project(s, j):
+            for g in range(PD):
+                project_pass(s, j, g)
 
         def weigh(s, j):
             if ("h", s // 4) not in tiles:
@@ -253,30 +280,36 @@ def tile_spectral_tikhonov_imaging_s8_kernel(
 
         image_v = image.rearrange("(g p t) n -> g t p n", g=PF, p=128)
 
-        def image_half(s, half, engs, store_by_bank=False):
-            for i in range(2):
-                n = 2 * half + i
-                bank = take_bank(("image", i), [128, 512])
-                for j in range(PM):
-                    first = 256 * (s % 2) + 128 * j
-                    nc.tensor.matmul_mx(
-                        out=bank[:],
-                        lhsT=tiles["h_codes", s // 2][:, first : first + 128].bitcast(FP8X4),
-                        lhsT_scale=tiles["h_scales", s // 2][:, first : first + 128],
-                        rhs=vt[:, j, 1024 * n : 1024 * n + 1024].bitcast(FP4X4),
-                        rhs_scale=vt_scale[:, j, 512 * n : 512 * n + 512],
-                        start=(j == 0),
-                        stop=(j == PM - 1),
-                    )
-            result = stage.tile([128, 1024], F32, name="result", tag="result")
-            rows_out = image_v[s // 4, s % 4, :, 1024 * half : 1024 * half + 1024]
-            for i in range(2):
-                copy_on[engs[i]](out=result[:, 512 * i : 512 * i + 512], in_=tiles["image", i][:])
-                give_bank(("image", i))
-                if store_by_bank:
-                    nc.sync.dma_start(out=rows_out[:, 512 * i : 512 * i + 512], in_=result[:, 512 * i : 512 * i + 512])
-            if not store_by_bank:
-                nc.sync.dma_start(out=rows_out, in_=result[:])
+        def image_bank(s, n):
+            bank = take_bank(("image", s, n), [128, 512])
+            for j in range(PM):
+                first = 256 * (s % 2) + 128 * j
+                nc.tensor.matmul_mx(
+                    out=bank[:],
+                    lhsT=tiles["h_codes", s // 2][:, first : first + 128].bitcast(FP8X4),
+                    lhsT_scale=tiles["h_scales", s // 2][:, first : first + 128],
+                    rhs=vt[:, j, 1024 * n : 1024 * n + 1024].bitcast(FP4X4),
+                    rhs_scale=vt_scale[:, j, 512 * n : 512 * n + 512],
+                    start=(j == 0),
+                    stop=(j == PM - 1),
+                )
+
+        def image_half(s, half):
+            image_bank(s, 2 * half)
+            image_bank(s, 2 * half + 1)
+
+        def empty_image(s, n, eng):
+            if n % 2 == 0:
+                tiles["result", s, n // 2] = stage.tile([128, 1024], F32, name="result", tag="result")
+            result = tiles["result", s, n // 2]
+            copy_on[eng](out=result[:, 512 * (n % 2) : 512 * (n % 2) + 512], in_=tiles["image", s, n][:])
+            give_bank(("image", s, n))
+            if n % 2 == 1:
+                nc.sync.dma_start(out=image_v[s // 4, s % 4, :, 1024 * (n // 2) : 1024 * (n // 2) + 1024], in_=result[:])
+
+        def store_image(s, half, engs):
+            empty_image(s, 2 * half, engs[0])
+            empty_image(s, 2 * half + 1, engs[1])
 
         basis_codes = keep.tile([128, PF * R], U32, name="basis_codes", align_bytes=256)
         basis_scales = keep.tile([128, PF * R], U8, name="basis_scales", align_bytes=256)
@@ -291,14 +324,13 @@ def tile_spectral_tikhonov_imaging_s8_kernel(
                 op0=MULT,
             )
 
-        def turn_basis(half):
-            if half == 0:
+        def turn_basis(half, g):
+            if half == 0 and g == 0:
                 tiles["basis_k"] = work.tile([128, PF * 2048], BF16, name="basis_k", tag="wide", bufs=3, align_bytes=64)
-            for g in range(PF):
-                bank = take_bank(("basis_turn", half, g), [128, 2, 2, 128])
-                for i in range(2):
-                    for w in range(2):
-                        nc.tensor.transpose(bank[:, w, i, :], tiles["basis", half][:, w, i, 128 * g : 128 * g + 128], ident[:])
+            bank = take_bank(("basis_turn", half, g), [128, 2, 2, 128])
+            for i in range(2):
+                for w in range(2):
+                    nc.tensor.transpose(bank[:, w, i, :], tiles["basis", half][:, w, i, 128 * g : 128 * g + 128], ident[:])
 
         def scale_basis(half, g):
             first = 2048 * half + 1024 * g
@@ -310,21 +342,23 @@ def tile_spectral_tikhonov_imaging_s8_kernel(
             )
             give_bank(("basis_turn", half, g))
 
-        def quantize_basis(lo=0, hi=2):
-            cols = slice(512 * lo, 512 * hi)
+        def quantize_basis(half):
+            cols = slice(512 * half, 512 * half + 512)
             nc.vector.quantize_mx(
-                out=basis_codes[:, cols].bitcast(FP8X4), scales=basis_scales[:, cols], in_=tiles["basis_k"][:, 2048 * lo : 2048 * hi]
+                out=basis_codes[:, cols].bitcast(FP8X4),
+                scales=basis_scales[:, cols],
+                in_=tiles["basis_k"][:, 2048 * half : 2048 * half + 2048],
             )
 
         frame_codes = keep.tile([128, PF, M], U32, name="frame_codes", align_bytes=256)
         frame_scales = keep.tile([128, PF, M], U8, name="frame_scales", align_bytes=256)
 
-        def group_h(g, j, eng):
-            if j == 0:
+        def group_h(g, j, eng, lo=0, hi=PARTS):
+            if j == 0 and lo == 0:
                 tiles["h_frames", g] = work.tile([128, PM * 2048], BF16, name="h_frames", tag="wide", bufs=3, align_bytes=64)
             dst = tiles["h_frames", g][:, 2048 * j : 2048 * j + 2048].rearrange("p (a i t) -> p a t i", i=4, t=4)
             src = tiles["h", g][:, :, 512 * j : 512 * j + 512].rearrange("p t (a i) -> p a t i", i=4)
-            copy_on[eng](out=dst, in_=src)
+            copy_on[eng](out=dst[:, 2 * lo : 2 * hi], in_=src[:, 2 * lo : 2 * hi])
 
         def quantize_h_frames(g, lo=0, hi=PM):
             cols = slice(512 * lo, 512 * hi)
@@ -334,180 +368,234 @@ def tile_spectral_tikhonov_imaging_s8_kernel(
                 in_=tiles["h_frames", g][:, 2048 * lo : 2048 * hi],
             )
 
-        def comps_rows(r, engs, store_by_bank=False):
-            for j in range(PM):
-                bank = take_bank(("comps", j), [128, 512])
-                cols = slice(512 * j, 512 * j + 512)
-                for g in range(PF):
-                    first = 512 * (r // 2) + 256 * g + 128 * (r % 2)
-                    nc.tensor.matmul_mx(
-                        out=bank[:],
-                        lhsT=basis_codes[:, first : first + 128].bitcast(FP8X4),
-                        lhsT_scale=basis_scales[:, first : first + 128],
-                        rhs=frame_codes[:, g, cols].bitcast(FP8X4),
-                        rhs_scale=frame_scales[:, g, cols],
-                        start=(g == 0),
-                        stop=(g == PF - 1),
-                    )
-            result = stage.tile([128, M], F32, name="result", tag="result")
-            rows_out = comps[128 * r : 128 * r + 128, :]
-            for j in range(PM):
-                cols = slice(512 * j, 512 * j + 512)
-                copy_on[engs[j]](
-                    out=result[:, cols].rearrange("p (q w e) -> p q w e", w=2, e=2),
-                    in_=tiles["comps", j][:].rearrange("p (w q e) -> p q w e", w=2, e=2),
+        def comps_bank(r, j):
+            bank = take_bank(("comps", r, j), [128, 512])
+            cols = slice(512 * j, 512 * j + 512)
+            for g in range(PF):
+                first = 512 * (r // 2) + 256 * g + 128 * (r % 2)
+                nc.tensor.matmul_mx(
+                    out=bank[:],
+                    lhsT=basis_codes[:, first : first + 128].bitcast(FP8X4),
+                    lhsT_scale=basis_scales[:, first : first + 128],
+                    rhs=frame_codes[:, g, cols].bitcast(FP8X4),
+                    rhs_scale=frame_scales[:, g, cols],
+                    start=(g == 0),
+                    stop=(g == PF - 1),
                 )
-                give_bank(("comps", j))
-                if store_by_bank:
-                    nc.sync.dma_start(out=rows_out[:, cols], in_=result[:, cols])
-            if not store_by_bank:
-                nc.sync.dma_start(out=rows_out, in_=result[:])
 
+        def comps_rows(r):
+            comps_bank(r, 0)
+            comps_bank(r, 1)
+
+        def empty_comps(r, j, eng):
+            if j == 0:
+                tiles["rows", r] = stage.tile([128, M], F32, name="result", tag="result")
+            result = tiles["rows", r]
+            copy_on[eng](
+                out=result[:, 512 * j : 512 * j + 512].rearrange("p (q w e) -> p q w e", w=2, e=2),
+                in_=tiles["comps", r, j][:].rearrange("p (w q e) -> p q w e", w=2, e=2),
+            )
+            give_bank(("comps", r, j))
+            if j == 1:
+                nc.sync.dma_start(out=comps[128 * r : 128 * r + 128, :], in_=result[:])
+
+        def store_comps(r, engs):
+            empty_comps(r, 0, engs[0])
+            empty_comps(r, 1, engs[1])
+
+        load_roots()
+        load_meas(0)
+        load_us(0)
+        load_meas(1)
+        load_us(1)
+        load_us(2)
+        load_meas(2)
+        load_meas(3)
         spread_roots()
+        clear_vt_scale()
+        load_vt()
+        load_basis()
         logarithms()
-        group_us(0, 0, "V")
-        group_us(1, 0, "V")
-        weights(0)
-        quantize_us(0, 0)
+        invert_lam()
         for g in range(PD):
             turn_meas(0, g)
-        empty_meas(0, 0, "S")
-        quantize_us(1, 0)
-        empty_meas(0, 1, "S")
-        empty_meas(0, 2, "V")
+        weights(0, 0, 256)
+        for g in range(PD):
+            empty_meas(0, g, "V")
+        weave_us(1, 0, 0)
+        weave_us(1, 0, 1)
+        group_us(0, 0, "S", 0, 12)
+        group_us(0, 0, "V", 12, 64)
+        empty_weave(1, 0, 0, "S")
+        empty_weave(1, 0, 1, "S")
+        quantize_meas(0, 0, 2)
+        quantize_us(0, 0)
         for g in range(PD):
             turn_meas(1, g)
-        quantize_meas(0)
+        quantize_us(1, 0)
         for g in range(PD):
             empty_meas(1, g, "S")
-        group_us(0, 1, "V", 0, 64)
-
-        for j in range(PM):
-            for s in (0, 1):
-                project_pass(s, j, 0)
-        group_us(1, 1, "S", 0, 40)
-        quantize_meas(1)
-        quantize_us(0, 1)
-        group_us(1, 1, "V", 40, 64)
+        quantize_meas(1, 0, 1)
+        project_pass(0, 0, 0)
+        weave_us(1, 1, 0)
+        weave_us(1, 1, 1)
+        group_us(0, 1, "V")
+        empty_weave(1, 1, 0, "S")
+        empty_weave(1, 1, 1, "S")
+        project_pass(1, 0, 0)
+        project_pass(0, 1, 0)
+        project_pass(1, 1, 0)
         for j in range(PM):
             for s in (2, 3):
                 project_pass(s, j, 0)
-        group_us(0, 2, "S", 0, 40)
-        for s in range(4):
-            project_pass(s, 0, 1)
-        group_us(0, 2, "V", 40, 64)
+        quantize_meas(1, 1, 3)
+        quantize_us(0, 1)
+        weights(0, 256, M)
         quantize_us(1, 1)
+        for j in range(PM):
+            for s in range(4):
+                project_pass(s, j, 1)
+        group_us(0, 2, "S", 0, 24)
+        group_us(0, 2, "V", 24, 64)
+        quantize_meas(0, 2, 3)
         group_us(1, 2, "S", 0, 40)
-        for s in range(4):
-            project_pass(s, 1, 1)
-        group_us(1, 2, "V", 40, 64)
         quantize_us(0, 2)
-        for s in range(3):
+        group_us(1, 2, "V", 40, 64)
+        for s in range(4):
             project_pass(s, 0, 2)
         quantize_us(1, 2)
+
         weights(1)
         weigh(0, 0)
-        project_pass(0, 1, 2)
-        project_pass(1, 1, 2)
-        project_pass(3, 0, 2)
-        project_pass(2, 1, 2)
-        project_pass(3, 1, 2)
+        for s in range(4):
+            project_pass(s, 1, 2)
         weigh(0, 1)
         weights(2)
         turn_h(0)
         turn_meas(2, 0)
         weigh(1, 0)
-        weigh(1, 1)
+        weights(3, 0, 512)
         turn_meas(2, 1)
-        turn_h(1)
-        weights(3)
+        weigh(1, 1)
         empty_h(0, "S")
         turn_meas(2, 2)
         empty_meas(2, 0, "S")
-        weigh(2, 0)
         quantize_h_modes(0, 0, 1)
-        weigh(2, 1)
-        empty_h(1, "S")
+        weigh(2, 0)
         empty_meas(2, 1, "S")
-        weigh(3, 0)
+        weigh(2, 1)
+        image_half(0, 0)
         empty_meas(2, 2, "S")
+        weigh(3, 0)
+        weights(3, 512, M)
+        quantize_meas(2, 0, 2)
+
+        image_half(0, 1)
+        quantize_meas(2, 2, 3)
+        weights(4, 0, 512)
         weigh(3, 1)
-        quantize_h_modes(0, 1, 2)
         split_meas(3)
-        image_half(0, 0, "SS")
-        quantize_meas(2)
-        image_half(0, 1, "SS")
+        project(4, 0)
+        store_image(0, 0, "SS")
+        project(4, 1)
+        group_h(0, 0, "V")
+        weights(4, 512, M)
+        store_image(0, 1, "SS")
+        weigh(4, 0)
+        turn_h(1)
         turn_h(2)
-        turn_h(3)
+        empty_h(1, "V")
+        weigh(4, 1)
         for g in range(PD):
             turn_meas(3, g)
-        empty_h(2, "V")
-        weights(4)
-        empty_h(3, "V")
+        empty_h(2, "S")
+        project(5, 0)
         empty_meas(3, 0, "S")
+        quantize_h_modes(0, 1, 2)
         empty_meas(3, 1, "S")
-        empty_meas(3, 2, "S")
-        widen_basis(0)
-        image_half(1, 0, "SS")
-        quantize_h_modes(1)
-        quantize_meas(3)
-        project(4)
-        weights(5)
-        group_h(0, 0, "V")
-        image_half(1, 1, "SS")
-        weigh(4, 0)
-        weigh(4, 1)
-        image_half(2, 0, "SS")
+        project(5, 1)
+        quantize_h_modes(1, 0, 1)
         group_h(0, 1, "V")
-        project(5)
-        weights(6)
-        image_half(2, 1, "SS")
+        empty_meas(3, 2, "S")
+        weights(5)
+        image_half(1, 0)
+        quantize_meas(3, 0, 2)
+        quantize_meas(3, 2, 3)
         weigh(5, 0)
         weigh(5, 1)
+        image_half(1, 1)
+        store_image(1, 0, "SS")
         quantize_h_frames(0)
-        project(6)
-        weights(7)
+        image_half(2, 0)
+        store_image(1, 1, "SS")
+        widen_basis(0)
+        image_half(2, 1)
+        weights(6)
+        project(6, 0)
+        store_image(2, 0, "SS")
+        project(6, 1)
+        store_image(2, 1, "SS")
         weigh(6, 0)
-        weigh(6, 1)
-        image_half(3, 0, "SS")
+        turn_h(3)
         turn_h(4)
+        weigh(6, 1)
         turn_h(5)
-        turn_basis(0)
-        turn_h(6)
-        empty_h(4, "V")
-        empty_h(5, "S")
+        weights(7, 0, 512)
+        turn_basis(0, 0)
+        empty_h(3, "V")
+        empty_h(4, "S")
+        turn_basis(0, 1)
+        project(7, 0)
+        quantize_h_modes(1, 1, 2)
         scale_basis(0, 0)
-        image_half(3, 1, "SS")
-        quantize_h_modes(2)
-        scale_basis(0, 1)
-        empty_h(6, "S")
-        project(7, (0,))
-        image_half(4, 0, "SS")
+        empty_h(5, "S")
+        image_half(3, 0)
         weigh(7, 0)
-        quantize_basis(0, 1)
-        widen_basis(1)
-        image_half(4, 1, "SS")
+        image_half(3, 1)
+        weights(7, 512, M)
+        quantize_h_modes(2)
+        store_image(3, 0, "SS")
+        scale_basis(0, 1)
+        image_half(4, 0)
+        store_image(3, 1, "SS")
         group_h(1, 0, "V")
-        image_half(5, 0, "SS")
-        quantize_h_modes(3, 0, 1)
-        image_half(5, 1, "SV")
-        project(7, (1,))
+        image_half(4, 1)
+        store_image(4, 0, "SS")
+        quantize_basis(0)
+        project(7, 1)
+        widen_basis(1)
+        store_image(4, 1, "SS")
+        image_half(5, 0)
         weigh(7, 1)
         quantize_h_frames(1, 0, 1)
-        image_half(6, 0, "SS")
+        image_half(5, 1)
+        store_image(5, 0, "SS")
         group_h(1, 1, "V")
-        image_half(6, 1, "SS")
+        turn_h(6)
         turn_h(7)
-        turn_basis(1)
+        store_image(5, 1, "SS")
+        turn_basis(1, 0)
+        turn_basis(1, 1)
+        empty_h(6, "V")
         quantize_h_frames(1, 1, 2)
         empty_h(7, "S")
+        comps_rows(0)
+        quantize_h_modes(3)
         scale_basis(1, 0)
-        comps_rows(0, "SS")
-        quantize_h_modes(3, 1, 2)
+        store_comps(0, "SS")
+        comps_rows(1)
         scale_basis(1, 1)
-        comps_rows(1, "SS")
-        image_half(7, 0, "SS")
-        quantize_basis(1, 2)
-        image_half(7, 1, "VS")
-        comps_rows(2, "VS")
-        comps_rows(3, "VS")
+        store_comps(1, "SS")
+        image_half(6, 0)
+        store_image(6, 0, "SS")
+        quantize_basis(1)
+        image_half(6, 1)
+        store_image(6, 1, "VS")
+        image_half(7, 0)
+        store_image(7, 0, "VS")
+        image_half(7, 1)
+        store_image(7, 1, "VS")
+        comps_rows(2)
+        store_comps(2, "VS")
+        comps_rows(3)
+        store_comps(3, "VS")

@@ -198,23 +198,6 @@ def tile_spectral_tikhonov_imaging_s8_kernel(
             src = tiles["us", g, j].rearrange("p k (q w e) -> p q k w e", w=2, e=2)
             copy_on[eng](out=dst[:, 2 * lo : 2 * hi], in_=src[:, 2 * lo : 2 * hi])
 
-        def weave_us(j, g, half):
-            bank = take_bank(("weave", j, g, half), [128, 2, 512], BF16)
-            src = tiles["us", g, j].rearrange("p k (q w e) -> p w q e k", w=2, e=2)
-            for w in range(2):
-                nc.tensor.matmul(
-                    out=bank[:, w, :].rearrange("p (q e k) -> p q e k", e=2, k=4),
-                    lhsT=ident_b[:],
-                    rhs=src[:, w, 64 * half : 64 * half + 64],
-                    start=True,
-                    stop=True,
-                )
-
-        def empty_weave(j, g, half, eng):
-            dst = us_k(j, g)[:].rearrange("p (w c) -> p w c", w=2)[:, :, 512 * half : 512 * half + 512]
-            copy_on[eng](out=dst, in_=tiles["weave", j, g, half][:])
-            give_bank(("weave", j, g, half))
-
         def quantize_us(j, g):
             cols = slice(512 * j, 512 * j + 512)
             nc.vector.quantize_mx(out=us_codes[:, g, cols].bitcast(FP8X4), scales=us_scales[:, g, cols], in_=tiles["us_k", j, g][:])
@@ -404,195 +387,191 @@ def tile_spectral_tikhonov_imaging_s8_kernel(
             empty_comps(r, 1, engs[1])
 
         load_roots()
-        load_meas(0)
         load_us(0)
+        load_meas(0)
         load_meas(1)
         load_us(1)
         load_us(2)
         load_meas(2)
-        load_meas(3)
         spread_roots()
         clear_vt_scale()
         load_vt()
+        load_meas(3)
         load_basis()
         logarithms()
         invert_lam()
-        for g in range(PD):
-            turn_meas(0, g)
+
+        group_us(0, 0, "V")
+        group_us(1, 0, "V")
         weights(0, 0, 256)
-        for g in range(PD):
-            empty_meas(0, g, "V")
-        weave_us(1, 0, 0)
-        weave_us(1, 0, 1)
-        group_us(0, 0, "S", 0, 12)
-        group_us(0, 0, "V", 12, 64)
-        empty_weave(1, 0, 0, "S")
-        empty_weave(1, 0, 1, "S")
-        quantize_meas(0, 0, 2)
         quantize_us(0, 0)
         for g in range(PD):
-            turn_meas(1, g)
+            turn_meas(0, g)
         quantize_us(1, 0)
+        empty_meas(0, 0, "S")
+        empty_meas(0, 1, "S")
+        empty_meas(0, 2, "V")
         for g in range(PD):
-            empty_meas(1, g, "S")
+            turn_meas(1, g)
+        weights(0, 256, M)
+        quantize_meas(0, 0, 2)
+        empty_meas(1, 0, "S")
+        quantize_meas(0, 2, 3)
+        empty_meas(1, 1, "S")
         quantize_meas(1, 0, 1)
-        project_pass(0, 0, 0)
-        weave_us(1, 1, 0)
-        weave_us(1, 1, 1)
-        group_us(0, 1, "V")
-        empty_weave(1, 1, 0, "S")
-        empty_weave(1, 1, 1, "S")
-        project_pass(1, 0, 0)
-        project_pass(0, 1, 0)
-        project_pass(1, 1, 0)
+        empty_meas(1, 2, "S")
+        for j in range(PM):
+            for s in range(2):
+                project_pass(s, j, 0)
         for j in range(PM):
             for s in (2, 3):
                 project_pass(s, j, 0)
+        group_us(0, 1, "V")
+        group_us(1, 1, "S", 0, 48)
         quantize_meas(1, 1, 3)
         quantize_us(0, 1)
-        weights(0, 256, M)
+        group_us(1, 1, "V", 48, 64)
+        for s in range(4):
+            project_pass(s, 0, 1)
+        group_us(0, 2, "S", 0, 32)
+        group_us(0, 2, "V", 32, 64)
         quantize_us(1, 1)
-        for j in range(PM):
-            for s in range(4):
-                project_pass(s, j, 1)
-        group_us(0, 2, "S", 0, 24)
-        group_us(0, 2, "V", 24, 64)
-        quantize_meas(0, 2, 3)
+        for s in range(4):
+            project_pass(s, 1, 1)
         group_us(1, 2, "S", 0, 40)
         quantize_us(0, 2)
         group_us(1, 2, "V", 40, 64)
-        for s in range(4):
+        for s in range(3):
             project_pass(s, 0, 2)
         quantize_us(1, 2)
 
         weights(1)
         weigh(0, 0)
-        for s in range(4):
-            project_pass(s, 1, 2)
+        project_pass(0, 1, 2)
+        project_pass(1, 1, 2)
+        project_pass(3, 0, 2)
+        project_pass(2, 1, 2)
+        project_pass(3, 1, 2)
         weigh(0, 1)
         weights(2)
         turn_h(0)
         turn_meas(2, 0)
         weigh(1, 0)
-        weights(3, 0, 512)
-        turn_meas(2, 1)
         weigh(1, 1)
+        turn_meas(2, 1)
+        turn_h(1)
+        weights(3)
         empty_h(0, "S")
         turn_meas(2, 2)
         empty_meas(2, 0, "S")
-        quantize_h_modes(0, 0, 1)
         weigh(2, 0)
-        empty_meas(2, 1, "S")
+        quantize_h_modes(0, 0, 1)
         weigh(2, 1)
-        image_half(0, 0)
-        empty_meas(2, 2, "S")
+        empty_h(1, "S")
+        empty_meas(2, 1, "S")
         weigh(3, 0)
-        weights(3, 512, M)
-        quantize_meas(2, 0, 2)
-
-        image_half(0, 1)
-        quantize_meas(2, 2, 3)
-        weights(4, 0, 512)
+        empty_meas(2, 2, "S")
         weigh(3, 1)
+        quantize_h_modes(0, 1, 2)
         split_meas(3)
-        project(4, 0)
+        image_half(0, 0)
         store_image(0, 0, "SS")
-        project(4, 1)
-        group_h(0, 0, "V")
-        weights(4, 512, M)
+        quantize_meas(2, 0, 2)
+        quantize_meas(2, 2, 3)
+        image_half(0, 1)
         store_image(0, 1, "SS")
-        weigh(4, 0)
-        turn_h(1)
         turn_h(2)
-        empty_h(1, "V")
-        weigh(4, 1)
+        turn_h(3)
         for g in range(PD):
             turn_meas(3, g)
-        empty_h(2, "S")
-        project(5, 0)
+        empty_h(2, "V")
+        weights(4)
+        empty_h(3, "V")
         empty_meas(3, 0, "S")
-        quantize_h_modes(0, 1, 2)
         empty_meas(3, 1, "S")
-        project(5, 1)
-        quantize_h_modes(1, 0, 1)
-        group_h(0, 1, "V")
         empty_meas(3, 2, "S")
-        weights(5)
+        widen_basis(0)
         image_half(1, 0)
+        store_image(1, 0, "SS")
+        quantize_h_modes(1)
         quantize_meas(3, 0, 2)
         quantize_meas(3, 2, 3)
+        project(4, 0)
+        project(4, 1)
+        weights(5)
+        group_h(0, 0, "V")
+        image_half(1, 1)
+        store_image(1, 1, "SS")
+        weigh(4, 0)
+        weigh(4, 1)
+        image_half(2, 0)
+        store_image(2, 0, "SS")
+        group_h(0, 1, "V")
+        project(5, 0)
+        project(5, 1)
+        weights(6)
+        image_half(2, 1)
+        store_image(2, 1, "SS")
         weigh(5, 0)
         weigh(5, 1)
-        image_half(1, 1)
-        store_image(1, 0, "SS")
         quantize_h_frames(0)
-        image_half(2, 0)
-        store_image(1, 1, "SS")
-        widen_basis(0)
-        image_half(2, 1)
-        weights(6)
         project(6, 0)
-        store_image(2, 0, "SS")
         project(6, 1)
-        store_image(2, 1, "SS")
+        weights(7)
         weigh(6, 0)
-        turn_h(3)
-        turn_h(4)
         weigh(6, 1)
-        turn_h(5)
-        weights(7, 0, 512)
-        turn_basis(0, 0)
-        empty_h(3, "V")
-        empty_h(4, "S")
-        turn_basis(0, 1)
-        project(7, 0)
-        quantize_h_modes(1, 1, 2)
-        scale_basis(0, 0)
-        empty_h(5, "S")
         image_half(3, 0)
-        weigh(7, 0)
-        image_half(3, 1)
-        weights(7, 512, M)
-        quantize_h_modes(2)
         store_image(3, 0, "SS")
-        scale_basis(0, 1)
-        image_half(4, 0)
+        turn_h(4)
+        turn_h(5)
+        turn_basis(0, 0)
+        turn_basis(0, 1)
+        turn_h(6)
+        empty_h(4, "V")
+        empty_h(5, "S")
+        scale_basis(0, 0)
+        image_half(3, 1)
         store_image(3, 1, "SS")
-        group_h(1, 0, "V")
-        image_half(4, 1)
+        quantize_h_modes(2)
+        scale_basis(0, 1)
+        empty_h(6, "S")
+        project(7, 0)
+        image_half(4, 0)
         store_image(4, 0, "SS")
+        weigh(7, 0)
         quantize_basis(0)
-        project(7, 1)
         widen_basis(1)
+        image_half(4, 1)
         store_image(4, 1, "SS")
+        group_h(1, 0, "V")
         image_half(5, 0)
+        store_image(5, 0, "SS")
+        quantize_h_modes(3, 0, 1)
+        image_half(5, 1)
+        store_image(5, 1, "SV")
+        project(7, 1)
         weigh(7, 1)
         quantize_h_frames(1, 0, 1)
-        image_half(5, 1)
-        store_image(5, 0, "SS")
-        group_h(1, 1, "V")
-        turn_h(6)
-        turn_h(7)
-        store_image(5, 1, "SS")
-        turn_basis(1, 0)
-        turn_basis(1, 1)
-        empty_h(6, "V")
-        quantize_h_frames(1, 1, 2)
-        empty_h(7, "S")
-        comps_rows(0)
-        quantize_h_modes(3)
-        scale_basis(1, 0)
-        store_comps(0, "SS")
-        comps_rows(1)
-        scale_basis(1, 1)
-        store_comps(1, "SS")
         image_half(6, 0)
         store_image(6, 0, "SS")
-        quantize_basis(1)
+        group_h(1, 1, "V")
         image_half(6, 1)
-        store_image(6, 1, "VS")
+        store_image(6, 1, "SS")
+        turn_h(7)
+        turn_basis(1, 0)
+        turn_basis(1, 1)
+        quantize_h_frames(1, 1, 2)
+        empty_h(7, "S")
+        scale_basis(1, 0)
+        comps_rows(0)
+        store_comps(0, "SS")
+        quantize_h_modes(3, 1, 2)
+        scale_basis(1, 1)
+        comps_rows(1)
+        store_comps(1, "SS")
         image_half(7, 0)
-        store_image(7, 0, "VS")
+        store_image(7, 0, "SS")
+        quantize_basis(1)
         image_half(7, 1)
         store_image(7, 1, "VS")
         comps_rows(2)

@@ -82,8 +82,11 @@ def tile_spectral_tikhonov_imaging_s8_kernel(
             tiles["meas", un] = work.tile([128, 2, D], BF16, name="raw_meas", tag="raw_meas", bufs=4)
             nc.sync.dma_start(out=tiles["meas", un][:], in_=meas_v[un // 2, :, 2 * (un % 2) : 2 * (un % 2) + 2, :])
 
+        def wide_tile(shape, name):
+            return work.tile(shape, BF16, name=name, tag="wide", bufs=3, align_bytes=64)
+
         def load_us(g):
-            whole = work.tile([128, 4, M], BF16, name="raw_us", tag="wide", bufs=3, align_bytes=64)
+            whole = wide_tile([128, 4, M], "raw_us")
             nc.sync.dma_start(out=whole[:], in_=us_v[g])
             for j in range(PM):
                 tiles["us", g, j] = whole[:, :, 512 * j : 512 * j + 512]
@@ -163,7 +166,12 @@ def tile_spectral_tikhonov_imaging_s8_kernel(
             if g == 0:
                 tiles["meas_codes", un] = keep.tile([128, PD, 256], U32, name="meas_codes%d" % un, align_bytes=256)
                 tiles["meas_scales", un] = keep.tile([128, PD, 256], U8, name="meas_scales%d" % un, align_bytes=256)
-                tiles["meas_k", un] = work.tile([128, PD * 1024], BF16, name="meas_k", align_bytes=64)
+                if un < 3:
+                    tiles["meas_k", un] = work.tile([128, PD * 1024], BF16, name="meas_k", align_bytes=64)
+                else:
+                    tiles["meas_k", un] = wide_tile([128, PD * 1024], "meas_k")
+                    tiles["basis_k"] = wide_tile([128, PF * 2048], "basis_k")
+                    tiles["h_frames", 1] = wide_tile([128, PM * 2048], "h_frames")
             bank = take_bank(("meas_turn", un, g), [128, 2, 2, 128])
             for e in range(2):
                 for w in range(2):
@@ -308,8 +316,6 @@ def tile_spectral_tikhonov_imaging_s8_kernel(
             )
 
         def turn_basis(half, g):
-            if half == 0 and g == 0:
-                tiles["basis_k"] = work.tile([128, PF * 2048], BF16, name="basis_k", tag="wide", bufs=3, align_bytes=64)
             bank = take_bank(("basis_turn", half, g), [128, 2, 2, 128])
             for i in range(2):
                 for w in range(2):
@@ -337,11 +343,21 @@ def tile_spectral_tikhonov_imaging_s8_kernel(
         frame_scales = keep.tile([128, PF, M], U8, name="frame_scales", align_bytes=256)
 
         def group_h(g, j, eng, lo=0, hi=PARTS):
-            if j == 0 and lo == 0:
-                tiles["h_frames", g] = work.tile([128, PM * 2048], BF16, name="h_frames", tag="wide", bufs=3, align_bytes=64)
             dst = tiles["h_frames", g][:, 2048 * j : 2048 * j + 2048].rearrange("p (a i t) -> p a t i", i=4, t=4)
             src = tiles["h", g][:, :, 512 * j : 512 * j + 512].rearrange("p t (a i) -> p a t i", i=4)
             copy_on[eng](out=dst[:, 2 * lo : 2 * hi], in_=src[:, 2 * lo : 2 * hi])
+
+        def group_h_aside(j):
+            if j == 0:
+                tiles["h_frames", 0] = wide_tile([128, PM * 2048], "h_frames")
+            nc.gpsimd.tensor_scalar(
+                out=tiles["h_frames", 0][:, 2048 * j : 2048 * j + 2048].rearrange("p (c t) -> p c t", t=4),
+                in0=tiles["h", 0][:, :, 512 * j : 512 * j + 512].rearrange("p t c -> p c t"),
+                scalar1=1.0,
+                scalar2=0.0,
+                op0=MULT,
+                op1=ADD,
+            )
 
         def quantize_h_frames(g, lo=0, hi=PM):
             cols = slice(512 * lo, 512 * hi)
@@ -496,25 +512,24 @@ def tile_spectral_tikhonov_imaging_s8_kernel(
         quantize_h_modes(1)
         quantize_meas(3, 0, 2)
         quantize_meas(3, 2, 3)
+        group_h_aside(0)
+        group_h_aside(1)
         project(4, 0)
         project(4, 1)
         weights(5)
-        group_h(0, 0, "V")
         image_half(1, 1)
-        store_image(1, 1, "SS")
         weigh(4, 0)
         weigh(4, 1)
+        store_image(1, 1, "SV")
         image_half(2, 0)
-        store_image(2, 0, "SS")
-        group_h(0, 1, "V")
+        store_image(2, 0, "SV")
         project(5, 0)
         project(5, 1)
         weights(6)
         image_half(2, 1)
-        store_image(2, 1, "SS")
         weigh(5, 0)
         weigh(5, 1)
-        quantize_h_frames(0)
+        store_image(2, 1, "SV")
         project(6, 0)
         project(6, 1)
         weights(7)
@@ -522,12 +537,13 @@ def tile_spectral_tikhonov_imaging_s8_kernel(
         weigh(6, 1)
         image_half(3, 0)
         store_image(3, 0, "SS")
+        quantize_h_frames(0)
         turn_h(4)
         turn_h(5)
         turn_basis(0, 0)
         turn_basis(0, 1)
         turn_h(6)
-        empty_h(4, "V")
+        empty_h(4, "S")
         empty_h(5, "S")
         scale_basis(0, 0)
         image_half(3, 1)

@@ -83,10 +83,13 @@ def tile_spectral_tikhonov_imaging_s8_kernel(
             nc.sync.dma_start(out=tiles["meas", un][:], in_=meas_v[un // 2, :, 2 * (un % 2) : 2 * (un % 2) + 2, :])
 
         def wide_tile(shape, name):
-            return work.tile(shape, BF16, name=name, tag="wide", bufs=3, align_bytes=64)
+            return work.tile(shape, BF16, name=name, tag="wide", bufs=2, align_bytes=64)
+
+        def relay_tile(shape, name):
+            return work.tile(shape, BF16, name=name, tag="relay", bufs=1, align_bytes=64)
 
         def load_us(g):
-            whole = wide_tile([128, 4, M], "raw_us")
+            whole = (relay_tile if g == 0 else wide_tile)([128, 4, M], "raw_us")
             nc.sync.dma_start(out=whole[:], in_=us_v[g])
             for j in range(PM):
                 tiles["us", g, j] = whole[:, :, 512 * j : 512 * j + 512]
@@ -169,7 +172,7 @@ def tile_spectral_tikhonov_imaging_s8_kernel(
                 if un < 3:
                     tiles["meas_k", un] = work.tile([128, PD * 1024], BF16, name="meas_k", align_bytes=64)
                 else:
-                    tiles["meas_k", un] = wide_tile([128, PD * 1024], "meas_k")
+                    tiles["meas_k", un] = relay_tile([128, PD * 1024], "meas_k")
                     tiles["basis_k"] = wide_tile([128, PF * 2048], "basis_k")
                     tiles["h_frames", 1] = wide_tile([128, PM * 2048], "h_frames")
             bank = take_bank(("meas_turn", un, g), [128, 2, 2, 128])
@@ -349,7 +352,7 @@ def tile_spectral_tikhonov_imaging_s8_kernel(
 
         def group_h_aside(j):
             if j == 0:
-                tiles["h_frames", 0] = wide_tile([128, PM * 2048], "h_frames")
+                tiles["h_frames", 0] = relay_tile([128, PM * 2048], "h_frames")
             nc.gpsimd.tensor_scalar(
                 out=tiles["h_frames", 0][:, 2048 * j : 2048 * j + 2048].rearrange("p (c t) -> p c t", t=4),
                 in0=tiles["h", 0][:, :, 512 * j : 512 * j + 512].rearrange("p t c -> p c t"),

from contextlib import ExitStack

import concourse.mybir as mybir
from concourse.masks import make_identity

F, D, M, P, R = 1024, 1536, 1024, 2048, 512
FLOPS = 2 * (F * D * M + F * M * P + R * F * M)

F32 = mybir.dt.float32
BF16 = mybir.dt.bfloat16
U32 = mybir.dt.uint32
U8 = mybir.dt.uint8
I32 = mybir.dt.int32
E4M3 = mybir.dt.float8_e4m3fn
FP8X4 = mybir.dt.float8_e4m3fn_x4
FP4X4 = mybir.dt.float4_e2m1fn_x4
LN = mybir.ActivationFunctionType.Ln
SIGMOID = mybir.ActivationFunctionType.Sigmoid
MULT = mybir.AluOpType.mult
ADD = mybir.AluOpType.add
MAX = mybir.AluOpType.max

PD = D // 512
PM = M // 512
PF = F // 512
BANKS = 8
ROOT_ROW = 124
PARTS = 64
OUT_BUFS = 7
WEIGHT_BUFS = 4
TINY = 1e-18


def tile_spectral_tikhonov_imaging_s8_kernel(
    tc, meas, us, sigma, lam, vt_words, vt_scales, basis_bytes, basis_scale, image, comps
):
    nc = tc.nc
    with ExitStack() as ctx:
        keep = ctx.enter_context(tc.tile_pool(name="keep", bufs=1))
        work = ctx.enter_context(tc.tile_pool(name="work", bufs=2))
        stage = ctx.enter_context(tc.tile_pool(name="stage", bufs=OUT_BUFS))
        psum = ctx.enter_context(tc.psum_pool(name="psum", bufs=1))
        ctx.enter_context(tc.manual_schedule())

        copy_on = {"S": nc.scalar.copy, "V": nc.vector.tensor_copy}
        tiles = {}
        free_banks = list(range(BANKS))
        held = {}

        def take_bank(key, shape, dtype=F32):
            held[key] = free_banks[0]
            free_banks.remove(held[key])
            tiles[key] = psum.tile(shape, dtype, name="bank", tag="bank%d" % held[key], bufs=1)
            return tiles[key]

        def give_bank(key):
            free_banks.append(held[key])

        ident = keep.tile([128, 128], F32, name="ident")
        make_identity(nc, ident[:])
        root_rows = keep.tile([128, 512], BF16, name="root_rows")
        nc.vector.memset(root_rows[0:ROOT_ROW, :], 0.0)
        zero = keep.tile([128, 1], F32, name="zero")
        nc.vector.memset(zero[:], 0.0)
        one = keep.tile([128, 1], F32, name="one")
        nc.vector.memset(one[:], 1.0)
        tiny = keep.tile([128, 1], F32, name="tiny")
        nc.vector.tensor_scalar(out=tiny[:], in0=zero[:], scalar1=TINY, scalar2=None, op0=ADD)
        ident_b = keep.tile([128, 128], BF16, name="ident_b")
        nc.vector.tensor_copy(out=ident_b[:], in_=ident[:])
        vt_scale = keep.tile([128, PM, P], U8, name="vt_scale", align_bytes=256)

        meas_v = meas.rearrange("(g p t) d -> g p t d", g=PF, p=128)
        us_v = us.rearrange("(g p k) m -> g p k m", p=128, k=4)

        def load_roots():
            for side, vec in enumerate((lam, sigma)):
                first = ROOT_ROW + 2 * side
                nc.sync.dma_start(out=root_rows[first : first + 2, :], in_=vec.rearrange("(g x) -> g x", g=2))

        def load_meas(un):
            tiles["meas", un] = work.tile([128, 2, D], BF16, name="raw_meas", tag="raw_meas", bufs=4)
            nc.sync.dma_start(out=tiles["meas", un][:], in_=meas_v[un // 2, :, 2 * (un % 2) : 2 * (un % 2) + 2, :])

        def wide_tile(shape, name):
            return work.tile(shape, BF16, name=name, tag="wide", bufs=2, align_bytes=64)

        def relay_tile(shape, name):
            return work.tile(shape, BF16, name=name, tag="relay", bufs=1, align_bytes=64)

        def load_us(g):
            whole = (relay_tile if g == 0 else wide_tile)([128, 4, M], "raw_us")
            nc.sync.dma_start(out=whole[:], in_=us_v[g])
            for j in range(PM):
                tiles["us", g, j] = whole[:, :, 512 * j : 512 * j + 512]

        vt = keep.tile([128, PM, 2 * P], U8, name="vt", align_bytes=256)
        basis_raw = keep.tile([128, 4, F], U8, name="basis_raw")
        frame_scale = keep.tile([128, PF, 4], F32, name="frame_scale")

        def clear_vt_scale():
            nc.vector.memset(vt_scale[:].bitcast(I32), 0)

        def load_vt():
            for quad in range(4):
                nc.sync.dma_start(
                    out=vt_scale[32 * quad : 32 * quad + 4, :, :].bitcast(I32),
                    in_=vt_scales[:, 4 * quad : 4 * quad + 4, :].rearrange("g r n -> r g n").bitcast(I32),
                )
            nc.sync.dma_start(out=vt[:], in_=vt_words.rearrange("g p n -> p g n"))

        def load_basis():
            nc.sync.dma_start(out=basis_raw[:], in_=basis_bytes.rearrange("(r p) f -> p r f", p=128))
            nc.sync.dma_start(out=frame_scale[:], in_=basis_scale.rearrange("o (g p t) -> p (o g) t", p=128, t=4))

        log_sigma = keep.tile([128, M], F32, name="log_sigma")
        log_lam = keep.tile([128, PF, 4], F32, name="log_lam")
        inverse = keep.tile([128, PF * 4], F32, name="inverse")

        def spread_roots():
            size = keep.tile([128, 512], BF16, name="size")
            nc.vector.scalar_tensor_tensor(out=size[:], in0=root_rows[:], scalar=-1.0, in1=root_rows[:], op0=MULT, op1=MAX)
            bank = take_bank("lam", [128, 4, 2])
            for t in range(4):
                nc.tensor.matmul(
                    out=bank[:, t, :], lhsT=root_rows[:, t:512:4], rhs=ident_b[:, ROOT_ROW : ROOT_ROW + 2], start=True, stop=True
                )
            for j in range(PM):
                bank = take_bank(("sigma", j), [128, 512])
                row = ident_b[:, ROOT_ROW + 2 + j : ROOT_ROW + 3 + j].to_broadcast([128, 128])
                nc.tensor.matmul(out=bank[:], lhsT=row, rhs=size[:], start=True, stop=True)

        def logarithms():
            lam_columns = tiles["lam"][:].rearrange("p t g -> p g t")
            nc.scalar.activation(out=log_lam[:], in_=lam_columns, func=LN, bias=tiny[:])
            shifted = keep.tile([128, PF, 4], F32, name="shifted")
            nc.vector.tensor_scalar(out=shifted[:], in0=lam_columns, scalar1=TINY, scalar2=None, op0=ADD)
            give_bank("lam")
            for j in range(PM):
                nc.scalar.activation(
                    out=log_sigma[:, 512 * j : 512 * j + 512].rearrange("p (w q e) -> p w q e", w=2, e=2),
                    in_=tiles["sigma", j][:].rearrange("p (q w e) -> p w q e", w=2, e=2),
                    func=LN,
                    bias=tiny[:],
                )
                give_bank(("sigma", j))
            tiles["shifted"] = shifted

        def invert_lam():
            nc.vector.reciprocal(out=inverse[:], in_=tiles["shifted"][:].rearrange("p g t -> p (g t)"))

        def weights(s, lo=0, hi=M):
            if lo == 0:
                tiles["weight", s] = work.tile([128, M], F32, name="weight", bufs=WEIGHT_BUFS)
            nc.scalar.activation(
                out=tiles["weight", s][:, lo:hi],
                in_=log_sigma[:, lo:hi],
                func=SIGMOID,
                scale=-2.0,
                bias=log_lam[:, s // 4, s % 4 : s % 4 + 1],
            )

        def split_meas(un, eng="V"):
            tiles["split", un] = work.tile([128, 2, 2, D // 4], F32, name="split", tag="raw_meas", bufs=4)
            words = tiles["meas", un][:].bitcast(F32)
            copy_on[eng](out=tiles["split", un][:], in_=words.rearrange("r e (c w) -> r e w c", w=2))

        def turn_meas(un, g):
            if g == 0:
                tiles["meas_codes", un] = keep.tile([128, PD, 256], U32, name="meas_codes%d" % un, align_bytes=256)
                tiles["meas_scales", un] = keep.tile([128, PD, 256], U8, name="meas_scales%d" % un, align_bytes=256)
                if un < 3:
                    tiles["meas_k", un] = work.tile([128, PD * 1024], BF16, name="meas_k", align_bytes=64)
                else:
                    tiles["meas_k", un] = relay_tile([128, PD * 1024], "meas_k")
                    tiles["basis_k"] = wide_tile([128, PF * 2048], "basis_k")
                    tiles["h_frames", 1] = wide_tile([128, PM * 2048], "h_frames")
            bank = take_bank(("meas_turn", un, g), [128, 2, 2, 128])
            for e in range(2):
                for w in range(2):
                    if ("split", un) in tiles:
                        src = tiles["split", un][:, e, w, 128 * g : 128 * g + 128]
                    else:
                        src = tiles["meas", un][:].bitcast(F32)[:, e, 256 * g + w : 256 * g + 256 : 2]
                    nc.tensor.transpose(bank[:, e, w, :], src, ident[:])

        def empty_meas(un, g, eng):
            dst = tiles["meas_k", un][:, 1024 * g : 1024 * g + 1024].bitcast(F32).rearrange("p (e r w) -> p e r w", e=2, w=2)
            copy_on[eng](out=dst, in_=tiles["meas_turn", un, g][:].rearrange("p e w r -> p e r w"))
            give_bank(("meas_turn", un, g))

        def quantize_meas(un, lo, hi):
            nc.vector.quantize_mx(
                out=tiles["meas_codes", un][:, lo:hi, :].rearrange("p g c -> p (g c)").bitcast(FP8X4),
                scales=tiles["meas_scales", un][:, lo:hi, :].rearrange("p g c -> p (g c)"),
                in_=tiles["meas_k", un][:, 1024 * lo : 1024 * hi],
            )

        us_codes = keep.tile([128, PD, M], U32, name="us_codes", align_bytes=256)
        us_scales = keep.tile([128, PD, M], U8, name="us_scales", align_bytes=256)

        def us_k(j, g):
            if ("us_k", j, g) not in tiles:
                tiles["us_k", j, g] = work.tile([128, 2048], BF16, name="us_k", align_bytes=64, bufs=4)
            return tiles["us_k", j, g]

        def group_us(j, g, eng, lo=0, hi=PARTS):
            dst = us_k(j, g)[:].rearrange("p (w q e k) -> p q k w e", w=2, e=2, k=4)
            src = tiles["us", g, j].rearrange("p k (q w e) -> p q k w e", w=2, e=2)
            copy_on[eng](out=dst[:, 2 * lo : 2 * hi], in_=src[:, 2 * lo : 2 * hi])

        def quantize_us(j, g):
            cols = slice(512 * j, 512 * j + 512)
            nc.vector.quantize_mx(out=us_codes[:, g, cols].bitcast(FP8X4), scales=us_scales[:, g, cols], in_=tiles["us_k", j, g][:])

        def project_pass(s, j, g):
            if g == 0:
                take_bank(("c", s, j), [128, 512])
            frames = slice(128 * (s % 2), 128 * (s % 2) + 128)
            cols = slice(512 * j, 512 * j + 512)
            nc.tensor.matmul_mx(
                out=tiles["c", s, j][:],
                lhsT=tiles["meas_codes", s // 2][:, g, frames].bitcast(FP8X4),
                lhsT_scale=tiles["meas_scales", s // 2][:, g, frames],
                rhs=us_codes[:, g, cols].bitcast(FP8X4),
                rhs_scale=us_scales[:, g, cols],
                start=(g == 0),
                stop=(g == PD - 1),
            )

        def project(s, j):
            for g in range(PD):
                project_pass(s, j, g)

        def weigh(s, j):
            if ("h", s // 4) not in tiles:
                tiles["h", s // 4] = keep.tile([128, 4, M], BF16, name="h%d" % (s // 4))
            cols = slice(512 * j, 512 * j + 512)
            nc.vector.scalar_tensor_tensor(
                out=tiles["h", s // 4][:, s % 4, cols],
                in0=tiles["c", s, j][:],
                scalar=inverse[:, s : s + 1],
                in1=tiles["weight", s][:, cols],
                op0=MULT,
                op1=MULT,
            )
            give_bank(("c", s, j))

        def turn_h(s):
            bank = take_bank(("h_turn", s), [128, PM, 2, 128])
            words = tiles["h", s // 4][:, s % 4, :].bitcast(F32)
            for j in range(PM):
                for w in range(2):
                    first = 256 * j + 128 * w
                    nc.tensor.transpose(bank[:, j, w, :], words[:, first : first + 128], ident[:])

        def empty_h(s, eng):
            if s % 2 == 0:
                tiles["h_modes", s // 2] = work.tile([128, 2, 1024], BF16, name="h_modes", align_bytes=64)
            dst = tiles["h_modes", s // 2][:, s % 2, :].bitcast(F32).rearrange("q (j r w) -> q j r w", j=PM, w=2)
            copy_on[eng](out=dst, in_=tiles["h_turn", s][:].rearrange("q j w r -> q j r w"))
            give_bank(("h_turn", s))

        def quantize_h_modes(un, lo=0, hi=2):
            if lo == 0:
                tiles["h_codes", un] = keep.tile([128, 512], U32, name="h_codes%d" % un, align_bytes=256)
                tiles["h_scales", un] = keep.tile([128, 512], U8, name="h_scales%d" % un, align_bytes=256)
            cols = slice(256 * lo, 256 * hi)
            nc.vector.quantize_mx(
                out=tiles["h_codes", un][:, cols].bitcast(FP8X4),
                scales=tiles["h_scales", un][:, cols],
                in_=tiles["h_modes", un][:, lo:hi, :].rearrange("q e c -> q (e c)"),
            )

        image_v = image.rearrange("(g p t) n -> g t p n", g=PF, p=128)

        def image_bank(s, n):
            bank = take_bank(("image", s, n), [128, 512])
            for j in range(PM):
                first = 256 * (s % 2) + 128 * j
                nc.tensor.matmul_mx(
                    out=bank[:],
                    lhsT=tiles["h_codes", s // 2][:, first : first + 128].bitcast(FP8X4),
                    lhsT_scale=tiles["h_scales", s // 2][:, first : first + 128],
                    rhs=vt[:, j, 1024 * n : 1024 * n + 1024].bitcast(FP4X4),
                    rhs_scale=vt_scale[:, j, 512 * n : 512 * n + 512],
                    start=(j == 0),
                    stop=(j == PM - 1),
                )

        def image_half(s, half):
            image_bank(s, 2 * half)
            image_bank(s, 2 * half + 1)

        def empty_image(s, n, eng):
            if n % 2 == 0:
                tiles["result", s, n // 2] = stage.tile([128, 1024], F32, name="result", tag="result")
            result = tiles["result", s, n // 2]
            copy_on[eng](out=result[:, 512 * (n % 2) : 512 * (n % 2) + 512], in_=tiles["image", s, n][:])
            give_bank(("image", s, n))
            if n % 2 == 1:
                nc.sync.dma_start(out=image_v[s // 4, s % 4, :, 1024 * (n // 2) : 1024 * (n // 2) + 1024], in_=result[:])

        def store_image(s, half, engs):
            empty_image(s, 2 * half, engs[0])
            empty_image(s, 2 * half + 1, engs[1])

        basis_codes = keep.tile([128, PF * R], U32, name="basis_codes", align_bytes=256)
        basis_scales = keep.tile([128, PF * R], U8, name="basis_scales", align_bytes=256)

        def widen_basis(half):
            tiles["basis", half] = work.tile([128, 2, 2, F // 4], F32, name="basis")
            nc.vector.tensor_scalar(
                out=tiles["basis", half][:].bitcast(BF16).rearrange("n w i (c e) -> n (i c) w e", e=2),
                in0=basis_raw[:, 2 * half : 2 * half + 2, :].bitcast(E4M3).rearrange("n i (c w e) -> n (i c) w e", w=2, e=2),
                scalar1=one[:],
                scalar2=None,
                op0=MULT,
            )

        def turn_basis(half, g):
            bank = take_bank(("basis_turn", half, g), [128, 2, 2, 128])
            for i in range(2):
                for w in range(2):
                    nc.tensor.transpose(bank[:, w, i, :], tiles["basis", half][:, w, i, 128 * g : 128 * g + 128], ident[:])

        def scale_basis(half, g):
            first = 2048 * half + 1024 * g
            nc.vector.tensor_tensor(
                out=tiles["basis_k"][:, first : first + 1024].rearrange("p (c w e) -> p c w e", w=2, e=2),
                in0=tiles["basis_turn", half, g][:].bitcast(BF16).rearrange("p w i (n e) -> p (i n) w e", e=2),
                in1=frame_scale[:, g, :].rearrange("p (w e) -> p w e", e=2).unsqueeze(1).to_broadcast([128, 256, 2, 2]),
                op=MULT,
            )
            give_bank(("basis_turn", half, g))

        def quantize_basis(half):
            cols = slice(512 * half, 512 * half + 512)
            nc.vector.quantize_mx(
                out=basis_codes[:, cols].bitcast(FP8X4),
                scales=basis_scales[:, cols],
                in_=tiles["basis_k"][:, 2048 * half : 2048 * half + 2048],
            )

        frame_codes = keep.tile([128, PF, M], U32, name="frame_codes", align_bytes=256)
        frame_scales = keep.tile([128, PF, M], U8, name="frame_scales", align_bytes=256)

        def group_h(g, j, eng, lo=0, hi=PARTS):
            dst = tiles["h_frames", g][:, 2048 * j : 2048 * j + 2048].rearrange("p (a i t) -> p a t i", i=4, t=4)
            src = tiles["h", g][:, :, 512 * j : 512 * j + 512].rearrange("p t (a i) -> p a t i", i=4)
            copy_on[eng](out=dst[:, 2 * lo : 2 * hi], in_=src[:, 2 * lo : 2 * hi])

        def group_h_aside(j):
            if j == 0:
                tiles["h_frames", 0] = relay_tile([128, PM * 2048], "h_frames")
            nc.gpsimd.tensor_scalar(
                out=tiles["h_frames", 0][:, 2048 * j : 2048 * j + 2048].rearrange("p (c t) -> p c t", t=4),
                in0=tiles["h", 0][:, :, 512 * j : 512 * j + 512].rearrange("p t c -> p c t"),
                scalar1=1.0,
                scalar2=0.0,
                op0=MULT,
                op1=ADD,
            )

        def quantize_h_frames(g, lo=0, hi=PM):
            cols = slice(512 * lo, 512 * hi)
            nc.vector.quantize_mx(
                out=frame_codes[:, g, cols].bitcast(FP8X4),
                scales=frame_scales[:, g, cols],
                in_=tiles["h_frames", g][:, 2048 * lo : 2048 * hi],
            )

        def comps_bank(r, j):
            bank = take_bank(("comps", r, j), [128, 512])
            cols = slice(512 * j, 512 * j + 512)
            for g in range(PF):
                first = 512 * (r // 2) + 256 * g + 128 * (r % 2)
                nc.tensor.matmul_mx(
                    out=bank[:],
                    lhsT=basis_codes[:, first : first + 128].bitcast(FP8X4),
                    lhsT_scale=basis_scales[:, first : first + 128],
                    rhs=frame_codes[:, g, cols].bitcast(FP8X4),
                    rhs_scale=frame_scales[:, g, cols],
                    start=(g == 0),
                    stop=(g == PF - 1),
                )

        def comps_rows(r):
            comps_bank(r, 0)
            comps_bank(r, 1)

        def empty_comps(r, j, eng):
            if j == 0:
                tiles["rows", r] = stage.tile([128, M], F32, name="result", tag="result")
            result = tiles["rows", r]
            copy_on[eng](
                out=result[:, 512 * j : 512 * j + 512].rearrange("p (q w e) -> p q w e", w=2, e=2),
                in_=tiles["comps", r, j][:].rearrange("p (w q e) -> p q w e", w=2, e=2),
            )
            give_bank(("comps", r, j))
            if j == 1:
                nc.sync.dma_start(out=comps[128 * r : 128 * r + 128, :], in_=result[:])

        def store_comps(r, engs):
            empty_comps(r, 0, engs[0])
            empty_comps(r, 1, engs[1])

        load_roots()
        load_us(0)
        load_meas(0)
        load_meas(1)
        load_us(1)
        load_us(2)
        load_meas(2)
        spread_roots()
        clear_vt_scale()
        load_vt()
        load_meas(3)
        load_basis()
        logarithms()
        invert_lam()

        group_us(0, 0, "V")
        group_us(1, 0, "V")
        weights(0, 0, 256)
        quantize_us(0, 0)
        for g in range(PD):
            turn_meas(0, g)
        quantize_us(1, 0)
        empty_meas(0, 0, "S")
        empty_meas(0, 1, "S")
        empty_meas(0, 2, "V")
        for g in range(PD):
            turn_meas(1, g)
        weights(0, 256, M)
        quantize_meas(0, 0, 2)
        empty_meas(1, 0, "S")
        quantize_meas(0, 2, 3)
        empty_meas(1, 1, "S")
        quantize_meas(1, 0, 1)
        empty_meas(1, 2, "S")
        for j in range(PM):
            for s in range(2):
                project_pass(s, j, 0)
        for j in range(PM):
            for s in (2, 3):
                project_pass(s, j, 0)
        group_us(0, 1, "V")
        group_us(1, 1, "S", 0, 48)
        quantize_meas(1, 1, 3)
        quantize_us(0, 1)
        group_us(1, 1, "V", 48, 64)
        for s in range(4):
            project_pass(s, 0, 1)
        group_us(0, 2, "S", 0, 32)
        group_us(0, 2, "V", 32, 64)
        quantize_us(1, 1)
        for s in range(4):
            project_pass(s, 1, 1)
        group_us(1, 2, "S", 0, 40)
        quantize_us(0, 2)
        group_us(1, 2, "V", 40, 64)
        for s in range(3):
            project_pass(s, 0, 2)
        quantize_us(1, 2)

        weights(1)
        weigh(0, 0)
        project_pass(0, 1, 2)
        project_pass(1, 1, 2)
        project_pass(3, 0, 2)
        project_pass(2, 1, 2)
        project_pass(3, 1, 2)
        weigh(0, 1)
        weights(2)
        turn_h(0)
        turn_meas(2, 0)
        weigh(1, 0)
        weigh(1, 1)
        turn_meas(2, 1)
        turn_h(1)
        weights(3)
        empty_h(0, "S")
        turn_meas(2, 2)
        empty_meas(2, 0, "S")
        weigh(2, 0)
        quantize_h_modes(0, 0, 1)
        weigh(2, 1)
        empty_h(1, "S")
        empty_meas(2, 1, "S")
        weigh(3, 0)
        empty_meas(2, 2, "S")
        weigh(3, 1)
        quantize_h_modes(0, 1, 2)
        split_meas(3)
        image_half(0, 0)
        store_image(0, 0, "SS")
        quantize_meas(2, 0, 2)
        quantize_meas(2, 2, 3)
        image_half(0, 1)
        store_image(0, 1, "SS")
        turn_h(2)
        turn_h(3)
        for g in range(PD):
            turn_meas(3, g)
        empty_h(2, "V")
        weights(4)
        empty_h(3, "V")
        empty_meas(3, 0, "S")
        empty_meas(3, 1, "S")
        empty_meas(3, 2, "S")
        widen_basis(0)
        image_half(1, 0)
        store_image(1, 0, "SS")
        quantize_h_modes(1)
        quantize_meas(3, 0, 2)
        quantize_meas(3, 2, 3)
        group_h_aside(0)
        group_h_aside(1)
        project(4, 0)
        project(4, 1)
        weights(5)
        image_half(1, 1)
        weigh(4, 0)
        weigh(4, 1)
        store_image(1, 1, "SV")
        image_half(2, 0)
        store_image(2, 0, "SV")
        project(5, 0)
        project(5, 1)
        weights(6)
        image_half(2, 1)
        weigh(5, 0)
        weigh(5, 1)
        store_image(2, 1, "SV")
        project(6, 0)
        project(6, 1)
        weights(7)
        weigh(6, 0)
        weigh(6, 1)
        image_half(3, 0)
        store_image(3, 0, "SS")
        quantize_h_frames(0)
        turn_h(4)
        turn_h(5)
        turn_basis(0, 0)
        turn_basis(0, 1)
        turn_h(6)
        empty_h(4, "S")
        empty_h(5, "S")
        scale_basis(0, 0)
        image_half(3, 1)
        store_image(3, 1, "SS")
        quantize_h_modes(2)
        scale_basis(0, 1)
        empty_h(6, "S")
        project(7, 0)
        image_half(4, 0)
        store_image(4, 0, "SS")
        weigh(7, 0)
        quantize_basis(0)
        widen_basis(1)
        image_half(4, 1)
        store_image(4, 1, "SS")
        group_h(1, 0, "V")
        image_half(5, 0)
        store_image(5, 0, "SS")
        quantize_h_modes(3, 0, 1)
        image_half(5, 1)
        store_image(5, 1, "SV")
        project(7, 1)
        weigh(7, 1)
        quantize_h_frames(1, 0, 1)
        image_half(6, 0)
        store_image(6, 0, "SS")
        group_h(1, 1, "V")
        image_half(6, 1)
        store_image(6, 1, "SS")
        turn_h(7)
        turn_basis(1, 0)
        turn_basis(1, 1)
        quantize_h_frames(1, 1, 2)
        empty_h(7, "S")
        scale_basis(1, 0)
        comps_rows(0)
        store_comps(0, "SS")
        quantize_h_modes(3, 1, 2)
        scale_basis(1, 1)
        comps_rows(1)
        store_comps(1, "SS")
        image_half(7, 0)
        store_image(7, 0, "SS")
        quantize_basis(1)
        image_half(7, 1)
        store_image(7, 1, "VS")
        comps_rows(2)
        store_comps(2, "VS")
        comps_rows(3)
        store_comps(3, "VS")
